import numpy as np
import ml_dtypes


def mxq(x, axis, fmt="e4m3"):
    dtype, down = {"e4m3": (ml_dtypes.float8_e4m3fn, 7), "e5m2": (ml_dtypes.float8_e5m2, 14)}[fmt]
    v = np.moveaxis(np.asarray(x, np.float32).astype(ml_dtypes.bfloat16).astype(np.float64), axis, -1)
    blocks = v.reshape(v.shape[:-1] + (-1, 32))
    amax = np.abs(blocks).max(-1, keepdims=True)
    byte = np.maximum(np.where(amax > 0, np.frexp(amax)[1] - 1 + 127, 0) - down, 1)
    scale = np.exp2(byte - 127.0)
    codes = (blocks / scale).astype(np.float32).astype(dtype).astype(np.float64)
    return np.moveaxis((codes * scale).reshape(v.shape), -1, axis)


WIDE = False


def mx_kscale(k):
    if not WIDE:
        return np.ones(k)
    levels = np.array([10, -10, 5, -5, 0])
    if k % 512:
        return np.exp2(np.random.permutation(np.resize(levels, k // 32))).repeat(32)
    a = np.empty((k // 512, 16))
    for p in range(k // 512):
        a[p, :8] = np.random.permutation(np.resize(levels, 8))
        for g in range(8):
            far = levels[np.abs(levels - a[p, g]) >= 10]
            a[p, g + 8] = far[np.random.randint(len(far))]
    return np.exp2(a.ravel()).repeat(32)


def f64(x):
    return np.asarray(x).astype(np.float64)


def striped(idx):
    return np.tile(idx.reshape(-1, 16).T, (8, 1)).astype(np.uint16)


def unstriped(offs):
    return offs[:16].T.reshape(-1).astype(np.int64)


E2M1 = np.array([0.0, 0.5, 1.0, 1.5, 2.0, 3.0, 4.0, 6.0, -0.0, -0.5, -1.0, -1.5, -2.0, -3.0, -4.0, -6.0])


def pack_weight(w, fmt):
    k, n = w.shape
    w = f64(np.asarray(w, np.float32).astype(ml_dtypes.bfloat16)).reshape(k // 32, 32, n)
    amax = np.abs(w).max(1)
    if fmt == "e4m3":
        byte = np.frexp(amax)[1] - 1 + 127 - 7
    else:
        mant, ex = np.frexp(amax / 6.0)
        byte = np.where(mant > 0.5, ex, ex - 1) + 127
    byte = np.clip(np.where(amax > 0, byte, 1), 1, 254)
    scaled = (w * np.exp2(127.0 - byte)[:, None, :]).reshape(k, n).astype(np.float32)
    by_word = np.ascontiguousarray(scaled.reshape(k // 512, 128, 4, n).transpose(0, 1, 3, 2))
    if fmt == "e4m3":
        words = by_word.astype(ml_dtypes.float8_e4m3fn).view(np.uint8)
    else:
        c = by_word.astype(ml_dtypes.float4_e2m1fn).view(np.uint8) & 0xF
        words = (c[..., 0::2] | (c[..., 1::2] << 4)).reshape(k // 512, 128, 2 * n)
    return np.ascontiguousarray(words), np.ascontiguousarray(byte.astype(np.uint8).reshape(k // 512, 16, n))


def unpack_weight(words, scales, fmt):
    g, _, n = scales.shape
    words = np.ascontiguousarray(words).reshape(g, 128, n, -1)
    if fmt == "e4m3":
        vals = words.view(ml_dtypes.float8_e4m3fn).astype(np.float64)
    else:
        nib = np.empty((g, 128, n, 4), np.uint8)
        nib[..., 0::2] = words & 0xF
        nib[..., 1::2] = words >> 4
        vals = E2M1[nib]
    vals = vals * np.repeat(np.exp2(scales.astype(np.float64) - 127.0), 8, axis=1)[..., None]
    return vals.transpose(0, 1, 3, 2).reshape(g * 512, n)


def gelu(v):
    return 0.5 * v * (1.0 + np.tanh(np.sqrt(2.0 / np.pi) * (v + 0.044715 * v**3)))


K, H, N, T, T2, S = 1024, 1024, 384, 2048, 2048, 1024

def setup_inputs():
    n = np.random.standard_normal
    s = mx_kscale(K)[:, None]
    u = mx_kscale(H)[:, None]
    tab_words, tab_scales = pack_weight(n((K, T)) * s, "e4m3")
    wf_words, wf_scales = pack_weight(0.7 * n((K, H)) / np.sqrt(K) / s * u.T, "e2m1")
    wr_words, wr_scales = pack_weight(n((H, N)) / np.sqrt(H) / u, "e4m3")
    return {
        "tab_words": tab_words, "tab_scales": tab_scales,
        "offs": striped(np.random.permutation(T)[:S]),
        "xT": (np.round(16 * n((K, T2))) / 16 * s).astype(np.float32),
        "offs2": striped(np.random.permutation(T2)[:S]),
        "offs3": striped(np.random.permutation(T2)[:S]),
        "wf_words": wf_words, "wf_scales": wf_scales,
        "wx": (0.5 * n((K, H)) / np.sqrt(K) / s * u.T).astype(np.float32),
        "lo": (-np.random.uniform(0.4, 1.0, H) * u[:, 0]).astype(np.float32),
        "hi": (np.random.uniform(0.5, 1.4, H) * u[:, 0]).astype(np.float32),
        "wr_words": wr_words, "wr_scales": wr_scales,
        "slope": np.exp(0.4 * n((N, S))).astype(np.float32),
    }

def reference(tab_words, tab_scales, offs, xT, offs2, offs3, wf_words, wf_scales, wx, lo, hi, wr_words, wr_scales, slope):
    v = unpack_weight(tab_words, tab_scales, "e4m3")[:, unstriped(offs)]
    x = f64(xT)[:, unstriped(offs2)] + f64(xT)[:, unstriped(offs3)]
    wf = unpack_weight(wf_words, wf_scales, "e2m1")
    wxq = mxq(f64(wx), 0, "e4m3")
    xq = mxq(x, 0, "e4m3")
    d = wf.T @ v + wxq.T @ xq
    h = np.minimum(np.maximum(d, f64(lo)[:, None]), f64(hi)[:, None])
    wr = unpack_weight(wr_words, wr_scales, "e4m3")
    y = wr.T @ mxq(h, 0, "e4m3")
    return f64(slope) * y

@@ -1,0 +1,396 @@
+from contextlib import ExitStack
+
+import concourse.mybir as mybir
+
+K, H, N, T, S = 1024, 1024, 384, 2048, 1024
+FLOPS = 2 * S * (2 * K * H + H * N)
+
+F32 = mybir.dt.float32
+BF16 = mybir.dt.bfloat16
+I32 = mybir.dt.int32
+U32 = mybir.dt.uint32
+U16 = mybir.dt.uint16
+U8 = mybir.dt.uint8
+FP8X4 = mybir.dt.float8_e4m3fn_x4
+FP4X4 = mybir.dt.float4_e2m1fn_x4
+ADD = mybir.AluOpType.add
+MULT = mybir.AluOpType.mult
+MAX = mybir.AluOpType.max
+MIN = mybir.AluOpType.min
+
+P = 128
+PACK = 4
+K_PASS = P * PACK
+PASSES = K // K_PASS
+CHUNK = 256
+CHUNKS = S // CHUNK
+LAST = CHUNKS - 1
+LIST_ROWS = 16
+FP4_WIDTH = 128
+SHIFT_ROWS = 112
+N_TILES = N // P
+
+
+def tile_list_wildfire_spread_rates_kernel(
+    tc, tab_words, tab_scales, offs, xT, offs2, offs3, wf_words, wf_scales, wx, lo, hi, wr_words, wr_scales, slope, out
+):
+    nc = tc.nc
+    with ExitStack() as ctx:
+        keep = ctx.enter_context(tc.tile_pool(name="keep", bufs=1))
+        work = ctx.enter_context(tc.tile_pool(name="work", bufs=1))
+        psum = ctx.enter_context(tc.psum_pool(name="psum", bufs=1))
+
+        fuel_list = keep.tile([P, S // LIST_ROWS], U16, name="fuel_list")
+        upwind_list = keep.tile([P, S // LIST_ROWS], U16, name="upwind_list")
+        downwind_list = keep.tile([P, S // LIST_ROWS], U16, name="downwind_list")
+        x_planes = [keep.tile([P, T], F32, name="x_plane%d" % i) for i in range(PASSES * PACK)]
+        tab_codes = [keep.tile([P, T], U32, name="tab_codes%d" % a) for a in range(PASSES)]
+        tab_bytes = keep.tile([P, T], U8, name="tab_bytes")
+        v_codes = [keep.tile([P, S], U32, name="v_codes%d" % a, align_bytes=64) for a in range(PASSES)]
+        v_scales = [keep.tile([P, S], U8, name="v_scales%d" % a, align_bytes=64) for a in range(PASSES)]
+        wf_raw = keep.tile([P, PASSES * H], U16, name="wf_raw")
+        wf_codes = keep.tile([P, PASSES * H * 2], U8, name="wf_codes", align_bytes=64)
+        wf_raw_scales = keep.tile([P, H], U8, name="wf_raw_scales")
+        wf_planes = [keep.tile([P, H], U8, name="wf_planes%d" % a, align_bytes=64) for a in range(PASSES)]
+        wr_codes = keep.tile([P, PASSES, N], U32, name="wr_codes", align_bytes=64)
+        wr_planes = keep.tile([P, N], U8, name="wr_planes", align_bytes=64)
+        lo_cols = keep.tile([P, PASSES, PACK], F32, name="lo_cols")
+        hi_cols = keep.tile([P, PASSES, PACK], F32, name="hi_cols")
+        picked_tiles = [keep.tile([P, CHUNK], F32, name="picked%d" % i) for i in range(LAST)]
+        picked = [buf[:] for buf in picked_tiles]
+
+        for plane in (tab_bytes, wf_raw_scales, v_scales[1], wf_planes[1], wr_planes):
+            nc.vector.memset(plane[:].bitcast(I32), 0)
+
+        def load_scale_rows(plane, scales):
+            for q in range(4):
+                nc.sync.dma_start(
+                    out=plane[32 * q : 32 * q + 4 * PASSES, :].bitcast(I32),
+                    in_=scales[:, 4 * q : 4 * q + 4, :].bitcast(I32),
+                )
+
+        def load_x_plane(i):
+            a, t = divmod(i, PACK)
+            rows = xT[a * K_PASS : (a + 1) * K_PASS, :].rearrange("(p t) c -> p t c", t=PACK)
+            nc.sync.dma_start(out=x_planes[i][:], in_=rows[:, t, :])
+
+        wx_raw = {}
+
+        def load_wx(a, b):
+            wx_raw[a, b] = work.tile([P, PACK * K_PASS], F32, name="wx_raw%d%d" % (a, b), tag="wide", bufs=2)
+            rows = wx[a * K_PASS : (a + 1) * K_PASS, b * K_PASS : (b + 1) * K_PASS]
+            nc.sync.dma_start(
+                out=wx_raw[a, b][:].rearrange("p (i c) -> p i c", i=PACK), in_=rows.rearrange("(p i) c -> p i c", i=PACK)
+            )
+
+        def load_tab(a):
+            nc.sync.dma_start(
+                out=tab_codes[a][:].bitcast(I32), in_=tab_words[a].rearrange("p t i -> p (t i)").bitcast(I32)
+            )
+
+        slope_cols = [work.tile([P, N_TILES, CHUNK], F32, name="slope%d" % c, tag="slope%d" % c) for c in range(CHUNKS)]
+
+        nc.sync.dma_start(fuel_list[:], offs)
+        load_scale_rows(tab_bytes, tab_scales)
+        nc.sync.dma_start(upwind_list[:], offs2)
+        nc.sync.dma_start(downwind_list[:], offs3)
+        load_x_plane(0)
+        load_x_plane(1)
+        nc.sync.dma_start(
+            out=wf_raw[:].bitcast(I32).rearrange("p (a c) -> p a c", a=PASSES),
+            in_=wf_words.bitcast(I32).rearrange("a p c -> p a c"),
+        )
+        load_scale_rows(wf_raw_scales, wf_scales)
+        load_wx(0, 0)
+        load_x_plane(2)
+        load_wx(1, 0)
+        load_x_plane(3)
+        load_wx(0, 1)
+        load_x_plane(4)
+        load_wx(1, 1)
+        load_x_plane(5)
+        load_tab(0)
+        load_tab(1)
+        load_x_plane(6)
+        load_x_plane(7)
+        nc.sync.dma_start(out=lo_cols[:], in_=lo.rearrange("(b p t) -> p b t", b=PASSES, t=PACK))
+        nc.sync.dma_start(out=hi_cols[:], in_=hi.rearrange("(b p t) -> p b t", b=PASSES, t=PACK))
+        nc.sync.dma_start(
+            out=wr_codes[:].bitcast(I32), in_=wr_words.rearrange("a p c i -> p a (c i)").bitcast(I32)
+        )
+        load_scale_rows(wr_planes, wr_scales)
+        for c in range(CHUNKS):
+            nc.sync.dma_start(
+                out=slope_cols[c][:], in_=slope[:, c * CHUNK : (c + 1) * CHUNK].rearrange("(n p) j -> p n j", p=P)
+            )
+
+        def shift_second_pass(planes):
+            nc.scalar.dma_start(
+                out=planes[1][0:SHIFT_ROWS, :].bitcast(I32), in_=planes[0][4 : 4 + SHIFT_ROWS, :].bitcast(I32)
+            )
+
+        wx_codes = {}
+        wx_scales = {}
+
+        def quantize_wx(a, b):
+            grouped = work.tile([P, PACK * K_PASS], BF16, name="wx_bf%d%d" % (a, b), tag="wx_bf", bufs=2, align_bytes=64)
+            nc.scalar.copy(
+                out=grouped[:].rearrange("p (t m i) -> p m t i", t=PACK, i=PACK),
+                in_=wx_raw[a, b][:].rearrange("p (i m t) -> p m t i", i=PACK, t=PACK),
+            )
+            wx_codes[a, b] = keep.tile([P, K_PASS], U32, name="wx_codes%d%d" % (a, b), align_bytes=64)
+            wx_scales[a, b] = keep.tile([P, K_PASS], U8, name="wx_scales%d%d" % (a, b), align_bytes=64)
+            nc.vector.quantize_mx(out=wx_codes[a, b][:].bitcast(FP8X4), scales=wx_scales[a, b][:], in_=grouped[:])
+
+        def reorder_wf():
+            nc.vector.tensor_copy(
+                out=wf_codes[:].bitcast(U16).rearrange("p (g t m) -> p g t m", t=PACK, m=P),
+                in_=wf_raw[:].rearrange("p (g m t) -> p g t m", t=PACK, m=P),
+            )
+            nc.vector.tensor_copy(
+                out=wf_planes[0][:].rearrange("p (b t m) -> p b t m", t=PACK, m=P),
+                in_=wf_raw_scales[:].rearrange("p (b m t) -> p b t m", t=PACK, m=P),
+            )
+            shift_second_pass(wf_planes)
+
+        x_sums = {}
+        x_mixed = {}
+        x_codes = {}
+        x_scales = {}
+
+        def scratch(tag):
+            buf = work.tile([P, CHUNK], F32, name="scratch_" + tag, tag=tag, align_bytes=64)
+            return buf[:]
+
+        def gather_x(pieces, buffers):
+            for (i, c), buf in zip(pieces, buffers):
+                cols = slice(c * CHUNK // LIST_ROWS, (c + 1) * CHUNK // LIST_ROWS)
+                nc.vector.tensor_copy(buf, x_planes[i][:].indirect(upwind_list[:, cols]))
+            for (i, c), buf in zip(pieces, buffers):
+                a, t = divmod(i, PACK)
+                if (c, a) not in x_sums:
+                    x_sums[c, a] = work.tile(
+                        [P, PACK, CHUNK], F32, name="x_sum%d%d" % (c, a), tag="x_sum%d%d" % (c % LAST, a)
+                    )
+                cols = slice(c * CHUNK // LIST_ROWS, (c + 1) * CHUNK // LIST_ROWS)
+                nc.vector.tensor_tensor(x_sums[c, a][:, t, :], x_planes[i][:].indirect(downwind_list[:, cols]), buf, ADD)
+
+        def interleave(dst, src):
+            nc.scalar.copy(
+                out=dst[:].rearrange("p (c i t) -> p c t i", i=PACK, t=PACK),
+                in_=src[:].rearrange("p t (c i) -> p c t i", i=PACK),
+            )
+
+        def mix_x(c, a):
+            x_mixed[c, a] = work.tile(
+                [P, PACK * CHUNK], BF16, name="x_mixed%d%d" % (c, a), tag="x_mixed%d" % (c % LAST), align_bytes=64
+            )
+            interleave(x_mixed[c, a], x_sums[c, a])
+
+        def quantize_x(c, a):
+            x_codes[c, a] = work.tile([P, CHUNK], U32, name="x_codes%d%d" % (c, a), tag="xq%d%d" % (c, a), align_bytes=64)
+            x_scales[c, a] = keep.tile([P, CHUNK], U8, name="x_scales%d%d" % (c, a), align_bytes=64)
+            nc.vector.quantize_mx(out=x_codes[c, a][:].bitcast(FP8X4), scales=x_scales[c, a][:], in_=x_mixed[c, a][:])
+
+        d_banks = {}
+
+        def d_fuel_and_first_x(c, b):
+            for pair in range(2):
+                bank = psum.tile([P, 2 * CHUNK], F32, name="d%d%d%d" % (c, b, pair), tag="d", bufs=6)
+                d_banks[c, b, pair] = bank
+                for a in range(PASSES):
+                    for u in range(2):
+                        col = b * K_PASS + (2 * pair + u) * P
+                        for j in range(0, CHUNK, FP4_WIDTH):
+                            cols = slice(c * CHUNK + j, c * CHUNK + j + FP4_WIDTH)
+                            nc.tensor.matmul_mx(
+                                out=bank[:, u * CHUNK + j : u * CHUNK + j + FP4_WIDTH],
+                                lhsT=wf_codes[:, 2 * (a * H + col) : 2 * (a * H + col + P)].bitcast(FP4X4),
+                                lhsT_scale=wf_planes[a][:, col : col + P],
+                                rhs=v_codes[a][:, cols].bitcast(FP8X4),
+                                rhs_scale=v_scales[a][:, cols],
+                                start=(a == 0 and u == 0 and j == 0),
+                                stop=False,
+                            )
+                d_x_pass(c, b, pair, 0)
+
+        def d_x_pass(c, b, pair, a):
+            for u in range(2):
+                cols = slice((2 * pair + u) * P, (2 * pair + u + 1) * P)
+                nc.tensor.matmul_mx(
+                    out=d_banks[c, b, pair][:, u * CHUNK : (u + 1) * CHUNK],
+                    lhsT=wx_codes[a, b][:, cols].bitcast(FP8X4),
+                    lhsT_scale=wx_scales[a, b][:, cols],
+                    rhs=x_codes[c, a][:].bitcast(FP8X4),
+                    rhs_scale=x_scales[c, a][:],
+                    start=False,
+                    stop=(a == PASSES - 1 and u == 1),
+                )
+
+        def d_last_pass(c, b):
+            for pair in range(2):
+                d_x_pass(c, b, pair, PASSES - 1)
+
+        d_sbuf = {}
+
+        def evacuate_d(c, b):
+            if c not in d_sbuf:
+                d_sbuf[c] = work.tile([P, PACK * K_PASS], F32, name="d_sbuf%d" % c, tag="wide", bufs=2)
+            for pair in range(2):
+                first = (2 * b + pair) * 2 * CHUNK
+                nc.scalar.copy(out=d_sbuf[c][:, first : first + 2 * CHUNK], in_=d_banks[c, b, pair][:])
+
+        h_planes = {}
+        h_mixed = {}
+        h_codes = {}
+        h_scales = {}
+
+        def clamp(c, b, from_psum):
+            h_planes[c, b] = work.tile(
+                [P, PACK, CHUNK], BF16, name="h_planes%d%d" % (c, b), tag="h_planes%d%d" % (c % 2, b), align_bytes=64
+            )
+            for t in range(PACK):
+                if from_psum:
+                    src = d_banks[c, b, t // 2][:, (t % 2) * CHUNK : (t % 2 + 1) * CHUNK]
+                else:
+                    src = d_sbuf[c][:, (PACK * b + t) * CHUNK : (PACK * b + t + 1) * CHUNK]
+                nc.vector.tensor_scalar(
+                    h_planes[c, b][:, t, :], src, lo_cols[:, b, t : t + 1], hi_cols[:, b, t : t + 1], MAX, MIN
+                )
+
+        def mix_h(c, b):
+            h_mixed[c, b] = work.tile(
+                [P, PACK * CHUNK], BF16, name="h_mixed%d%d" % (c, b), tag="h_mixed%d%d" % (c % 2, b), align_bytes=64
+            )
+            interleave(h_mixed[c, b], h_planes[c, b])
+
+        def quantize_h(c, b):
+            h_codes[c, b] = work.tile(
+                [P, CHUNK], U32, name="h_codes%d%d" % (c, b), tag="h_codes%d%d" % (c % 2, b), align_bytes=64
+            )
+            h_scales[c, b] = work.tile(
+                [P, CHUNK], U8, name="h_scales%d%d" % (c, b), tag="h_scales%d%d" % (c % 2, b), align_bytes=64
+            )
+            nc.vector.quantize_mx(out=h_codes[c, b][:].bitcast(FP8X4), scales=h_scales[c, b][:], in_=h_mixed[c, b][:])
+
+        y_banks = {}
+
+        def y_product(c):
+            for first in range(0, N_TILES, 2):
+                count = min(2, N_TILES - first)
+                bank = psum.tile([P, count, CHUNK], F32, name="y%d%d" % (c, first), tag="y%d" % first)
+                y_banks[c, first] = bank
+                for u in range(count):
+                    cols = slice((first + u) * P, (first + u + 1) * P)
+                    for b in range(PASSES):
+                        nc.tensor.matmul_mx(
+                            out=bank[:, u, :],
+                            lhsT=wr_codes[:, b, cols].bitcast(FP8X4),
+                            lhsT_scale=wr_planes[4 * b : P, cols],
+                            rhs=h_codes[c, b][:].bitcast(FP8X4),
+                            rhs_scale=h_scales[c, b][:],
+                            start=(b == 0),
+                            stop=(b == PASSES - 1),
+                        )
+
+        def finish(c):
+            for first in range(0, N_TILES, 2):
+                count = min(2, N_TILES - first)
+                result = work.tile([P, count, CHUNK], F32, name="res%d%d" % (c, first), tag="res%d%d" % (c % 2, first))
+                nc.vector.tensor_tensor(result[:], y_banks[c, first][:], slope_cols[c][:, first : first + count, :], MULT)
+                rows = out[first * P : (first + count) * P, c * CHUNK : (c + 1) * CHUNK]
+                nc.sync.dma_start(out=rows.rearrange("(n p) j -> p n j", p=P), in_=result[:])
+
+        early = range(LAST)
+        nc.vector.tensor_copy(v_scales[0][:], tab_bytes[:].indirect(fuel_list[:]))
+        shift_second_pass(v_scales)
+        gather_x([(0, c) for c in early], picked)
+        gather_x([(1, c) for c in early], picked)
+        reorder_wf()
+        gather_x([(2, c) for c in early], picked)
+        quantize_wx(0, 0)
+        gather_x([(3, c) for c in early], picked)
+        quantize_wx(1, 0)
+        quantize_wx(0, 1)
+        for c in early:
+            mix_x(c, 0)
+        gather_x([(4, c) for c in early], [picked[0], picked[1], scratch("xq00")])
+        quantize_x(0, 0)
+        gather_x([(5, c) for c in early], [picked[0], scratch("xq10"), scratch("xq20")])
+        quantize_x(1, 0)
+        quantize_x(2, 0)
+        quantize_wx(1, 1)
+        for a in range(PASSES):
+            nc.vector.tensor_copy(v_codes[a][:], tab_codes[a][:].indirect(fuel_list[:]))
+        d_fuel_and_first_x(0, 0)
+        d_fuel_and_first_x(0, 1)
+        d_fuel_and_first_x(1, 0)
+
+        gather_x([(6, 0), (7, 0)], picked)
+        mix_x(0, 1)
+        gather_x([(6, 1), (7, 1)], [picked[0], scratch("xq01")])
+        mix_x(1, 1)
+        quantize_x(0, 1)
+        d_last_pass(0, 0)
+        d_last_pass(0, 1)
+        evacuate_d(0, 0)
+        evacuate_d(0, 1)
+        gather_x([(6, 2), (7, 2)], [scratch("x_mixed0"), scratch("xq11")])
+        mix_x(2, 1)
+        quantize_x(1, 1)
+        d_last_pass(1, 0)
+        d_fuel_and_first_x(1, 1)
+        d_last_pass(1, 1)
+        d_fuel_and_first_x(2, 0)
+        clamp(0, 0, False)
+        clamp(0, 1, False)
+        mix_h(0, 0)
+        mix_h(0, 1)
+        evacuate_d(1, 0)
+        evacuate_d(1, 1)
+        gather_x([(0, 3), (1, 3)], [d_sbuf[0][:, 1792:2048], scratch("xq21")])
+        quantize_x(2, 1)
+        d_last_pass(2, 0)
+        d_fuel_and_first_x(2, 1)
+        d_last_pass(2, 1)
+        gather_x([(2, 3), (3, 3)], [scratch("x_mixed2"), d_sbuf[0][:, 1536:1792]])
+        mix_x(3, 0)
+        quantize_h(0, 0)
+        quantize_h(0, 1)
+        y_product(0)
+        clamp(1, 0, False)
+        clamp(1, 1, False)
+        finish(0)
+        evacuate_d(2, 0)
+        evacuate_d(2, 1)
+        mix_h(1, 0)
+        mix_h(1, 1)
+        gather_x([(4, 3), (5, 3)], [d_sbuf[1][:, 1792:2048], scratch("xq30")])
+        quantize_x(3, 0)
+        d_fuel_and_first_x(3, 0)
+        d_fuel_and_first_x(3, 1)
+        clamp(2, 0, False)
+        clamp(2, 1, False)
+        mix_h(2, 0)
+        mix_h(2, 1)
+        gather_x([(6, 3), (7, 3)], [d_sbuf[2][:, 1792:2048], d_sbuf[2][:, 1536:1792]])
+        mix_x(3, 1)
+        quantize_h(1, 0)
+        quantize_h(1, 1)
+        y_product(1)
+        finish(1)
+        quantize_h(2, 0)
+        quantize_h(2, 1)
+        y_product(2)
+        quantize_x(3, 1)
+        d_last_pass(3, 0)
+        d_last_pass(3, 1)
+        finish(2)
+        clamp(3, 0, True)
+        mix_h(3, 0)
+        clamp(3, 1, True)
+        mix_h(3, 1)
+        quantize_h(3, 0)
+        quantize_h(3, 1)
+        y_product(3)
+        finish(3)

@@ -50,16 +50,16 @@ def tile_list_wildfire_spread_rates_kernel(
         v_scales = [keep.tile([P, S], U8, name="v_scales%d" % a, align_bytes=64) for a in range(PASSES)]
         wf_raw = keep.tile([P, PASSES * H], U16, name="wf_raw")
         wf_codes = keep.tile([P, PASSES * H * 2], U8, name="wf_codes", align_bytes=64)
-        wf_raw_scales = keep.tile([P, H], U8, name="wf_raw_scales")
-        wf_planes = [keep.tile([P, H], U8, name="wf_planes%d" % a, align_bytes=64) for a in range(PASSES)]
+        wf_raw_scales = keep.tile([P, PASSES * H], U8, name="wf_raw_scales")
+        wf_planes = keep.tile([P, PASSES * H], U8, name="wf_planes", align_bytes=64)
         wr_codes = keep.tile([P, PASSES, N], U32, name="wr_codes", align_bytes=64)
         wr_planes = keep.tile([P, N], U8, name="wr_planes", align_bytes=64)
         lo_cols = keep.tile([P, PASSES, PACK], F32, name="lo_cols")
         hi_cols = keep.tile([P, PASSES, PACK], F32, name="hi_cols")
-        picked_tiles = [keep.tile([P, CHUNK], F32, name="picked%d" % i) for i in range(LAST)]
-        picked = [buf[:] for buf in picked_tiles]
+        picked_tile = keep.tile([P, LAST * CHUNK], F32, name="picked")
+        picked = [picked_tile[:, c * CHUNK : (c + 1) * CHUNK] for c in range(LAST)]
 
-        for plane in (tab_bytes, wf_raw_scales, v_scales[1], wf_planes[1], wr_planes):
+        for plane in (tab_bytes, wf_raw_scales, v_scales[1], wr_planes):
             nc.vector.memset(plane[:].bitcast(I32), 0)
 
         def load_scale_rows(plane, scales):
@@ -77,7 +77,7 @@ def tile_list_wildfire_spread_rates_kernel(
         wx_raw = {}
 
         def load_wx(a, b):
-            wx_raw[a, b] = work.tile([P, PACK * K_PASS], F32, name="wx_raw%d%d" % (a, b), tag="wide", bufs=2)
+            wx_raw[a, b] = work.tile([P, PACK * K_PASS], F32, name="wx_raw%d%d" % (a, b), tag="wide%d" % ((2 * b + a) % 3), align_bytes=64)
             rows = wx[a * K_PASS : (a + 1) * K_PASS, b * K_PASS : (b + 1) * K_PASS]
             nc.sync.dma_start(
                 out=wx_raw[a, b][:].rearrange("p (i c) -> p i c", i=PACK), in_=rows.rearrange("(p i) c -> p i c", i=PACK)
@@ -90,22 +90,26 @@ def tile_list_wildfire_spread_rates_kernel(
 
         slope_cols = [work.tile([P, N_TILES, CHUNK], F32, name="slope%d" % c, tag="slope%d" % c) for c in range(CHUNKS)]
 
-        nc.sync.dma_start(fuel_list[:], offs)
-        load_scale_rows(tab_bytes, tab_scales)
+        load_x_plane(0)
         nc.sync.dma_start(upwind_list[:], offs2)
         nc.sync.dma_start(downwind_list[:], offs3)
-        load_x_plane(0)
+        nc.sync.dma_start(fuel_list[:], offs)
+        load_scale_rows(tab_bytes, tab_scales)
         load_x_plane(1)
-        nc.sync.dma_start(
-            out=wf_raw[:].bitcast(I32).rearrange("p (a c) -> p a c", a=PASSES),
-            in_=wf_words.bitcast(I32).rearrange("a p c -> p a c"),
-        )
-        load_scale_rows(wf_raw_scales, wf_scales)
         load_wx(0, 0)
         load_x_plane(2)
         load_wx(1, 0)
         load_x_plane(3)
         load_wx(0, 1)
+        nc.sync.dma_start(
+            out=wf_raw[:].bitcast(I32).rearrange("p (a c) -> p a c", a=PASSES),
+            in_=wf_words.bitcast(I32).rearrange("a p c -> p a c"),
+        )
+        for q in range(4):
+            nc.sync.dma_start(
+                out=wf_raw_scales[32 * q : 32 * q + 4, :].bitcast(I32).rearrange("r (a c) -> r a c", a=PASSES),
+                in_=wf_scales[:, 4 * q : 4 * q + 4, :].bitcast(I32).rearrange("a r c -> r a c"),
+            )
         load_x_plane(4)
         load_wx(1, 1)
         load_x_plane(5)
@@ -132,13 +136,19 @@ def tile_list_wildfire_spread_rates_kernel(
         wx_codes = {}
         wx_scales = {}
 
-        def quantize_wx(a, b):
+        wx_grouped = {}
+
+        def cast_wx(a, b):
             grouped = work.tile([P, PACK * K_PASS], BF16, name="wx_bf%d%d" % (a, b), tag="wx_bf", bufs=2, align_bytes=64)
             nc.scalar.copy(
-                out=grouped[:].rearrange("p (t m i) -> p m t i", t=PACK, i=PACK),
-                in_=wx_raw[a, b][:].rearrange("p (i m t) -> p m t i", i=PACK, t=PACK),
+                out=grouped[:].rearrange("p (t m i) -> p t m i", t=PACK, i=PACK),
+                in_=wx_raw[a, b][:].rearrange("p (i m t) -> p t m i", i=PACK, t=PACK),
             )
-            wx_codes[a, b] = keep.tile([P, K_PASS], U32, name="wx_codes%d%d" % (a, b), align_bytes=64)
+            wx_grouped[a, b] = grouped
+
+        def quantize_wx(a, b):
+            grouped = wx_grouped[a, b]
+            wx_codes[a, b] = work.tile([P, K_PASS], U32, name="wx_codes%d%d" % (a, b), tag="wq%d%d" % (a, b), align_bytes=64)
             wx_scales[a, b] = keep.tile([P, K_PASS], U8, name="wx_scales%d%d" % (a, b), align_bytes=64)
             nc.vector.quantize_mx(out=wx_codes[a, b][:].bitcast(FP8X4), scales=wx_scales[a, b][:], in_=grouped[:])
 
@@ -148,10 +158,9 @@ def tile_list_wildfire_spread_rates_kernel(
                 in_=wf_raw[:].rearrange("p (g m t) -> p g t m", t=PACK, m=P),
             )
             nc.vector.tensor_copy(
-                out=wf_planes[0][:].rearrange("p (b t m) -> p b t m", t=PACK, m=P),
-                in_=wf_raw_scales[:].rearrange("p (b m t) -> p b t m", t=PACK, m=P),
+                out=wf_planes[:].rearrange("p (g t m) -> p g t m", t=PACK, m=P),
+                in_=wf_raw_scales[:].rearrange("p (g m t) -> p g t m", t=PACK, m=P),
             )
-            shift_second_pass(wf_planes)
 
         x_sums = {}
         x_mixed = {}
@@ -162,35 +171,52 @@ def tile_list_wildfire_spread_rates_kernel(
             buf = work.tile([P, CHUNK], F32, name="scratch_" + tag, tag=tag, align_bytes=64)
             return buf[:]
 
-        def gather_x(pieces, buffers):
-            for (i, c), buf in zip(pieces, buffers):
-                cols = slice(c * CHUNK // LIST_ROWS, (c + 1) * CHUNK // LIST_ROWS)
+        def gather_pieces(pieces, buffers):
+            for (i, first, dest), buf in zip(pieces, buffers):
+                cols = slice(first // LIST_ROWS, (first + dest.shape[1]) // LIST_ROWS)
                 nc.vector.tensor_copy(buf, x_planes[i][:].indirect(upwind_list[:, cols]))
-            for (i, c), buf in zip(pieces, buffers):
-                a, t = divmod(i, PACK)
-                if (c, a) not in x_sums:
-                    x_sums[c, a] = work.tile(
-                        [P, PACK, CHUNK], F32, name="x_sum%d%d" % (c, a), tag="x_sum%d%d" % (c % LAST, a)
-                    )
-                cols = slice(c * CHUNK // LIST_ROWS, (c + 1) * CHUNK // LIST_ROWS)
-                nc.vector.tensor_tensor(x_sums[c, a][:, t, :], x_planes[i][:].indirect(downwind_list[:, cols]), buf, ADD)
+            for (i, first, dest), buf in zip(pieces, buffers):
+                cols = slice(first // LIST_ROWS, (first + dest.shape[1]) // LIST_ROWS)
+                nc.vector.tensor_tensor(dest, x_planes[i][:].indirect(downwind_list[:, cols]), buf, ADD)
 
-        def interleave(dst, src):
-            nc.scalar.copy(
-                out=dst[:].rearrange("p (c i t) -> p c t i", i=PACK, t=PACK),
-                in_=src[:].rearrange("p t (c i) -> p c t i", i=PACK),
-            )
+        def gather_x(pieces, buffers):
+            for i, c in pieces:
+                a = i // PACK
+                if (c, a) not in x_sums:
+                    sums = work.tile([P, PACK, CHUNK], F32, name="x_sum%d%d" % (c, a), tag=sum_tags[c, a])
+                    x_sums[c, a] = sums[:]
+            gather_pieces([(i, c * CHUNK, x_sums[c, i // PACK][:, i % PACK, :]) for i, c in pieces], buffers)
+
+        sum_tags = {(0, 1): "sum_a", (1, 1): "sum_b", (2, 1): "sum_c", (3, 0): "sum_early", (3, 1): "sum_a"}
+        early_sums = work.tile([P, PACK, LAST * CHUNK], F32, name="early_sums", tag="sum_early")
+        for c in range(LAST):
+            x_sums[c, 0] = early_sums[:, :, c * CHUNK : (c + 1) * CHUNK]
+        half = LAST * CHUNK // 2
+
+        def gather_early(t):
+            pieces = [(t, u * half, early_sums[:, t, u * half : (u + 1) * half]) for u in range(2)]
+            gather_pieces(pieces, [picked_tile[:, 0:half], picked_tile[:, half : 2 * half]])
+
+        def interleave(copy, dst, src):
+            copy(out=dst.rearrange("p (j t) -> p j t", t=PACK), in_=src.rearrange("p t j -> p j t"))
+
+        mixed_tags = {(0, 1): "x_mixed0", (1, 1): "x_mixed1", (2, 1): "x_mixed2", (3, 0): "x_mixed0", (3, 1): "x_mixed1"}
 
         def mix_x(c, a):
-            x_mixed[c, a] = work.tile(
-                [P, PACK * CHUNK], BF16, name="x_mixed%d%d" % (c, a), tag="x_mixed%d" % (c % LAST), align_bytes=64
-            )
-            interleave(x_mixed[c, a], x_sums[c, a])
+            mixed = work.tile([P, PACK * CHUNK], BF16, name="x_mixed%d%d" % (c, a), tag=mixed_tags[c, a], align_bytes=64)
+            x_mixed[c, a] = mixed[:]
+            interleave(nc.scalar.copy, x_mixed[c, a], x_sums[c, a])
+
+        def mix_early_x():
+            mixed = work.tile([P, LAST * PACK * CHUNK], BF16, name="early_mixed", tag="wide0", align_bytes=64)
+            for c in range(LAST):
+                x_mixed[c, 0] = mixed[:, c * PACK * CHUNK : (c + 1) * PACK * CHUNK]
+                interleave(nc.scalar.copy, x_mixed[c, 0], x_sums[c, 0])
 
         def quantize_x(c, a):
             x_codes[c, a] = work.tile([P, CHUNK], U32, name="x_codes%d%d" % (c, a), tag="xq%d%d" % (c, a), align_bytes=64)
             x_scales[c, a] = keep.tile([P, CHUNK], U8, name="x_scales%d%d" % (c, a), align_bytes=64)
-            nc.vector.quantize_mx(out=x_codes[c, a][:].bitcast(FP8X4), scales=x_scales[c, a][:], in_=x_mixed[c, a][:])
+            nc.vector.quantize_mx(out=x_codes[c, a][:].bitcast(FP8X4), scales=x_scales[c, a][:], in_=x_mixed[c, a])
 
         d_banks = {}
 
@@ -206,7 +232,7 @@ def tile_list_wildfire_spread_rates_kernel(
                             nc.tensor.matmul_mx(
                                 out=bank[:, u * CHUNK + j : u * CHUNK + j + FP4_WIDTH],
                                 lhsT=wf_codes[:, 2 * (a * H + col) : 2 * (a * H + col + P)].bitcast(FP4X4),
-                                lhsT_scale=wf_planes[a][:, col : col + P],
+                                lhsT_scale=wf_planes[:, a * H + col : a * H + col + P],
                                 rhs=v_codes[a][:, cols].bitcast(FP8X4),
                                 rhs_scale=v_scales[a][:, cols],
                                 start=(a == 0 and u == 0 and j == 0),
@@ -235,7 +261,7 @@ def tile_list_wildfire_spread_rates_kernel(
 
         def evacuate_d(c, b):
             if c not in d_sbuf:
-                d_sbuf[c] = work.tile([P, PACK * K_PASS], F32, name="d_sbuf%d" % c, tag="wide", bufs=2)
+                d_sbuf[c] = work.tile([P, PACK * K_PASS], F32, name="d_sbuf%d" % c, tag="wide%d" % ((c + 1) % 3), align_bytes=64)
             for pair in range(2):
                 first = (2 * b + pair) * 2 * CHUNK
                 nc.scalar.copy(out=d_sbuf[c][:, first : first + 2 * CHUNK], in_=d_banks[c, b, pair][:])
@@ -258,11 +284,11 @@ def tile_list_wildfire_spread_rates_kernel(
                     h_planes[c, b][:, t, :], src, lo_cols[:, b, t : t + 1], hi_cols[:, b, t : t + 1], MAX, MIN
                 )
 
-        def mix_h(c, b):
+        def mix_h(c, b, copy=nc.scalar.copy):
             h_mixed[c, b] = work.tile(
                 [P, PACK * CHUNK], BF16, name="h_mixed%d%d" % (c, b), tag="h_mixed%d%d" % (c % 2, b), align_bytes=64
             )
-            interleave(h_mixed[c, b], h_planes[c, b])
+            interleave(copy, h_mixed[c, b][:], h_planes[c, b][:])
 
         def quantize_h(c, b):
             h_codes[c, b] = work.tile(
@@ -302,26 +328,28 @@ def tile_list_wildfire_spread_rates_kernel(
                 nc.sync.dma_start(out=rows.rearrange("(n p) j -> p n j", p=P), in_=result[:])
 
         early = range(LAST)
+        gather_early(0)
+        gather_early(1)
         nc.vector.tensor_copy(v_scales[0][:], tab_bytes[:].indirect(fuel_list[:]))
         shift_second_pass(v_scales)
-        gather_x([(0, c) for c in early], picked)
-        gather_x([(1, c) for c in early], picked)
-        reorder_wf()
-        gather_x([(2, c) for c in early], picked)
+        cast_wx(0, 0)
+        gather_early(2)
         quantize_wx(0, 0)
-        gather_x([(3, c) for c in early], picked)
+        cast_wx(1, 0)
+        gather_early(3)
         quantize_wx(1, 0)
+        cast_wx(0, 1)
+        reorder_wf()
+        gather_x([(4, c) for c in early], [picked[0], picked[1], scratch("wq01")])
         quantize_wx(0, 1)
-        for c in early:
-            mix_x(c, 0)
-        gather_x([(4, c) for c in early], [picked[0], picked[1], scratch("xq00")])
-        quantize_x(0, 0)
-        gather_x([(5, c) for c in early], [picked[0], scratch("xq10"), scratch("xq20")])
-        quantize_x(1, 0)
-        quantize_x(2, 0)
+        cast_wx(1, 1)
+        mix_early_x()
+        gather_x([(5, c) for c in early], [picked[0], picked[1], scratch("wq11")])
         quantize_wx(1, 1)
         for a in range(PASSES):
             nc.vector.tensor_copy(v_codes[a][:], tab_codes[a][:].indirect(fuel_list[:]))
+        for c in early:
+            quantize_x(c, 0)
         d_fuel_and_first_x(0, 0)
         d_fuel_and_first_x(0, 1)
         d_fuel_and_first_x(1, 0)
@@ -385,11 +413,12 @@ def tile_list_wildfire_spread_rates_kernel(
         quantize_x(3, 1)
         d_last_pass(3, 0)
         d_last_pass(3, 1)
+        evacuate_d(3, 1)
         finish(2)
         clamp(3, 0, True)
         mix_h(3, 0)
-        clamp(3, 1, True)
-        mix_h(3, 1)
+        clamp(3, 1, False)
+        mix_h(3, 1, nc.vector.tensor_copy)
         quantize_h(3, 0)
         quantize_h(3, 1)
         y_product(3)

@@ -22,12 +22,12 @@ P = 128
 PACK = 4
 K_PASS = P * PACK
 PASSES = K // K_PASS
-CHUNK = 256
-CHUNKS = S // CHUNK
-LAST = CHUNKS - 1
+BANK = 512
+WIDTHS = (512, 256, 256)
+STARTS = (0, 512, 768)
+NARROW = 256
 LIST_ROWS = 16
 FP4_WIDTH = 128
-SHIFT_ROWS = 112
 N_TILES = N // P
 
 
@@ -47,20 +47,34 @@ def tile_list_wildfire_spread_rates_kernel(
         tab_codes = [keep.tile([P, T], U32, name="tab_codes%d" % a) for a in range(PASSES)]
         tab_bytes = keep.tile([P, T], U8, name="tab_bytes")
         v_codes = [keep.tile([P, S], U32, name="v_codes%d" % a, align_bytes=64) for a in range(PASSES)]
-        v_scales = [keep.tile([P, S], U8, name="v_scales%d" % a, align_bytes=64) for a in range(PASSES)]
+        v_rows = keep.tile([P, S], U8, name="v_rows")
+        v_planes = keep.tile([P, PASSES * S], U8, name="v_planes", align_bytes=64)
         wf_raw = keep.tile([P, PASSES * H], U16, name="wf_raw")
         wf_codes = keep.tile([P, PASSES * H * 2], U8, name="wf_codes", align_bytes=64)
-        wf_raw_scales = keep.tile([P, PASSES * H], U8, name="wf_raw_scales")
+        wf_raw_scales = keep.tile([P, H], U8, name="wf_raw_scales")
+        wf_rows = keep.tile([P, H], U8, name="wf_rows")
         wf_planes = keep.tile([P, PASSES * H], U8, name="wf_planes", align_bytes=64)
         wr_codes = keep.tile([P, PASSES, N], U32, name="wr_codes", align_bytes=64)
         wr_planes = keep.tile([P, N], U8, name="wr_planes", align_bytes=64)
         lo_cols = keep.tile([P, PASSES, PACK], F32, name="lo_cols")
         hi_cols = keep.tile([P, PASSES, PACK], F32, name="hi_cols")
-        picked_tile = keep.tile([P, LAST * CHUNK], F32, name="picked")
-        picked = [picked_tile[:, c * CHUNK : (c + 1) * CHUNK] for c in range(LAST)]
+        picked = keep.tile([P, BANK + NARROW], F32, name="picked")
 
-        for plane in (tab_bytes, wf_raw_scales, v_scales[1], wr_planes):
+        for rows in (tab_bytes, wf_raw_scales):
+            nc.vector.memset(rows[32:64, :].bitcast(I32), 0)
+            nc.vector.memset(rows[64:P, :].bitcast(I32), 0)
+        for plane in (v_planes, wf_planes, wr_planes):
             nc.vector.memset(plane[:].bitcast(I32), 0)
+
+        def load_rows(rows, scales):
+            nc.sync.dma_start(out=rows[0:32, :].bitcast(I32), in_=scales.bitcast(I32).rearrange("a q c -> q a c"))
+
+        def spread_rows(planes, rows):
+            for q in range(4):
+                nc.sync.dma_start(
+                    out=planes[32 * q : 32 * q + 4, :].bitcast(I32).rearrange("r (a c) -> r a c", a=PASSES),
+                    in_=rows[8 * q : 8 * q + 8, :].bitcast(I32),
+                )
 
         def load_scale_rows(plane, scales):
             for q in range(4):
@@ -88,33 +102,36 @@ def tile_list_wildfire_spread_rates_kernel(
                 out=tab_codes[a][:].bitcast(I32), in_=tab_words[a].rearrange("p t i -> p (t i)").bitcast(I32)
             )
 
-        slope_cols = [work.tile([P, N_TILES, CHUNK], F32, name="slope%d" % c, tag="slope%d" % c) for c in range(CHUNKS)]
+        slope_cols = [keep.tile([P, N_TILES, w], F32, name="slope%d" % c) for c, w in enumerate(WIDTHS)]
 
+        nc.sync.dma_start(fuel_list[:], offs)
+        load_rows(tab_bytes, tab_scales)
+        load_rows(wf_raw_scales, wf_scales)
         load_x_plane(0)
         nc.sync.dma_start(upwind_list[:], offs2)
         nc.sync.dma_start(downwind_list[:], offs3)
-        nc.sync.dma_start(fuel_list[:], offs)
-        load_scale_rows(tab_bytes, tab_scales)
+        nc.vector.tensor_copy(v_rows[:], tab_bytes[:].indirect(fuel_list[:]))
+        nc.vector.tensor_copy(
+            out=wf_rows[:].rearrange("p (b t m) -> p b t m", t=PACK, m=P),
+            in_=wf_raw_scales[:].rearrange("p (b m t) -> p b t m", t=PACK, m=P),
+        )
         load_x_plane(1)
         load_wx(0, 0)
         load_x_plane(2)
         load_wx(1, 0)
         load_x_plane(3)
-        load_wx(0, 1)
         nc.sync.dma_start(
             out=wf_raw[:].bitcast(I32).rearrange("p (a c) -> p a c", a=PASSES),
             in_=wf_words.bitcast(I32).rearrange("a p c -> p a c"),
         )
-        for q in range(4):
-            nc.sync.dma_start(
-                out=wf_raw_scales[32 * q : 32 * q + 4, :].bitcast(I32).rearrange("r (a c) -> r a c", a=PASSES),
-                in_=wf_scales[:, 4 * q : 4 * q + 4, :].bitcast(I32).rearrange("a r c -> r a c"),
-            )
         load_x_plane(4)
-        load_wx(1, 1)
+        spread_rows(v_planes, v_rows)
         load_x_plane(5)
+        load_wx(0, 1)
         load_tab(0)
+        spread_rows(wf_planes, wf_rows)
         load_tab(1)
+        load_wx(1, 1)
         load_x_plane(6)
         load_x_plane(7)
         nc.sync.dma_start(out=lo_cols[:], in_=lo.rearrange("(b p t) -> p b t", b=PASSES, t=PACK))
@@ -123,14 +140,9 @@ def tile_list_wildfire_spread_rates_kernel(
             out=wr_codes[:].bitcast(I32), in_=wr_words.rearrange("a p c i -> p a (c i)").bitcast(I32)
         )
         load_scale_rows(wr_planes, wr_scales)
-        for c in range(CHUNKS):
+        for c, w in enumerate(WIDTHS):
             nc.sync.dma_start(
-                out=slope_cols[c][:], in_=slope[:, c * CHUNK : (c + 1) * CHUNK].rearrange("(n p) j -> p n j", p=P)
-            )
-
-        def shift_second_pass(planes):
-            nc.scalar.dma_start(
-                out=planes[1][0:SHIFT_ROWS, :].bitcast(I32), in_=planes[0][4 : 4 + SHIFT_ROWS, :].bitcast(I32)
+                out=slope_cols[c][:], in_=slope[:, STARTS[c] : STARTS[c] + w].rearrange("(n p) j -> p n j", p=P)
             )
 
         wx_codes = {}
@@ -139,7 +151,7 @@ def tile_list_wildfire_spread_rates_kernel(
         wx_grouped = {}
 
         def cast_wx(a, b):
-            grouped = work.tile([P, PACK * K_PASS], BF16, name="wx_bf%d%d" % (a, b), tag="wx_bf", bufs=2, align_bytes=64)
+            grouped = work.tile([P, PACK * K_PASS], BF16, name="wx_bf%d%d" % (a, b), tag="half%d" % a, align_bytes=64)
             nc.scalar.copy(
                 out=grouped[:].rearrange("p (t m i) -> p t m i", t=PACK, i=PACK),
                 in_=wx_raw[a, b][:].rearrange("p (i m t) -> p t m i", i=PACK, t=PACK),
@@ -157,269 +169,253 @@ def tile_list_wildfire_spread_rates_kernel(
                 out=wf_codes[:].bitcast(U16).rearrange("p (g t m) -> p g t m", t=PACK, m=P),
                 in_=wf_raw[:].rearrange("p (g m t) -> p g t m", t=PACK, m=P),
             )
-            nc.vector.tensor_copy(
-                out=wf_planes[:].rearrange("p (g t m) -> p g t m", t=PACK, m=P),
-                in_=wf_raw_scales[:].rearrange("p (g m t) -> p g t m", t=PACK, m=P),
-            )
 
         x_sums = {}
         x_mixed = {}
         x_codes = {}
         x_scales = {}
+        sum_tags = {(0, 0): "sum00", (0, 1): "sum01", (1, 0): "sum0", (1, 1): "sum1", (2, 0): "sum0", (2, 1): "sum1"}
+        mixed_tags = {(0, 0): "mixed0", (0, 1): "mixed0", (1, 0): "mixed1", (1, 1): "mixed2", (2, 0): "mixed1", (2, 1): "mixed2"}
 
-        def scratch(tag):
-            buf = work.tile([P, CHUNK], F32, name="scratch_" + tag, tag=tag, align_bytes=64)
-            return buf[:]
-
-        def gather_pieces(pieces, buffers):
-            for (i, first, dest), buf in zip(pieces, buffers):
-                cols = slice(first // LIST_ROWS, (first + dest.shape[1]) // LIST_ROWS)
-                nc.vector.tensor_copy(buf, x_planes[i][:].indirect(upwind_list[:, cols]))
-            for (i, first, dest), buf in zip(pieces, buffers):
-                cols = slice(first // LIST_ROWS, (first + dest.shape[1]) // LIST_ROWS)
-                nc.vector.tensor_tensor(dest, x_planes[i][:].indirect(downwind_list[:, cols]), buf, ADD)
-
-        def gather_x(pieces, buffers):
-            for i, c in pieces:
-                a = i // PACK
+        def gather_x(pieces, spare):
+            first = 0
+            jobs = []
+            for i, c, j, width in pieces:
+                a, t = divmod(i, PACK)
                 if (c, a) not in x_sums:
-                    sums = work.tile([P, PACK, CHUNK], F32, name="x_sum%d%d" % (c, a), tag=sum_tags[c, a])
-                    x_sums[c, a] = sums[:]
-            gather_pieces([(i, c * CHUNK, x_sums[c, i // PACK][:, i % PACK, :]) for i, c in pieces], buffers)
+                    x_sums[c, a] = work.tile(
+                        [P, PACK, WIDTHS[c]], F32, name="x_sum%d%d" % (c, a), tag=sum_tags[c, a], align_bytes=64
+                    )
+                cols = slice((STARTS[c] + j) // LIST_ROWS, (STARTS[c] + j + width) // LIST_ROWS)
+                jobs.append((x_planes[i], cols, spare[:, first : first + width], x_sums[c, a][:, t, j : j + width]))
+                first = first + width
+            for plane, cols, upwind, total in jobs:
+                nc.vector.tensor_copy(upwind, plane[:].indirect(upwind_list[:, cols]))
+            for plane, cols, upwind, total in jobs:
+                nc.vector.tensor_tensor(total, plane[:].indirect(downwind_list[:, cols]), upwind, ADD)
 
-        sum_tags = {(0, 1): "sum_a", (1, 1): "sum_b", (2, 1): "sum_c", (3, 0): "sum_early", (3, 1): "sum_a"}
-        early_sums = work.tile([P, PACK, LAST * CHUNK], F32, name="early_sums", tag="sum_early")
-        for c in range(LAST):
-            x_sums[c, 0] = early_sums[:, :, c * CHUNK : (c + 1) * CHUNK]
-        half = LAST * CHUNK // 2
+        def gather_plane(i):
+            gather_x([(i, 0, 0, BANK), (i, 1, 0, NARROW)], picked[:])
 
-        def gather_early(t):
-            pieces = [(t, u * half, early_sums[:, t, u * half : (u + 1) * half]) for u in range(2)]
-            gather_pieces(pieces, [picked_tile[:, 0:half], picked_tile[:, half : 2 * half]])
+        def gather_halves(i):
+            gather_x([(i, 0, 0, NARROW), (i, 0, NARROW, NARROW)], picked[:])
+
+        def gather_pair(c, i, spare):
+            gather_x([(i, c, 0, NARROW), (i + 1, c, 0, NARROW)], spare)
 
         def interleave(copy, dst, src):
             copy(out=dst.rearrange("p (j t) -> p j t", t=PACK), in_=src.rearrange("p t j -> p j t"))
 
-        mixed_tags = {(0, 1): "x_mixed0", (1, 1): "x_mixed1", (2, 1): "x_mixed2", (3, 0): "x_mixed0", (3, 1): "x_mixed1"}
-
-        def mix_x(c, a):
-            mixed = work.tile([P, PACK * CHUNK], BF16, name="x_mixed%d%d" % (c, a), tag=mixed_tags[c, a], align_bytes=64)
+        def mix_x(c, a, step):
+            mixed = work.tile([P, PACK * WIDTHS[c]], BF16, name="x_mixed%d%d" % (c, a), tag=mixed_tags[c, a], align_bytes=64)
             x_mixed[c, a] = mixed[:]
-            interleave(nc.scalar.copy, x_mixed[c, a], x_sums[c, a])
+            for j in range(0, WIDTHS[c], step):
+                interleave(nc.scalar.copy, mixed[:, PACK * j : PACK * (j + step)], x_sums[c, a][:, :, j : j + step])
 
-        def mix_early_x():
-            mixed = work.tile([P, LAST * PACK * CHUNK], BF16, name="early_mixed", tag="wide0", align_bytes=64)
-            for c in range(LAST):
-                x_mixed[c, 0] = mixed[:, c * PACK * CHUNK : (c + 1) * PACK * CHUNK]
-                interleave(nc.scalar.copy, x_mixed[c, 0], x_sums[c, 0])
-
-        def quantize_x(c, a):
-            x_codes[c, a] = work.tile([P, CHUNK], U32, name="x_codes%d%d" % (c, a), tag="xq%d%d" % (c, a), align_bytes=64)
-            x_scales[c, a] = keep.tile([P, CHUNK], U8, name="x_scales%d%d" % (c, a), align_bytes=64)
-            nc.vector.quantize_mx(out=x_codes[c, a][:].bitcast(FP8X4), scales=x_scales[c, a][:], in_=x_mixed[c, a])
+        def quantize_x(c, a, step):
+            w = WIDTHS[c]
+            x_codes[c, a] = work.tile([P, w], U32, name="x_codes%d%d" % (c, a), tag="xq%d%d" % (c, a), align_bytes=64)
+            x_scales[c, a] = keep.tile([P, w], U8, name="x_scales%d%d" % (c, a), align_bytes=64)
+            for j in range(0, w, step):
+                nc.vector.quantize_mx(
+                    out=x_codes[c, a][:, j : j + step].bitcast(FP8X4),
+                    scales=x_scales[c, a][:, j : j + step],
+                    in_=x_mixed[c, a][:, PACK * j : PACK * (j + step)],
+                )
 
         d_banks = {}
+        d_bank_ids = {(0, 0): (0, 1, 2, 3), (0, 1): (4, 5, 6, 7), (1, 0): (0, 1), (1, 1): (2, 3), (2, 0): (7, 0), (2, 1): (1, 2)}
+        y_bank_ids = {0: (4, 5, 6), 1: (3, 4), 2: (5, 6)}
 
-        def d_fuel_and_first_x(c, b):
-            for pair in range(2):
-                bank = psum.tile([P, 2 * CHUNK], F32, name="d%d%d%d" % (c, b, pair), tag="d", bufs=6)
-                d_banks[c, b, pair] = bank
-                for a in range(PASSES):
-                    for u in range(2):
-                        col = b * K_PASS + (2 * pair + u) * P
-                        for j in range(0, CHUNK, FP4_WIDTH):
-                            cols = slice(c * CHUNK + j, c * CHUNK + j + FP4_WIDTH)
-                            nc.tensor.matmul_mx(
-                                out=bank[:, u * CHUNK + j : u * CHUNK + j + FP4_WIDTH],
-                                lhsT=wf_codes[:, 2 * (a * H + col) : 2 * (a * H + col + P)].bitcast(FP4X4),
-                                lhsT_scale=wf_planes[:, a * H + col : a * H + col + P],
-                                rhs=v_codes[a][:, cols].bitcast(FP8X4),
-                                rhs_scale=v_scales[a][:, cols],
-                                start=(a == 0 and u == 0 and j == 0),
-                                stop=False,
-                            )
-                d_x_pass(c, b, pair, 0)
+        def bank_tile(number, name):
+            return psum.tile([P, BANK], F32, name=name, tag="bank%d" % number)
 
-        def d_x_pass(c, b, pair, a):
-            for u in range(2):
-                cols = slice((2 * pair + u) * P, (2 * pair + u + 1) * P)
+        def d_view(c, b, t):
+            w = WIDTHS[c]
+            k, u = divmod(t, BANK // w)
+            return d_banks[c, b, k][:, u * w : (u + 1) * w]
+
+        def d_x_pass(c, b, k, a):
+            per_bank = BANK // WIDTHS[c]
+            for t in range(k * per_bank, (k + 1) * per_bank):
+                cols = slice(t * P, (t + 1) * P)
                 nc.tensor.matmul_mx(
-                    out=d_banks[c, b, pair][:, u * CHUNK : (u + 1) * CHUNK],
+                    out=d_view(c, b, t),
                     lhsT=wx_codes[a, b][:, cols].bitcast(FP8X4),
                     lhsT_scale=wx_scales[a, b][:, cols],
                     rhs=x_codes[c, a][:].bitcast(FP8X4),
                     rhs_scale=x_scales[c, a][:],
                     start=False,
-                    stop=(a == PASSES - 1 and u == 1),
+                    stop=(a == PASSES - 1 and t == (k + 1) * per_bank - 1),
                 )
 
-        def d_last_pass(c, b):
-            for pair in range(2):
-                d_x_pass(c, b, pair, PASSES - 1)
+        def d_fuel(c, b):
+            w = WIDTHS[c]
+            per_bank = BANK // w
+            step = BANK if w == BANK else FP4_WIDTH
+            for k, number in enumerate(d_bank_ids[c, b]):
+                d_banks[c, b, k] = bank_tile(number, "d%d%d%d" % (c, b, k))
+                for a in range(PASSES):
+                    for t in range(k * per_bank, (k + 1) * per_bank):
+                        col = a * H + b * K_PASS + t * P
+                        for j in range(0, w, step):
+                            first = STARTS[c] + j
+                            nc.tensor.matmul_mx(
+                                out=d_view(c, b, t)[:, j : j + step],
+                                lhsT=wf_codes[:, 2 * col : 2 * (col + P)].bitcast(FP4X4),
+                                lhsT_scale=wf_planes[:, col : col + P],
+                                rhs=v_codes[a][:, first : first + step].bitcast(FP8X4),
+                                rhs_scale=v_planes[:, a * S + first : a * S + first + step],
+                                start=(a == 0 and t == k * per_bank and j == 0),
+                                stop=False,
+                            )
+
+        def d_x(c, b, a):
+            for k in range(len(d_bank_ids[c, b])):
+                d_x_pass(c, b, k, a)
 
         d_sbuf = {}
+        d_tags = {(0, 0): "wide1", (0, 1): "wide2", (1, 0): "wide0", (1, 1): "sum01", (2, 1): "wide1"}
 
         def evacuate_d(c, b):
-            if c not in d_sbuf:
-                d_sbuf[c] = work.tile([P, PACK * K_PASS], F32, name="d_sbuf%d" % c, tag="wide%d" % ((c + 1) % 3), align_bytes=64)
-            for pair in range(2):
-                first = (2 * b + pair) * 2 * CHUNK
-                nc.scalar.copy(out=d_sbuf[c][:, first : first + 2 * CHUNK], in_=d_banks[c, b, pair][:])
+            d_sbuf[c, b] = work.tile(
+                [P, PACK * WIDTHS[c]], F32, name="d_sbuf%d%d" % (c, b), tag=d_tags[c, b], align_bytes=64
+            )
+            for k in range(len(d_bank_ids[c, b])):
+                nc.scalar.copy(out=d_sbuf[c, b][:, k * BANK : (k + 1) * BANK], in_=d_banks[c, b, k][:])
 
         h_planes = {}
         h_mixed = {}
         h_codes = {}
         h_scales = {}
 
-        def clamp(c, b, from_psum):
-            h_planes[c, b] = work.tile(
-                [P, PACK, CHUNK], BF16, name="h_planes%d%d" % (c, b), tag="h_planes%d%d" % (c % 2, b), align_bytes=64
-            )
+        def clamp(c, b):
+            w = WIDTHS[c]
+            tag = "h_planes%d" % b if c == 1 else "half%d" % b
+            h_planes[c, b] = work.tile([P, PACK, w], BF16, name="h_planes%d%d" % (c, b), tag=tag, align_bytes=64)
             for t in range(PACK):
-                if from_psum:
-                    src = d_banks[c, b, t // 2][:, (t % 2) * CHUNK : (t % 2 + 1) * CHUNK]
-                else:
-                    src = d_sbuf[c][:, (PACK * b + t) * CHUNK : (PACK * b + t + 1) * CHUNK]
+                src = d_sbuf[c, b][:, t * w : (t + 1) * w] if (c, b) in d_sbuf else d_view(c, b, t)
                 nc.vector.tensor_scalar(
                     h_planes[c, b][:, t, :], src, lo_cols[:, b, t : t + 1], hi_cols[:, b, t : t + 1], MAX, MIN
                 )
 
-        def mix_h(c, b, copy=nc.scalar.copy):
+        def mix_h(c, b, copy):
             h_mixed[c, b] = work.tile(
-                [P, PACK * CHUNK], BF16, name="h_mixed%d%d" % (c, b), tag="h_mixed%d%d" % (c % 2, b), align_bytes=64
+                [P, PACK * WIDTHS[c]], BF16, name="h_mixed%d%d" % (c, b), tag="h_mixed%d%d" % (c % 2, b), align_bytes=64
             )
             interleave(copy, h_mixed[c, b][:], h_planes[c, b][:])
 
-        def quantize_h(c, b):
-            h_codes[c, b] = work.tile(
-                [P, CHUNK], U32, name="h_codes%d%d" % (c, b), tag="h_codes%d%d" % (c % 2, b), align_bytes=64
-            )
-            h_scales[c, b] = work.tile(
-                [P, CHUNK], U8, name="h_scales%d%d" % (c, b), tag="h_scales%d%d" % (c % 2, b), align_bytes=64
-            )
-            nc.vector.quantize_mx(out=h_codes[c, b][:].bitcast(FP8X4), scales=h_scales[c, b][:], in_=h_mixed[c, b][:])
-
         y_banks = {}
 
-        def y_product(c):
-            for first in range(0, N_TILES, 2):
-                count = min(2, N_TILES - first)
-                bank = psum.tile([P, count, CHUNK], F32, name="y%d%d" % (c, first), tag="y%d" % first)
-                y_banks[c, first] = bank
-                for u in range(count):
-                    cols = slice((first + u) * P, (first + u + 1) * P)
-                    for b in range(PASSES):
-                        nc.tensor.matmul_mx(
-                            out=bank[:, u, :],
-                            lhsT=wr_codes[:, b, cols].bitcast(FP8X4),
-                            lhsT_scale=wr_planes[4 * b : P, cols],
-                            rhs=h_codes[c, b][:].bitcast(FP8X4),
-                            rhs_scale=h_scales[c, b][:],
-                            start=(b == 0),
-                            stop=(b == PASSES - 1),
-                        )
+        def quantize_h_and_multiply(c, b):
+            w = WIDTHS[c]
+            tag = "mixed2" if (c, b) == (1, 0) else "h_codes%d%d" % (c % 2, b)
+            codes = work.tile([P, w], U32, name="h_codes%d%d" % (c, b), tag=tag, align_bytes=64)
+            tag = "sum1" if (c, b) == (1, 1) else "h_scales%d%d" % (c % 2, b)
+            scales = work.tile([P, w], U8, name="h_scales%d%d" % (c, b), tag=tag, align_bytes=64)
+            nc.vector.quantize_mx(out=codes[:].bitcast(FP8X4), scales=scales[:], in_=h_mixed[c, b][:])
+            per_bank = BANK // w
+            for n in range(N_TILES):
+                k, u = divmod(n, per_bank)
+                if b == 0 and u == 0:
+                    y_banks[c, k] = bank_tile(y_bank_ids[c][k], "y%d%d" % (c, k))
+                cols = slice(n * P, (n + 1) * P)
+                nc.tensor.matmul_mx(
+                    out=y_banks[c, k][:, u * w : (u + 1) * w],
+                    lhsT=wr_codes[:, b, cols].bitcast(FP8X4),
+                    lhsT_scale=wr_planes[4 * b : P, cols],
+                    rhs=codes[:].bitcast(FP8X4),
+                    rhs_scale=scales[:],
+                    start=(b == 0 and u == 0),
+                    stop=(b == PASSES - 1 and (u == per_bank - 1 or n == N_TILES - 1)),
+                )
 
         def finish(c):
-            for first in range(0, N_TILES, 2):
-                count = min(2, N_TILES - first)
-                result = work.tile([P, count, CHUNK], F32, name="res%d%d" % (c, first), tag="res%d%d" % (c % 2, first))
-                nc.vector.tensor_tensor(result[:], y_banks[c, first][:], slope_cols[c][:, first : first + count, :], MULT)
-                rows = out[first * P : (first + count) * P, c * CHUNK : (c + 1) * CHUNK]
-                nc.sync.dma_start(out=rows.rearrange("(n p) j -> p n j", p=P), in_=result[:])
+            w = WIDTHS[c]
+            per_bank = BANK // w
+            result = work.tile([P, N_TILES, w], F32, name="result%d" % c, tag=("sum01", "h_mixed00", "sum00")[c], align_bytes=64)
+            for k in range(len(y_bank_ids[c])):
+                tiles = slice(k * per_bank, min((k + 1) * per_bank, N_TILES))
+                count = tiles.stop - tiles.start
+                sums = y_banks[c, k][:, 0 : count * w].rearrange("p (n j) -> p n j", n=count)
+                nc.vector.tensor_tensor(result[:, tiles, :], sums, slope_cols[c][:, tiles, :], MULT)
+                rows = out[tiles.start * P : tiles.stop * P, STARTS[c] : STARTS[c] + w]
+                nc.sync.dma_start(out=rows.rearrange("(n p) j -> p n j", p=P), in_=result[:, tiles, :])
 
-        early = range(LAST)
-        gather_early(0)
-        gather_early(1)
-        nc.vector.tensor_copy(v_scales[0][:], tab_bytes[:].indirect(fuel_list[:]))
-        shift_second_pass(v_scales)
+        def as_spare(mixed):
+            return mixed[:, 0 : 2 * BANK].bitcast(F32)
+
+        gather_plane(0)
+        gather_plane(1)
         cast_wx(0, 0)
-        gather_early(2)
+        gather_plane(2)
         quantize_wx(0, 0)
         cast_wx(1, 0)
-        gather_early(3)
+        gather_plane(3)
         quantize_wx(1, 0)
-        cast_wx(0, 1)
+        mix_x(0, 0, BANK)
+        mix_x(1, 0, NARROW)
         reorder_wf()
-        gather_x([(4, c) for c in early], [picked[0], picked[1], scratch("wq01")])
-        quantize_wx(0, 1)
-        cast_wx(1, 1)
-        mix_early_x()
-        gather_x([(5, c) for c in early], [picked[0], picked[1], scratch("wq11")])
-        quantize_wx(1, 1)
+        gather_halves(4)
+        cast_wx(0, 1)
+        gather_halves(5)
+        quantize_x(0, 0, BANK)
+        quantize_x(1, 0, NARROW)
         for a in range(PASSES):
             nc.vector.tensor_copy(v_codes[a][:], tab_codes[a][:].indirect(fuel_list[:]))
-        for c in early:
-            quantize_x(c, 0)
-        d_fuel_and_first_x(0, 0)
-        d_fuel_and_first_x(0, 1)
-        d_fuel_and_first_x(1, 0)
-
-        gather_x([(6, 0), (7, 0)], picked)
-        mix_x(0, 1)
-        gather_x([(6, 1), (7, 1)], [picked[0], scratch("xq01")])
-        mix_x(1, 1)
-        quantize_x(0, 1)
-        d_last_pass(0, 0)
-        d_last_pass(0, 1)
-        evacuate_d(0, 0)
-        evacuate_d(0, 1)
-        gather_x([(6, 2), (7, 2)], [scratch("x_mixed0"), scratch("xq11")])
-        mix_x(2, 1)
-        quantize_x(1, 1)
-        d_last_pass(1, 0)
-        d_fuel_and_first_x(1, 1)
-        d_last_pass(1, 1)
-        d_fuel_and_first_x(2, 0)
-        clamp(0, 0, False)
-        clamp(0, 1, False)
-        mix_h(0, 0)
-        mix_h(0, 1)
-        evacuate_d(1, 0)
-        evacuate_d(1, 1)
-        gather_x([(0, 3), (1, 3)], [d_sbuf[0][:, 1792:2048], scratch("xq21")])
-        quantize_x(2, 1)
-        d_last_pass(2, 0)
-        d_fuel_and_first_x(2, 1)
-        d_last_pass(2, 1)
-        gather_x([(2, 3), (3, 3)], [scratch("x_mixed2"), d_sbuf[0][:, 1536:1792]])
-        mix_x(3, 0)
-        quantize_h(0, 0)
-        quantize_h(0, 1)
-        y_product(0)
-        clamp(1, 0, False)
-        clamp(1, 1, False)
+        quantize_wx(0, 1)
+        cast_wx(1, 1)
+        for b in range(PASSES):
+            d_fuel(0, b)
+            d_x(0, b, 0)
+        gather_halves(6)
+        gather_halves(7)
+        mix_x(0, 1, BANK)
+        gather_pair(1, 4, picked[:])
+        quantize_wx(1, 1)
+        quantize_x(0, 1, BANK)
+        for b in range(PASSES):
+            d_x(0, b, 1)
+            evacuate_d(0, b)
+            d_fuel(1, b)
+            d_x(1, b, 0)
+        gather_pair(1, 6, as_spare(x_mixed[0, 1]))
+        mix_x(1, 1, NARROW)
+        gather_pair(2, 0, as_spare(x_mixed[0, 1]))
+        clamp(0, 0)
+        mix_h(0, 0, nc.scalar.copy)
+        quantize_x(1, 1, NARROW)
+        clamp(0, 1)
+        mix_h(0, 1, nc.scalar.copy)
+        for b in range(PASSES):
+            d_x(1, b, 1)
+            evacuate_d(1, b)
+            d_fuel(2, b)
+        gather_pair(2, 2, d_sbuf[0, 1][:, 2 * BANK : 3 * BANK])
+        mix_x(2, 0, NARROW)
+        quantize_h_and_multiply(0, 0)
+        gather_pair(2, 4, as_spare(h_mixed[0, 0][:]))
+        quantize_h_and_multiply(0, 1)
+        for b in range(PASSES):
+            clamp(1, b)
+            mix_h(1, b, nc.scalar.copy)
+        gather_pair(2, 6, d_sbuf[1, 1][:, NARROW : NARROW + BANK])
+        mix_x(2, 1, NARROW)
+        quantize_x(2, 0, NARROW)
+        for b in range(PASSES):
+            d_x(2, b, 0)
         finish(0)
-        evacuate_d(2, 0)
+        quantize_x(2, 1, NARROW)
+        for b in range(PASSES):
+            d_x(2, b, 1)
         evacuate_d(2, 1)
-        mix_h(1, 0)
-        mix_h(1, 1)
-        gather_x([(4, 3), (5, 3)], [d_sbuf[1][:, 1792:2048], scratch("xq30")])
-        quantize_x(3, 0)
-        d_fuel_and_first_x(3, 0)
-        d_fuel_and_first_x(3, 1)
-        clamp(2, 0, False)
-        clamp(2, 1, False)
-        mix_h(2, 0)
-        mix_h(2, 1)
-        gather_x([(6, 3), (7, 3)], [d_sbuf[2][:, 1792:2048], d_sbuf[2][:, 1536:1792]])
-        mix_x(3, 1)
-        quantize_h(1, 0)
-        quantize_h(1, 1)
-        y_product(1)
+        clamp(2, 0)
+        mix_h(2, 0, nc.scalar.copy)
+        clamp(2, 1)
+        for b in range(PASSES):
+            quantize_h_and_multiply(1, b)
+        mix_h(2, 1, nc.vector.tensor_copy)
+        quantize_h_and_multiply(2, 0)
+        quantize_h_and_multiply(2, 1)
         finish(1)
-        quantize_h(2, 0)
-        quantize_h(2, 1)
-        y_product(2)
-        quantize_x(3, 1)
-        d_last_pass(3, 0)
-        d_last_pass(3, 1)
-        evacuate_d(3, 1)
         finish(2)
-        clamp(3, 0, True)
-        mix_h(3, 0)
-        clamp(3, 1, False)
-        mix_h(3, 1, nc.vector.tensor_copy)
-        quantize_h(3, 0)
-        quantize_h(3, 1)
-        y_product(3)
-        finish(3)

@@ -23,12 +23,13 @@ PACK = 4
 K_PASS = P * PACK
 PASSES = K // K_PASS
 BANK = 512
-WIDTHS = (512, 256, 256)
-STARTS = (0, 512, 768)
-NARROW = 256
+CHUNK = 256
+CHUNKS = S // CHUNK
 LIST_ROWS = 16
 FP4_WIDTH = 128
 N_TILES = N // P
+D_SLOTS = ((0, 1), (2, 3), (0, 1), (2, 0))
+Y_SLOTS = (3, 3, 1, 3)
 
 
 def tile_list_wildfire_spread_rates_kernel(
@@ -44,21 +45,22 @@ def tile_list_wildfire_spread_rates_kernel(
         upwind_list = keep.tile([P, S // LIST_ROWS], U16, name="upwind_list")
         downwind_list = keep.tile([P, S // LIST_ROWS], U16, name="downwind_list")
         x_planes = [keep.tile([P, T], F32, name="x_plane%d" % i) for i in range(PASSES * PACK)]
-        tab_codes = [keep.tile([P, T], U32, name="tab_codes%d" % a) for a in range(PASSES)]
+        tab_codes = [work.tile([P, T], U32, name="tab_codes%d" % a, tag="tab%d" % a) for a in range(PASSES)]
         tab_bytes = keep.tile([P, T], U8, name="tab_bytes")
-        v_codes = [keep.tile([P, S], U32, name="v_codes%d" % a, align_bytes=64) for a in range(PASSES)]
-        v_rows = keep.tile([P, S], U8, name="v_rows")
+        v_codes = {}
+        v_rows = work.tile([P, S], U8, name="v_rows", tag="v_rows")
         v_planes = keep.tile([P, PASSES * S], U8, name="v_planes", align_bytes=64)
         wf_raw = keep.tile([P, PASSES * H], U16, name="wf_raw")
-        wf_codes = keep.tile([P, PASSES * H * 2], U8, name="wf_codes", align_bytes=64)
         wf_raw_scales = keep.tile([P, H], U8, name="wf_raw_scales")
-        wf_rows = keep.tile([P, H], U8, name="wf_rows")
+        wf_rows = work.tile([P, H], U8, name="wf_rows", tag="wf_rows")
         wf_planes = keep.tile([P, PASSES * H], U8, name="wf_planes", align_bytes=64)
         wr_codes = keep.tile([P, PASSES, N], U32, name="wr_codes", align_bytes=64)
         wr_planes = keep.tile([P, N], U8, name="wr_planes", align_bytes=64)
         lo_cols = keep.tile([P, PASSES, PACK], F32, name="lo_cols")
         hi_cols = keep.tile([P, PASSES, PACK], F32, name="hi_cols")
-        picked = keep.tile([P, BANK + NARROW], F32, name="picked")
+        picked = [work.tile([P, BANK], F32, name="picked%d" % u, tag="picked%d" % u, align_bytes=64) for u in range(2)]
+        wf_codes = keep.tile([P, PASSES * H * 2], U8, name="wf_codes", align_bytes=64)
+        wx_raw = [work.tile([P, PACK * H], F32, name="wx_raw%d" % a, tag="wide%d" % a) for a in range(PASSES)]
 
         for rows in (tab_bytes, wf_raw_scales):
             nc.vector.memset(rows[32:64, :].bitcast(I32), 0)
@@ -88,21 +90,15 @@ def tile_list_wildfire_spread_rates_kernel(
             rows = xT[a * K_PASS : (a + 1) * K_PASS, :].rearrange("(p t) c -> p t c", t=PACK)
             nc.sync.dma_start(out=x_planes[i][:], in_=rows[:, t, :])
 
-        wx_raw = {}
-
-        def load_wx(a, b):
-            wx_raw[a, b] = work.tile([P, PACK * K_PASS], F32, name="wx_raw%d%d" % (a, b), tag="wide%d" % ((2 * b + a) % 3), align_bytes=64)
-            rows = wx[a * K_PASS : (a + 1) * K_PASS, b * K_PASS : (b + 1) * K_PASS]
-            nc.sync.dma_start(
-                out=wx_raw[a, b][:].rearrange("p (i c) -> p i c", i=PACK), in_=rows.rearrange("(p i) c -> p i c", i=PACK)
-            )
+        def load_wx(a, u):
+            rows = wx[a * K_PASS : (a + 1) * K_PASS, :].rearrange("(p i) c -> p (i c)", i=PACK)
+            cols = slice(2 * u * H, 2 * (u + 1) * H)
+            nc.sync.dma_start(out=wx_raw[a][:, cols], in_=rows[:, cols])
 
         def load_tab(a):
             nc.sync.dma_start(
                 out=tab_codes[a][:].bitcast(I32), in_=tab_words[a].rearrange("p t i -> p (t i)").bitcast(I32)
             )
-
-        slope_cols = [keep.tile([P, N_TILES, w], F32, name="slope%d" % c) for c, w in enumerate(WIDTHS)]
 
         nc.sync.dma_start(fuel_list[:], offs)
         load_rows(tab_bytes, tab_scales)
@@ -115,54 +111,50 @@ def tile_list_wildfire_spread_rates_kernel(
             out=wf_rows[:].rearrange("p (b t m) -> p b t m", t=PACK, m=P),
             in_=wf_raw_scales[:].rearrange("p (b m t) -> p b t m", t=PACK, m=P),
         )
-        load_x_plane(1)
-        load_wx(0, 0)
-        load_x_plane(2)
-        load_wx(1, 0)
-        load_x_plane(3)
         nc.sync.dma_start(
             out=wf_raw[:].bitcast(I32).rearrange("p (a c) -> p a c", a=PASSES),
             in_=wf_words.bitcast(I32).rearrange("a p c -> p a c"),
         )
-        load_x_plane(4)
-        spread_rows(v_planes, v_rows)
-        load_x_plane(5)
+        load_x_plane(1)
+        load_wx(0, 0)
         load_wx(0, 1)
+        load_x_plane(2)
+        load_wx(1, 0)
+        load_wx(1, 1)
+        load_x_plane(3)
         load_tab(0)
         spread_rows(wf_planes, wf_rows)
+        spread_rows(v_planes, v_rows)
+        for i in range(PACK, 2 * PACK - 1):
+            load_x_plane(i)
         load_tab(1)
-        load_wx(1, 1)
-        load_x_plane(6)
-        load_x_plane(7)
+        load_x_plane(2 * PACK - 1)
         nc.sync.dma_start(out=lo_cols[:], in_=lo.rearrange("(b p t) -> p b t", b=PASSES, t=PACK))
         nc.sync.dma_start(out=hi_cols[:], in_=hi.rearrange("(b p t) -> p b t", b=PASSES, t=PACK))
         nc.sync.dma_start(
             out=wr_codes[:].bitcast(I32), in_=wr_words.rearrange("a p c i -> p a (c i)").bitcast(I32)
         )
         load_scale_rows(wr_planes, wr_scales)
-        for c, w in enumerate(WIDTHS):
-            nc.sync.dma_start(
-                out=slope_cols[c][:], in_=slope[:, STARTS[c] : STARTS[c] + w].rearrange("(n p) j -> p n j", p=P)
-            )
 
         wx_codes = {}
         wx_scales = {}
-
         wx_grouped = {}
 
         def cast_wx(a, b):
-            grouped = work.tile([P, PACK * K_PASS], BF16, name="wx_bf%d%d" % (a, b), tag="half%d" % a, align_bytes=64)
+            grouped = work.tile([P, PACK * K_PASS], BF16, name="wx_bf%d%d" % (a, b), tag="wx_bf%d%d" % (a, b), align_bytes=64)
+            src = wx_raw[a][:].rearrange("p (i c) -> p i c", i=PACK)[:, :, b * K_PASS : (b + 1) * K_PASS]
             nc.scalar.copy(
-                out=grouped[:].rearrange("p (t m i) -> p t m i", t=PACK, i=PACK),
-                in_=wx_raw[a, b][:].rearrange("p (i m t) -> p t m i", i=PACK, t=PACK),
+                out=grouped[:].rearrange("p (t m i) -> p m t i", t=PACK, i=PACK),
+                in_=src.rearrange("p i (m t) -> p m t i", t=PACK),
             )
             wx_grouped[a, b] = grouped
 
-        def quantize_wx(a, b):
-            grouped = wx_grouped[a, b]
-            wx_codes[a, b] = work.tile([P, K_PASS], U32, name="wx_codes%d%d" % (a, b), tag="wq%d%d" % (a, b), align_bytes=64)
+        def quantize_wx(a, b, codes):
+            wx_codes[a, b] = codes
             wx_scales[a, b] = keep.tile([P, K_PASS], U8, name="wx_scales%d%d" % (a, b), align_bytes=64)
-            nc.vector.quantize_mx(out=wx_codes[a, b][:].bitcast(FP8X4), scales=wx_scales[a, b][:], in_=grouped[:])
+            nc.vector.quantize_mx(
+                out=codes.bitcast(FP8X4), scales=wx_scales[a, b][:], in_=wx_grouped[a, b][:]
+            )
 
         def reorder_wf():
             nc.vector.tensor_copy(
@@ -170,252 +162,285 @@ def tile_list_wildfire_spread_rates_kernel(
                 in_=wf_raw[:].rearrange("p (g m t) -> p g t m", t=PACK, m=P),
             )
 
-        x_sums = {}
-        x_mixed = {}
-        x_codes = {}
-        x_scales = {}
-        sum_tags = {(0, 0): "sum00", (0, 1): "sum01", (1, 0): "sum0", (1, 1): "sum1", (2, 0): "sum0", (2, 1): "sum1"}
-        mixed_tags = {(0, 0): "mixed0", (0, 1): "mixed0", (1, 0): "mixed1", (1, 1): "mixed2", (2, 0): "mixed1", (2, 1): "mixed2"}
-
-        def gather_x(pieces, spare):
-            first = 0
+        def gather_x(pieces):
             jobs = []
-            for i, c, j, width in pieces:
-                a, t = divmod(i, PACK)
-                if (c, a) not in x_sums:
-                    x_sums[c, a] = work.tile(
-                        [P, PACK, WIDTHS[c]], F32, name="x_sum%d%d" % (c, a), tag=sum_tags[c, a], align_bytes=64
-                    )
-                cols = slice((STARTS[c] + j) // LIST_ROWS, (STARTS[c] + j + width) // LIST_ROWS)
-                jobs.append((x_planes[i], cols, spare[:, first : first + width], x_sums[c, a][:, t, j : j + width]))
-                first = first + width
+            for i, j, width, upwind, total in pieces:
+                jobs.append((x_planes[i], slice(j // LIST_ROWS, (j + width) // LIST_ROWS), upwind, total))
             for plane, cols, upwind, total in jobs:
                 nc.vector.tensor_copy(upwind, plane[:].indirect(upwind_list[:, cols]))
             for plane, cols, upwind, total in jobs:
                 nc.vector.tensor_tensor(total, plane[:].indirect(downwind_list[:, cols]), upwind, ADD)
 
-        def gather_plane(i):
-            gather_x([(i, 0, 0, BANK), (i, 1, 0, NARROW)], picked[:])
-
-        def gather_halves(i):
-            gather_x([(i, 0, 0, NARROW), (i, 0, NARROW, NARROW)], picked[:])
-
-        def gather_pair(c, i, spare):
-            gather_x([(i, c, 0, NARROW), (i + 1, c, 0, NARROW)], spare)
-
         def interleave(copy, dst, src):
             copy(out=dst.rearrange("p (j t) -> p j t", t=PACK), in_=src.rearrange("p t j -> p j t"))
 
-        def mix_x(c, a, step):
-            mixed = work.tile([P, PACK * WIDTHS[c]], BF16, name="x_mixed%d%d" % (c, a), tag=mixed_tags[c, a], align_bytes=64)
-            x_mixed[c, a] = mixed[:]
-            for j in range(0, WIDTHS[c], step):
-                interleave(nc.scalar.copy, mixed[:, PACK * j : PACK * (j + step)], x_sums[c, a][:, :, j : j + step])
+        first_sums = [work.tile([P, PACK, BANK], F32, name="first_sums%d" % u, tag="sums%d" % u, align_bytes=64) for u in range(2)]
+        first_mixed = [
+            work.tile([P, PACK * BANK], BF16, name="first_mixed%d" % u, tag="mixed%d" % u, align_bytes=64) for u in range(2)
+        ]
+        first_codes = {}
+        first_scales = keep.tile([P, S], U8, name="first_scales", align_bytes=64)
 
-        def quantize_x(c, a, step):
-            w = WIDTHS[c]
-            x_codes[c, a] = work.tile([P, w], U32, name="x_codes%d%d" % (c, a), tag="xq%d%d" % (c, a), align_bytes=64)
-            x_scales[c, a] = keep.tile([P, w], U8, name="x_scales%d%d" % (c, a), align_bytes=64)
-            for j in range(0, w, step):
-                nc.vector.quantize_mx(
-                    out=x_codes[c, a][:, j : j + step].bitcast(FP8X4),
-                    scales=x_scales[c, a][:, j : j + step],
-                    in_=x_mixed[c, a][:, PACK * j : PACK * (j + step)],
-                )
+        def gather_first(t, spares):
+            gather_x([(t, u * BANK, BANK, spares[u], first_sums[u][:, t, :]) for u in range(2)])
+
+        def mix_first(u):
+            interleave(nc.scalar.copy, first_mixed[u][:], first_sums[u][:])
+
+        def quantize_first(u, tag):
+            first_codes[u] = work.tile([P, BANK], U32, name="first_codes%d" % u, tag=tag, align_bytes=64)
+            cols = slice(u * BANK, (u + 1) * BANK)
+            nc.vector.quantize_mx(
+                out=first_codes[u][:].bitcast(FP8X4), scales=first_scales[:, cols], in_=first_mixed[u][:]
+            )
+
+        x_sums = {}
+        x_sum_tags = ("wx_bf10", "wx_bf11", "mixed0", "mixed1")
+        x_mixed = {}
+        x_codes = {}
+        x_scales = [keep.tile([P, CHUNK], U8, name="x_scales%d" % c, align_bytes=64) for c in range(CHUNKS)]
+
+        def gather_plane(t, spares):
+            gather_x([(PACK + t, c * CHUNK, CHUNK, spares[c], x_sums[c][:, t, :]) for c in range(2)])
+
+        def new_sums(c):
+            x_sums[c] = work.tile([P, PACK, CHUNK], F32, name="x_sums%d" % c, tag=x_sum_tags[c], align_bytes=64)
+
+        def gather_pair(c, t, spares):
+            gather_x([(PACK + t + s, c * CHUNK, CHUNK, spares[s], x_sums[c][:, t + s, :]) for s in range(2)])
+
+        def halves(spare):
+            return [spare[:, s * CHUNK : (s + 1) * CHUNK] for s in range(2)]
+
+        def gather_v(a, u, tag):
+            v_codes[a, u] = work.tile([P, BANK], U32, name="v_codes%d%d" % (a, u), tag=tag, align_bytes=64)
+            cols = slice(u * BANK // LIST_ROWS, (u + 1) * BANK // LIST_ROWS)
+            nc.vector.tensor_copy(v_codes[a, u][:], tab_codes[a][:].indirect(fuel_list[:, cols]))
+
+        def mix_x(c):
+            x_mixed[c] = work.tile(
+                [P, PACK * CHUNK], BF16, name="x_mixed%d" % c, tag=("xm0", "xm1", "xq2", "xq3")[c], align_bytes=64
+            )
+            interleave(nc.scalar.copy, x_mixed[c][:], x_sums[c][:])
+
+        def quantize_x(c):
+            x_codes[c] = work.tile([P, CHUNK], U32, name="x_codes%d" % c, tag="xq%d" % (c + 1), align_bytes=64)
+            nc.vector.quantize_mx(out=x_codes[c][:].bitcast(FP8X4), scales=x_scales[c][:], in_=x_mixed[c][:])
 
         d_banks = {}
-        d_bank_ids = {(0, 0): (0, 1, 2, 3), (0, 1): (4, 5, 6, 7), (1, 0): (0, 1), (1, 1): (2, 3), (2, 0): (7, 0), (2, 1): (1, 2)}
-        y_bank_ids = {0: (4, 5, 6), 1: (3, 4), 2: (5, 6)}
-
-        def bank_tile(number, name):
-            return psum.tile([P, BANK], F32, name=name, tag="bank%d" % number)
+        per_bank = BANK // CHUNK
 
         def d_view(c, b, t):
-            w = WIDTHS[c]
-            k, u = divmod(t, BANK // w)
-            return d_banks[c, b, k][:, u * w : (u + 1) * w]
+            k, u = divmod(t, per_bank)
+            return d_banks[c, b, k][:, u * CHUNK : (u + 1) * CHUNK]
 
-        def d_x_pass(c, b, k, a):
-            per_bank = BANK // WIDTHS[c]
-            for t in range(k * per_bank, (k + 1) * per_bank):
-                cols = slice(t * P, (t + 1) * P)
-                nc.tensor.matmul_mx(
-                    out=d_view(c, b, t),
-                    lhsT=wx_codes[a, b][:, cols].bitcast(FP8X4),
-                    lhsT_scale=wx_scales[a, b][:, cols],
-                    rhs=x_codes[c, a][:].bitcast(FP8X4),
-                    rhs_scale=x_scales[c, a][:],
-                    start=False,
-                    stop=(a == PASSES - 1 and t == (k + 1) * per_bank - 1),
-                )
+        def x_pass(c, b, t, a):
+            cols = slice(t * P, (t + 1) * P)
+            if a == 0:
+                codes, scales = first_codes[c // 2][:, c % 2 * CHUNK : (c % 2 + 1) * CHUNK], first_scales[:, c * CHUNK : (c + 1) * CHUNK]
+            else:
+                codes, scales = x_codes[c][:], x_scales[c][:]
+            nc.tensor.matmul_mx(
+                out=d_view(c, b, t),
+                lhsT=wx_codes[a, b][:, cols].bitcast(FP8X4),
+                lhsT_scale=wx_scales[a, b][:, cols],
+                rhs=codes.bitcast(FP8X4),
+                rhs_scale=scales,
+                start=(a == 0 and t % per_bank == 0),
+                stop=(a == PASSES - 1 and t % per_bank == per_bank - 1),
+            )
 
-        def d_fuel(c, b):
-            w = WIDTHS[c]
-            per_bank = BANK // w
-            step = BANK if w == BANK else FP4_WIDTH
-            for k, number in enumerate(d_bank_ids[c, b]):
-                d_banks[c, b, k] = bank_tile(number, "d%d%d%d" % (c, b, k))
-                for a in range(PASSES):
+        def open_d(c, halves_of_d):
+            for b in halves_of_d:
+                slot = D_SLOTS[c][b]
+                for k in range(PACK // per_bank):
+                    d_banks[c, b, k] = psum.tile([P, BANK], F32, name="d%d%d%d" % (c, b, k), tag="bank%d%d" % (slot, k))
                     for t in range(k * per_bank, (k + 1) * per_bank):
-                        col = a * H + b * K_PASS + t * P
-                        for j in range(0, w, step):
-                            first = STARTS[c] + j
-                            nc.tensor.matmul_mx(
-                                out=d_view(c, b, t)[:, j : j + step],
-                                lhsT=wf_codes[:, 2 * col : 2 * (col + P)].bitcast(FP4X4),
-                                lhsT_scale=wf_planes[:, col : col + P],
-                                rhs=v_codes[a][:, first : first + step].bitcast(FP8X4),
-                                rhs_scale=v_planes[:, a * S + first : a * S + first + step],
-                                start=(a == 0 and t == k * per_bank and j == 0),
-                                stop=False,
-                            )
+                        x_pass(c, b, t, 0)
+                    for a in range(PASSES):
+                        for t in range(k * per_bank, (k + 1) * per_bank):
+                            col = a * H + b * K_PASS + t * P
+                            for j in range(0, CHUNK, FP4_WIDTH):
+                                first = c * CHUNK + j
+                                nc.tensor.matmul_mx(
+                                    out=d_view(c, b, t)[:, j : j + FP4_WIDTH],
+                                    lhsT=wf_codes[:, 2 * col : 2 * (col + P)].bitcast(FP4X4),
+                                    lhsT_scale=wf_planes[:, col : col + P],
+                                    rhs=v_codes[a, first // BANK][:, first % BANK : first % BANK + FP4_WIDTH].bitcast(FP8X4),
+                                    rhs_scale=v_planes[:, a * S + first : a * S + first + FP4_WIDTH],
+                                    start=False,
+                                    stop=False,
+                                )
 
-        def d_x(c, b, a):
-            for k in range(len(d_bank_ids[c, b])):
-                d_x_pass(c, b, k, a)
+        def close_d(c):
+            for b in range(PASSES):
+                for t in range(PACK):
+                    x_pass(c, b, t, 1)
 
         d_sbuf = {}
-        d_tags = {(0, 0): "wide1", (0, 1): "wide2", (1, 0): "wide0", (1, 1): "sum01", (2, 1): "wide1"}
 
         def evacuate_d(c, b):
-            d_sbuf[c, b] = work.tile(
-                [P, PACK * WIDTHS[c]], F32, name="d_sbuf%d%d" % (c, b), tag=d_tags[c, b], align_bytes=64
-            )
-            for k in range(len(d_bank_ids[c, b])):
+            d_sbuf[c, b] = d_ring[:, PASSES * (c % 2) + b, :]
+            for k in range(PACK // per_bank):
                 nc.scalar.copy(out=d_sbuf[c, b][:, k * BANK : (k + 1) * BANK], in_=d_banks[c, b, k][:])
 
         h_planes = {}
         h_mixed = {}
-        h_codes = {}
-        h_scales = {}
 
         def clamp(c, b):
-            w = WIDTHS[c]
-            tag = "h_planes%d" % b if c == 1 else "half%d" % b
-            h_planes[c, b] = work.tile([P, PACK, w], BF16, name="h_planes%d%d" % (c, b), tag=tag, align_bytes=64)
+            h_planes[c, b] = work.tile([P, PACK, CHUNK], BF16, name="h_planes%d%d" % (c, b), tag="h_planes%d%d" % (c % 2, b))
             for t in range(PACK):
-                src = d_sbuf[c, b][:, t * w : (t + 1) * w] if (c, b) in d_sbuf else d_view(c, b, t)
+                src = d_sbuf[c, b][:, t * CHUNK : (t + 1) * CHUNK] if (c, b) in d_sbuf else d_view(c, b, t)
                 nc.vector.tensor_scalar(
                     h_planes[c, b][:, t, :], src, lo_cols[:, b, t : t + 1], hi_cols[:, b, t : t + 1], MAX, MIN
                 )
 
         def mix_h(c, b, copy):
             h_mixed[c, b] = work.tile(
-                [P, PACK * WIDTHS[c]], BF16, name="h_mixed%d%d" % (c, b), tag="h_mixed%d%d" % (c % 2, b), align_bytes=64
+                [P, PACK * CHUNK], BF16, name="h_mixed%d%d" % (c, b), tag="h_mixed%d%d" % (c % 2, b), align_bytes=64
             )
             interleave(copy, h_mixed[c, b][:], h_planes[c, b][:])
 
         y_banks = {}
 
-        def quantize_h_and_multiply(c, b):
-            w = WIDTHS[c]
-            tag = "mixed2" if (c, b) == (1, 0) else "h_codes%d%d" % (c % 2, b)
-            codes = work.tile([P, w], U32, name="h_codes%d%d" % (c, b), tag=tag, align_bytes=64)
-            tag = "sum1" if (c, b) == (1, 1) else "h_scales%d%d" % (c % 2, b)
-            scales = work.tile([P, w], U8, name="h_scales%d%d" % (c, b), tag=tag, align_bytes=64)
-            nc.vector.quantize_mx(out=codes[:].bitcast(FP8X4), scales=scales[:], in_=h_mixed[c, b][:])
-            per_bank = BANK // w
+        def quantize_h_and_multiply(c, b, place=None):
+            if place is None:
+                place = work.tile(
+                    [P, CHUNK], U32, name="h_codes%d%d" % (c, b), tag="h_codes%d%d" % (c % 2, b), align_bytes=64
+                )
+            codes = place[:, 0:CHUNK]
+            scales = work.tile([P, CHUNK], U8, name="h_scales%d%d" % (c, b), tag="h_scales%d%d" % (c % 2, b), align_bytes=64)
+            nc.vector.quantize_mx(out=codes.bitcast(FP8X4), scales=scales[:], in_=h_mixed[c, b][:])
             for n in range(N_TILES):
                 k, u = divmod(n, per_bank)
                 if b == 0 and u == 0:
-                    y_banks[c, k] = bank_tile(y_bank_ids[c][k], "y%d%d" % (c, k))
+                    y_banks[c, k] = psum.tile([P, BANK], F32, name="y%d%d" % (c, k), tag="bank%d%d" % (Y_SLOTS[c], k))
                 cols = slice(n * P, (n + 1) * P)
                 nc.tensor.matmul_mx(
-                    out=y_banks[c, k][:, u * w : (u + 1) * w],
+                    out=y_banks[c, k][:, u * CHUNK : (u + 1) * CHUNK],
                     lhsT=wr_codes[:, b, cols].bitcast(FP8X4),
                     lhsT_scale=wr_planes[4 * b : P, cols],
-                    rhs=codes[:].bitcast(FP8X4),
+                    rhs=codes.bitcast(FP8X4),
                     rhs_scale=scales[:],
                     start=(b == 0 and u == 0),
                     stop=(b == PASSES - 1 and (u == per_bank - 1 or n == N_TILES - 1)),
                 )
 
-        def finish(c):
-            w = WIDTHS[c]
-            per_bank = BANK // w
-            result = work.tile([P, N_TILES, w], F32, name="result%d" % c, tag=("sum01", "h_mixed00", "sum00")[c], align_bytes=64)
-            for k in range(len(y_bank_ids[c])):
+        def finish(c, places):
+            cols = slice(c * CHUNK, (c + 1) * CHUNK)
+            for k in range(2):
                 tiles = slice(k * per_bank, min((k + 1) * per_bank, N_TILES))
                 count = tiles.stop - tiles.start
-                sums = y_banks[c, k][:, 0 : count * w].rearrange("p (n j) -> p n j", n=count)
-                nc.vector.tensor_tensor(result[:, tiles, :], sums, slope_cols[c][:, tiles, :], MULT)
-                rows = out[tiles.start * P : tiles.stop * P, STARTS[c] : STARTS[c] + w]
-                nc.sync.dma_start(out=rows.rearrange("(n p) j -> p n j", p=P), in_=result[:, tiles, :])
+                result = places[k][:, 0 : count * CHUNK].rearrange("p (n j) -> p n j", n=count)
+                sums = y_banks[c, k][:, 0 : count * CHUNK].rearrange("p (n j) -> p n j", n=count)
+                nc.vector.tensor_tensor(result, sums, slope_cols[:, tiles, cols], MULT)
+                rows = out[tiles.start * P : tiles.stop * P, cols]
+                nc.sync.dma_start(out=rows.rearrange("(n p) j -> p n j", p=P), in_=result)
 
-        def as_spare(mixed):
-            return mixed[:, 0 : 2 * BANK].bitcast(F32)
+        def flat(sums):
+            return sums[:].rearrange("p t j -> p (t j)")
 
-        gather_plane(0)
-        gather_plane(1)
+        def spare_tile(width, tag):
+            return work.tile([P, width], F32, name="spare_" + tag, tag=tag, align_bytes=64)[:]
+
+        def codes_tile(name, tag):
+            return work.tile([P, K_PASS], U32, name=name, tag=tag, align_bytes=64)[:]
+
+        gather_first(0, [tile[:] for tile in picked])
+        gather_first(1, [tile[:] for tile in picked])
         cast_wx(0, 0)
-        gather_plane(2)
-        quantize_wx(0, 0)
-        cast_wx(1, 0)
-        gather_plane(3)
-        quantize_wx(1, 0)
-        mix_x(0, 0, BANK)
-        mix_x(1, 0, NARROW)
-        reorder_wf()
-        gather_halves(4)
         cast_wx(0, 1)
-        gather_halves(5)
-        quantize_x(0, 0, BANK)
-        quantize_x(1, 0, NARROW)
-        for a in range(PASSES):
-            nc.vector.tensor_copy(v_codes[a][:], tab_codes[a][:].indirect(fuel_list[:]))
-        quantize_wx(0, 1)
+        slope_cols = work.tile([P, N_TILES, S], F32, name="slope_cols", tag="wide0")
+        nc.sync.dma_start(out=slope_cols[:], in_=slope.rearrange("(n p) j -> p n j", p=P))
+        gather_first(2, [tile[:] for tile in picked])
+        for b in range(PASSES):
+            quantize_wx(0, b, codes_tile("wx_codes0%d" % b, "picked%d" % b))
+        reorder_wf()
+        cast_wx(1, 0)
         cast_wx(1, 1)
+        gather_first(3, [spare_tile(BANK, "wx_bf00"), spare_tile(BANK, "wx_bf01")])
+        d_ring = work.tile([P, 2 * PASSES, PACK * CHUNK], F32, name="d_ring", tag="wide1")
+        mix_first(0)
+        mix_first(1)
+        late_codes = work.tile([P, PASSES, K_PASS], U32, name="late_codes", tag="wx_bf00", align_bytes=64)
         for b in range(PASSES):
-            d_fuel(0, b)
-            d_x(0, b, 0)
-        gather_halves(6)
-        gather_halves(7)
-        mix_x(0, 1, BANK)
-        gather_pair(1, 4, picked[:])
-        quantize_wx(1, 1)
-        quantize_x(0, 1, BANK)
-        for b in range(PASSES):
-            d_x(0, b, 1)
+            quantize_wx(1, b, late_codes[:, b, :])
+        gather_v(0, 0, "wx_bf01")
+        new_sums(0)
+        new_sums(1)
+        gather_plane(0, [spare_tile(CHUNK, "plane4a"), spare_tile(CHUNK, "plane4b")])
+        quantize_first(0, "plane4a")
+        spares = [spare_tile(CHUNK, "plane5a"), spare_tile(CHUNK, "plane4b")]
+        gather_plane(1, spares)
+        quantize_first(1, "plane5a")
+        spares = [spare_tile(CHUNK, "plane6a"), spares[1]]
+        gather_plane(2, spares)
+        gather_v(1, 0, "plane6a")
+        spares = [spare_tile(CHUNK, "plane7a"), spares[1]]
+        gather_plane(3, spares)
+        gather_v(0, 1, "plane7a")
+        gather_v(1, 1, "plane4b")
+        both = range(PASSES)
+
+        def as_floats(planes):
+            return flat(planes).bitcast(F32)
+
+        def fresh_places(c):
+            return [keep.tile([P, BANK // (k + 1)], F32, name="result%d%d" % (c, k))[:] for k in range(2)]
+
+        for c in range(2):
+            open_d(c, both)
+            mix_x(c)
+        quantize_x(0)
+        close_d(0)
+        new_sums(2)
+        gather_pair(2, 0, halves(flat(x_sums[0])))
+        quantize_x(1)
+        close_d(1)
+        for b in both:
             evacuate_d(0, b)
-            d_fuel(1, b)
-            d_x(1, b, 0)
-        gather_pair(1, 6, as_spare(x_mixed[0, 1]))
-        mix_x(1, 1, NARROW)
-        gather_pair(2, 0, as_spare(x_mixed[0, 1]))
-        clamp(0, 0)
-        mix_h(0, 0, nc.scalar.copy)
-        quantize_x(1, 1, NARROW)
-        clamp(0, 1)
-        mix_h(0, 1, nc.scalar.copy)
-        for b in range(PASSES):
-            d_x(1, b, 1)
+        open_d(2, both)
+        for b in both:
+            clamp(0, b)
+            mix_h(0, b, nc.scalar.copy)
+        for b in both:
             evacuate_d(1, b)
-            d_fuel(2, b)
-        gather_pair(2, 2, d_sbuf[0, 1][:, 2 * BANK : 3 * BANK])
-        mix_x(2, 0, NARROW)
-        quantize_h_and_multiply(0, 0)
-        gather_pair(2, 4, as_spare(h_mixed[0, 0][:]))
-        quantize_h_and_multiply(0, 1)
-        for b in range(PASSES):
+        gather_pair(2, 2, halves(d_sbuf[0, 1]))
+        mix_x(2)
+        for b in both:
+            quantize_h_and_multiply(0, b)
+        open_d(3, [0])
+        new_sums(3)
+        gather_pair(3, 0, halves(as_floats(h_planes[0, 1])))
+        for b in both:
             clamp(1, b)
+        quantize_x(2)
+        close_d(2)
+        finish(0, fresh_places(0))
+        for b in both:
             mix_h(1, b, nc.scalar.copy)
-        gather_pair(2, 6, d_sbuf[1, 1][:, NARROW : NARROW + BANK])
-        mix_x(2, 1, NARROW)
-        quantize_x(2, 0, NARROW)
-        for b in range(PASSES):
-            d_x(2, b, 0)
-        finish(0)
-        quantize_x(2, 1, NARROW)
-        for b in range(PASSES):
-            d_x(2, b, 1)
-        evacuate_d(2, 1)
-        clamp(2, 0)
-        mix_h(2, 0, nc.scalar.copy)
-        clamp(2, 1)
-        for b in range(PASSES):
+        for b in both:
+            evacuate_d(2, b)
+        open_d(3, [1])
+        gather_pair(3, 2, halves(flat(x_sums[2])))
+        mix_x(3)
+        for b in both:
             quantize_h_and_multiply(1, b)
-        mix_h(2, 1, nc.vector.tensor_copy)
-        quantize_h_and_multiply(2, 0)
-        quantize_h_and_multiply(2, 1)
-        finish(1)
-        finish(2)
+        for b in both:
+            clamp(2, b)
+        quantize_x(3)
+        close_d(3)
+        for b in both:
+            mix_h(2, b, nc.scalar.copy)
+        finish(1, [flat(x_sums[3])[:, 0:BANK], flat(x_sums[3])[:, BANK : 2 * BANK]])
+        clamp(3, 0)
+        mix_h(3, 0, nc.scalar.copy)
+        held = work.tile([P, PASSES * CHUNK], U32, name="held_codes", tag="xq%d" % CHUNKS, align_bytes=64)
+        quantize_h_and_multiply(2, 0, held[:, 0:CHUNK])
+        clamp(3, 1)
+        quantize_h_and_multiply(2, 1, held[:, CHUNK : 2 * CHUNK])
+        mix_h(3, 1, nc.vector.tensor_copy)
+        for b in both:
+            quantize_h_and_multiply(3, b)
+        finish(2, [as_floats(h_planes[3, 1]), as_floats(h_planes[3, 0])])
+        finish(3, fresh_places(3))

@@ -45,12 +45,12 @@ def tile_list_wildfire_spread_rates_kernel(
         upwind_list = keep.tile([P, S // LIST_ROWS], U16, name="upwind_list")
         downwind_list = keep.tile([P, S // LIST_ROWS], U16, name="downwind_list")
         x_planes = [keep.tile([P, T], F32, name="x_plane%d" % i) for i in range(PASSES * PACK)]
-        tab_codes = [work.tile([P, T], U32, name="tab_codes%d" % a, tag="tab%d" % a) for a in range(PASSES)]
+        tab_codes = [work.tile([P, T], U32, name="tab_codes%d" % a, tag="tab%d" % a, align_bytes=64) for a in range(PASSES)]
         tab_bytes = keep.tile([P, T], U8, name="tab_bytes")
         v_codes = {}
         v_rows = work.tile([P, S], U8, name="v_rows", tag="v_rows")
         v_planes = keep.tile([P, PASSES * S], U8, name="v_planes", align_bytes=64)
-        wf_raw = keep.tile([P, PASSES * H], U16, name="wf_raw")
+        wf_raw = keep.tile([P, PASSES * H * 2], U8, name="wf_raw")
         wf_raw_scales = keep.tile([P, H], U8, name="wf_raw_scales")
         wf_rows = work.tile([P, H], U8, name="wf_rows", tag="wf_rows")
         wf_planes = keep.tile([P, PASSES * H], U8, name="wf_planes", align_bytes=64)
@@ -58,8 +58,6 @@ def tile_list_wildfire_spread_rates_kernel(
         wr_planes = keep.tile([P, N], U8, name="wr_planes", align_bytes=64)
         lo_cols = keep.tile([P, PASSES, PACK], F32, name="lo_cols")
         hi_cols = keep.tile([P, PASSES, PACK], F32, name="hi_cols")
-        picked = [work.tile([P, BANK], F32, name="picked%d" % u, tag="picked%d" % u, align_bytes=64) for u in range(2)]
-        wf_codes = keep.tile([P, PASSES * H * 2], U8, name="wf_codes", align_bytes=64)
         wx_raw = [work.tile([P, PACK * H], F32, name="wx_raw%d" % a, tag="wide%d" % a) for a in range(PASSES)]
 
         for rows in (tab_bytes, wf_raw_scales):
@@ -107,7 +105,7 @@ def tile_list_wildfire_spread_rates_kernel(
         nc.sync.dma_start(upwind_list[:], offs2)
         nc.sync.dma_start(downwind_list[:], offs3)
         nc.vector.tensor_copy(v_rows[:], tab_bytes[:].indirect(fuel_list[:]))
-        nc.vector.tensor_copy(
+        nc.gpsimd.tensor_copy(
             out=wf_rows[:].rearrange("p (b t m) -> p b t m", t=PACK, m=P),
             in_=wf_raw_scales[:].rearrange("p (b m t) -> p b t m", t=PACK, m=P),
         )
@@ -117,18 +115,19 @@ def tile_list_wildfire_spread_rates_kernel(
         )
         load_x_plane(1)
         load_wx(0, 0)
-        load_wx(0, 1)
         load_x_plane(2)
-        load_wx(1, 0)
-        load_wx(1, 1)
+        load_wx(0, 1)
         load_x_plane(3)
         load_tab(0)
+        load_x_plane(4)
         spread_rows(wf_planes, wf_rows)
         spread_rows(v_planes, v_rows)
-        for i in range(PACK, 2 * PACK - 1):
-            load_x_plane(i)
+        load_x_plane(5)
+        load_wx(1, 0)
+        load_wx(1, 1)
+        load_x_plane(6)
         load_tab(1)
-        load_x_plane(2 * PACK - 1)
+        load_x_plane(7)
         nc.sync.dma_start(out=lo_cols[:], in_=lo.rearrange("(b p t) -> p b t", b=PASSES, t=PACK))
         nc.sync.dma_start(out=hi_cols[:], in_=hi.rearrange("(b p t) -> p b t", b=PASSES, t=PACK))
         nc.sync.dma_start(
@@ -141,7 +140,7 @@ def tile_list_wildfire_spread_rates_kernel(
         wx_grouped = {}
 
         def cast_wx(a, b):
-            grouped = work.tile([P, PACK * K_PASS], BF16, name="wx_bf%d%d" % (a, b), tag="wx_bf%d%d" % (a, b), align_bytes=64)
+            grouped = work.tile([P, PACK * K_PASS], BF16, name="wx_bf%d%d" % (a, b), tag=("wx_bf%d", "sums%d")[a] % b, align_bytes=64)
             src = wx_raw[a][:].rearrange("p (i c) -> p i c", i=PACK)[:, :, b * K_PASS : (b + 1) * K_PASS]
             nc.scalar.copy(
                 out=grouped[:].rearrange("p (t m i) -> p m t i", t=PACK, i=PACK),
@@ -156,10 +155,14 @@ def tile_list_wildfire_spread_rates_kernel(
                 out=codes.bitcast(FP8X4), scales=wx_scales[a, b][:], in_=wx_grouped[a, b][:]
             )
 
-        def reorder_wf():
-            nc.vector.tensor_copy(
-                out=wf_codes[:].bitcast(U16).rearrange("p (g t m) -> p g t m", t=PACK, m=P),
-                in_=wf_raw[:].rearrange("p (g m t) -> p g t m", t=PACK, m=P),
+        wf_codes = {}
+
+        def reorder_wf(a, b, tag):
+            wf_codes[a, b] = work.tile([P, 2 * K_PASS], U8, name="wf_codes%d%d" % (a, b), tag=tag, align_bytes=64)
+            col = a * H + b * K_PASS
+            nc.gpsimd.tensor_copy(
+                out=wf_codes[a, b][:].rearrange("p (t m e) -> p t m e", t=PACK, e=2),
+                in_=wf_raw[:, 2 * col : 2 * (col + K_PASS)].rearrange("p (m t e) -> p t m e", t=PACK, e=2),
             )
 
         def gather_x(pieces):
@@ -195,7 +198,7 @@ def tile_list_wildfire_spread_rates_kernel(
             )
 
         x_sums = {}
-        x_sum_tags = ("wx_bf10", "wx_bf11", "mixed0", "mixed1")
+        x_sum_tags = ("wx_bf0", "sums_of_1", "mixed0", "mixed1")
         x_mixed = {}
         x_codes = {}
         x_scales = [keep.tile([P, CHUNK], U8, name="x_scales%d" % c, align_bytes=64) for c in range(CHUNKS)]
@@ -212,10 +215,12 @@ def tile_list_wildfire_spread_rates_kernel(
         def halves(spare):
             return [spare[:, s * CHUNK : (s + 1) * CHUNK] for s in range(2)]
 
-        def gather_v(a, u, tag):
-            v_codes[a, u] = work.tile([P, BANK], U32, name="v_codes%d%d" % (a, u), tag=tag, align_bytes=64)
-            cols = slice(u * BANK // LIST_ROWS, (u + 1) * BANK // LIST_ROWS)
-            nc.vector.tensor_copy(v_codes[a, u][:], tab_codes[a][:].indirect(fuel_list[:, cols]))
+        def gather_v(a, first, width, tag):
+            picks = work.tile([P, width], U32, name="v_codes%d_%d" % (a, first), tag=tag, align_bytes=64)
+            cols = slice(first // LIST_ROWS, (first + width) // LIST_ROWS)
+            nc.vector.tensor_copy(picks[:], tab_codes[a][:].indirect(fuel_list[:, cols]))
+            for j in range(0, width, FP4_WIDTH):
+                v_codes[a, first + j] = picks[:, j : j + FP4_WIDTH]
 
         def mix_x(c):
             x_mixed[c] = work.tile(
@@ -264,9 +269,9 @@ def tile_list_wildfire_spread_rates_kernel(
                                 first = c * CHUNK + j
                                 nc.tensor.matmul_mx(
                                     out=d_view(c, b, t)[:, j : j + FP4_WIDTH],
-                                    lhsT=wf_codes[:, 2 * col : 2 * (col + P)].bitcast(FP4X4),
+                                    lhsT=wf_codes[a, b][:, 2 * t * P : 2 * (t + 1) * P].bitcast(FP4X4),
                                     lhsT_scale=wf_planes[:, col : col + P],
-                                    rhs=v_codes[a, first // BANK][:, first % BANK : first % BANK + FP4_WIDTH].bitcast(FP8X4),
+                                    rhs=v_codes[a, first].bitcast(FP8X4),
                                     rhs_scale=v_planes[:, a * S + first : a * S + first + FP4_WIDTH],
                                     start=False,
                                     stop=False,
@@ -346,47 +351,46 @@ def tile_list_wildfire_spread_rates_kernel(
         def codes_tile(name, tag):
             return work.tile([P, K_PASS], U32, name=name, tag=tag, align_bytes=64)[:]
 
-        gather_first(0, [tile[:] for tile in picked])
-        gather_first(1, [tile[:] for tile in picked])
+        picked = spare_tile(BANK, "plane0a")
+        for t in range(3):
+            gather_first(t, [picked, spare_tile(BANK, "plane%db" % t)])
+            reorder_wf(t // 2, t % 2, "plane%db" % t)
         cast_wx(0, 0)
         cast_wx(0, 1)
         slope_cols = work.tile([P, N_TILES, S], F32, name="slope_cols", tag="wide0")
         nc.sync.dma_start(out=slope_cols[:], in_=slope.rearrange("(n p) j -> p n j", p=P))
-        gather_first(2, [tile[:] for tile in picked])
-        for b in range(PASSES):
-            quantize_wx(0, b, codes_tile("wx_codes0%d" % b, "picked%d" % b))
-        reorder_wf()
-        cast_wx(1, 0)
-        cast_wx(1, 1)
-        gather_first(3, [spare_tile(BANK, "wx_bf00"), spare_tile(BANK, "wx_bf01")])
-        d_ring = work.tile([P, 2 * PASSES, PACK * CHUNK], F32, name="d_ring", tag="wide1")
+        gather_first(3, [spare_tile(BANK, "plane3a"), spare_tile(BANK, "plane3b")])
         mix_first(0)
         mix_first(1)
-        late_codes = work.tile([P, PASSES, K_PASS], U32, name="late_codes", tag="wx_bf00", align_bytes=64)
+        early_codes = work.tile([P, PASSES, K_PASS], U32, name="early_codes", tag="plane3a", align_bytes=64)
         for b in range(PASSES):
-            quantize_wx(1, b, late_codes[:, b, :])
-        gather_v(0, 0, "wx_bf01")
+            quantize_wx(0, b, early_codes[:, b, :])
+        reorder_wf(1, 1, "wx_bf1")
+        gather_v(0, 0, S, "plane3b")
         new_sums(0)
         new_sums(1)
-        gather_plane(0, [spare_tile(CHUNK, "plane4a"), spare_tile(CHUNK, "plane4b")])
+        spares = [spare_tile(CHUNK, "plane4a"), spare_tile(CHUNK, "plane4b")]
+        gather_plane(0, spares)
         quantize_first(0, "plane4a")
-        spares = [spare_tile(CHUNK, "plane5a"), spare_tile(CHUNK, "plane4b")]
-        gather_plane(1, spares)
+        gather_plane(1, [spare_tile(CHUNK, "plane5a"), spares[1]])
         quantize_first(1, "plane5a")
-        spares = [spare_tile(CHUNK, "plane6a"), spares[1]]
-        gather_plane(2, spares)
-        gather_v(1, 0, "plane6a")
-        spares = [spare_tile(CHUNK, "plane7a"), spares[1]]
-        gather_plane(3, spares)
-        gather_v(0, 1, "plane7a")
-        gather_v(1, 1, "plane4b")
+        cast_wx(1, 0)
+        cast_wx(1, 1)
+        d_ring = work.tile([P, 2 * PASSES, PACK * CHUNK], F32, name="d_ring", tag="wide1")
+        gather_plane(2, [spare_tile(CHUNK, "plane6a"), spare_tile(CHUNK, "plane4b")])
+        quantize_wx(1, 0, codes_tile("wx_codes10", "plane6a"))
+        gather_v(1, 0, BANK, "plane4b")
+        gather_plane(3, [spare_tile(CHUNK, "plane7a"), spare_tile(CHUNK, "plane7b")])
+        quantize_wx(1, 1, codes_tile("wx_codes11", "plane7a"))
+        gather_v(1, BANK, BANK, "plane7b")
         both = range(PASSES)
 
         def as_floats(planes):
             return flat(planes).bitcast(F32)
 
-        def fresh_places(c):
-            return [keep.tile([P, BANK // (k + 1)], F32, name="result%d%d" % (c, k))[:] for k in range(2)]
+        def fresh_places(c, tag):
+            place = work.tile([P, 2 * BANK], F32, name="result%d" % c, tag=tag, align_bytes=64)
+            return [place[:, k * BANK : (k + 1) * BANK] for k in range(2)]
 
         for c in range(2):
             open_d(c, both)
@@ -416,7 +420,7 @@ def tile_list_wildfire_spread_rates_kernel(
             clamp(1, b)
         quantize_x(2)
         close_d(2)
-        finish(0, fresh_places(0))
+        finish(0, fresh_places(0, "tab0"))
         for b in both:
             mix_h(1, b, nc.scalar.copy)
         for b in both:
@@ -443,4 +447,4 @@ def tile_list_wildfire_spread_rates_kernel(
         for b in both:
             quantize_h_and_multiply(3, b)
         finish(2, [as_floats(h_planes[3, 1]), as_floats(h_planes[3, 0])])
-        finish(3, fresh_places(3))
+        finish(3, fresh_places(3, "sums0"))

@@ -23,13 +23,14 @@ PACK = 4
 K_PASS = P * PACK
 PASSES = K // K_PASS
 BANK = 512
-CHUNK = 256
-CHUNKS = S // CHUNK
+NARROW = 256
+WIDTHS = (BANK, NARROW, NARROW)
+STARTS = (0, BANK, BANK + NARROW)
 LIST_ROWS = 16
 FP4_WIDTH = 128
 N_TILES = N // P
-D_SLOTS = ((0, 1), (2, 3), (0, 1), (2, 0))
-Y_SLOTS = (3, 3, 1, 3)
+D_BANKS = {(0, 0): (0, 1, 2, 3), (0, 1): (4, 5, 6, 7), (1, 0): (0, 1), (1, 1): (2, 3), (2, 0): (4, 5), (2, 1): (6, 7)}
+Y_BANKS = ((0, 1, 2), (3, 4), (5, 6))
 
 
 def tile_list_wildfire_spread_rates_kernel(
@@ -165,117 +166,113 @@ def tile_list_wildfire_spread_rates_kernel(
                 in_=wf_raw[:, 2 * col : 2 * (col + K_PASS)].rearrange("p (m t e) -> p t m e", t=PACK, e=2),
             )
 
-        def gather_x(pieces):
-            jobs = []
-            for i, j, width, upwind, total in pieces:
-                jobs.append((x_planes[i], slice(j // LIST_ROWS, (j + width) // LIST_ROWS), upwind, total))
-            for plane, cols, upwind, total in jobs:
-                nc.vector.tensor_copy(upwind, plane[:].indirect(upwind_list[:, cols]))
-            for plane, cols, upwind, total in jobs:
-                nc.vector.tensor_tensor(total, plane[:].indirect(downwind_list[:, cols]), upwind, ADD)
+        def list_cols(first, width):
+            return slice(first // LIST_ROWS, (first + width) // LIST_ROWS)
+
+        def pick_upwind(i, first, upwind):
+            cols = list_cols(first, upwind.shape[1])
+            nc.vector.tensor_copy(upwind, x_planes[i][:].indirect(upwind_list[:, cols]))
+
+        def add_downwind(i, first, upwind, total):
+            cols = list_cols(first, upwind.shape[1])
+            nc.vector.tensor_tensor(total, x_planes[i][:].indirect(downwind_list[:, cols]), upwind, ADD)
+
+        def gather_halves(i, spares, sums):
+            width = spares[0].shape[1]
+            for u in range(2):
+                pick_upwind(i, u * width, spares[u])
+            for u in range(2):
+                add_downwind(i, u * width, spares[u], sums[u])
 
         def interleave(copy, dst, src):
-            copy(out=dst.rearrange("p (j t) -> p j t", t=PACK), in_=src.rearrange("p t j -> p j t"))
+            copy(
+                out=dst.rearrange("p (c i t) -> p c t i", i=PACK, t=PACK), in_=src.rearrange("p t (c i) -> p c t i", i=PACK)
+            )
 
         first_sums = [work.tile([P, PACK, BANK], F32, name="first_sums%d" % u, tag="sums%d" % u, align_bytes=64) for u in range(2)]
         first_mixed = [
             work.tile([P, PACK * BANK], BF16, name="first_mixed%d" % u, tag="mixed%d" % u, align_bytes=64) for u in range(2)
         ]
-        first_codes = {}
-        first_scales = keep.tile([P, S], U8, name="first_scales", align_bytes=64)
+        x_codes = {}
+        x_scales = {}
 
         def gather_first(t, spares):
-            gather_x([(t, u * BANK, BANK, spares[u], first_sums[u][:, t, :]) for u in range(2)])
+            gather_halves(t, spares, [first_sums[u][:, t, :] for u in range(2)])
 
-        def mix_first(u):
-            interleave(nc.scalar.copy, first_mixed[u][:], first_sums[u][:])
+        def quantize_first(c, codes):
+            u, first = divmod(STARTS[c], BANK)
+            x_codes[c, 0] = codes
+            x_scales[c, 0] = keep.tile([P, WIDTHS[c]], U8, name="first_scales%d" % c, align_bytes=64)[:]
+            values = first_mixed[u][:, PACK * first : PACK * (first + WIDTHS[c])]
+            nc.vector.quantize_mx(out=codes.bitcast(FP8X4), scales=x_scales[c, 0], in_=values)
 
-        def quantize_first(u, tag):
-            first_codes[u] = work.tile([P, BANK], U32, name="first_codes%d" % u, tag=tag, align_bytes=64)
-            cols = slice(u * BANK, (u + 1) * BANK)
-            nc.vector.quantize_mx(
-                out=first_codes[u][:].bitcast(FP8X4), scales=first_scales[:, cols], in_=first_mixed[u][:]
-            )
+        def gather_v(a, first, picks):
+            width = picks.shape[1]
+            nc.vector.tensor_copy(picks, tab_codes[a][:].indirect(fuel_list[:, list_cols(first, width)]))
+            for j in range(0, width, BANK):
+                v_codes[a, (first + j) // BANK] = picks[:, j : j + BANK]
 
-        x_sums = {}
-        x_sum_tags = ("wx_bf0", "sums_of_1", "mixed0", "mixed1")
         x_mixed = {}
-        x_codes = {}
-        x_scales = [keep.tile([P, CHUNK], U8, name="x_scales%d" % c, align_bytes=64) for c in range(CHUNKS)]
 
-        def gather_plane(t, spares):
-            gather_x([(PACK + t, c * CHUNK, CHUNK, spares[c], x_sums[c][:, t, :]) for c in range(2)])
+        def interleave_shared(copies, dst, src):
+            w = src.shape[2] // len(copies)
+            for u, copy in enumerate(copies):
+                interleave(copy, dst[:, PACK * u * w : PACK * (u + 1) * w], src[:, :, u * w : (u + 1) * w])
 
-        def new_sums(c):
-            x_sums[c] = work.tile([P, PACK, CHUNK], F32, name="x_sums%d" % c, tag=x_sum_tags[c], align_bytes=64)
-
-        def gather_pair(c, t, spares):
-            gather_x([(PACK + t + s, c * CHUNK, CHUNK, spares[s], x_sums[c][:, t + s, :]) for s in range(2)])
-
-        def halves(spare):
-            return [spare[:, s * CHUNK : (s + 1) * CHUNK] for s in range(2)]
-
-        def gather_v(a, first, width, tag):
-            picks = work.tile([P, width], U32, name="v_codes%d_%d" % (a, first), tag=tag, align_bytes=64)
-            cols = slice(first // LIST_ROWS, (first + width) // LIST_ROWS)
-            nc.vector.tensor_copy(picks[:], tab_codes[a][:].indirect(fuel_list[:, cols]))
-            for j in range(0, width, FP4_WIDTH):
-                v_codes[a, first + j] = picks[:, j : j + FP4_WIDTH]
-
-        def mix_x(c):
-            x_mixed[c] = work.tile(
-                [P, PACK * CHUNK], BF16, name="x_mixed%d" % c, tag=("xm0", "xm1", "xq2", "xq3")[c], align_bytes=64
-            )
-            interleave(nc.scalar.copy, x_mixed[c][:], x_sums[c][:])
+        def mix_x(c, sums, copies, tag):
+            x_mixed[c] = work.tile([P, PACK * WIDTHS[c]], BF16, name="x_mixed%d" % c, tag=tag, align_bytes=64)
+            interleave_shared(copies, x_mixed[c][:], sums)
 
         def quantize_x(c):
-            x_codes[c] = work.tile([P, CHUNK], U32, name="x_codes%d" % c, tag="xq%d" % (c + 1), align_bytes=64)
-            nc.vector.quantize_mx(out=x_codes[c][:].bitcast(FP8X4), scales=x_scales[c][:], in_=x_mixed[c][:])
+            x_codes[c, 1] = work.tile([P, WIDTHS[c]], U32, name="x_codes%d" % c, tag="x_codes%d" % c, align_bytes=64)[:]
+            x_scales[c, 1] = keep.tile([P, WIDTHS[c]], U8, name="x_scales%d" % c, align_bytes=64)[:]
+            nc.vector.quantize_mx(out=x_codes[c, 1].bitcast(FP8X4), scales=x_scales[c, 1], in_=x_mixed[c][:])
 
         d_banks = {}
-        per_bank = BANK // CHUNK
 
         def d_view(c, b, t):
-            k, u = divmod(t, per_bank)
-            return d_banks[c, b, k][:, u * CHUNK : (u + 1) * CHUNK]
+            w = WIDTHS[c]
+            k, u = divmod(t, BANK // w)
+            return d_banks[c, b, k][:, u * w : (u + 1) * w]
 
         def x_pass(c, b, t, a):
+            per_bank = BANK // WIDTHS[c]
             cols = slice(t * P, (t + 1) * P)
-            if a == 0:
-                codes, scales = first_codes[c // 2][:, c % 2 * CHUNK : (c % 2 + 1) * CHUNK], first_scales[:, c * CHUNK : (c + 1) * CHUNK]
-            else:
-                codes, scales = x_codes[c][:], x_scales[c][:]
             nc.tensor.matmul_mx(
                 out=d_view(c, b, t),
                 lhsT=wx_codes[a, b][:, cols].bitcast(FP8X4),
                 lhsT_scale=wx_scales[a, b][:, cols],
-                rhs=codes.bitcast(FP8X4),
-                rhs_scale=scales,
+                rhs=x_codes[c, a].bitcast(FP8X4),
+                rhs_scale=x_scales[c, a],
                 start=(a == 0 and t % per_bank == 0),
                 stop=(a == PASSES - 1 and t % per_bank == per_bank - 1),
             )
 
-        def open_d(c, halves_of_d):
-            for b in halves_of_d:
-                slot = D_SLOTS[c][b]
-                for k in range(PACK // per_bank):
-                    d_banks[c, b, k] = psum.tile([P, BANK], F32, name="d%d%d%d" % (c, b, k), tag="bank%d%d" % (slot, k))
-                    for t in range(k * per_bank, (k + 1) * per_bank):
-                        x_pass(c, b, t, 0)
-                    for a in range(PASSES):
-                        for t in range(k * per_bank, (k + 1) * per_bank):
-                            col = a * H + b * K_PASS + t * P
-                            for j in range(0, CHUNK, FP4_WIDTH):
-                                first = c * CHUNK + j
-                                nc.tensor.matmul_mx(
-                                    out=d_view(c, b, t)[:, j : j + FP4_WIDTH],
-                                    lhsT=wf_codes[a, b][:, 2 * t * P : 2 * (t + 1) * P].bitcast(FP4X4),
-                                    lhsT_scale=wf_planes[:, col : col + P],
-                                    rhs=v_codes[a, first].bitcast(FP8X4),
-                                    rhs_scale=v_planes[:, a * S + first : a * S + first + FP4_WIDTH],
-                                    start=False,
-                                    stop=False,
-                                )
+        def fuel_pass(c, b, t, a):
+            step = BANK if WIDTHS[c] == BANK else FP4_WIDTH
+            col = a * H + b * K_PASS + t * P
+            for j in range(0, WIDTHS[c], step):
+                first = STARTS[c] + j
+                nc.tensor.matmul_mx(
+                    out=d_view(c, b, t)[:, j : j + step],
+                    lhsT=wf_codes[a, b][:, 2 * t * P : 2 * (t + 1) * P].bitcast(FP4X4),
+                    lhsT_scale=wf_planes[:, col : col + P],
+                    rhs=v_codes[a, first // BANK][:, first % BANK : first % BANK + step].bitcast(FP8X4),
+                    rhs_scale=v_planes[:, a * S + first : a * S + first + step],
+                    start=False,
+                    stop=False,
+                )
+
+        def open_d(c, b):
+            per_bank = BANK // WIDTHS[c]
+            for k, number in enumerate(D_BANKS[c, b]):
+                d_banks[c, b, k] = psum.tile([P, BANK], F32, name="d%d%d%d" % (c, b, k), tag="bank%d" % number)
+                tiles = range(k * per_bank, (k + 1) * per_bank)
+                for t in tiles:
+                    x_pass(c, b, t, 0)
+                for a in range(PASSES):
+                    for t in tiles:
+                        fuel_pass(c, b, t, a)
 
         def close_d(c):
             for b in range(PASSES):
@@ -284,45 +281,52 @@ def tile_list_wildfire_spread_rates_kernel(
 
         d_sbuf = {}
 
-        def evacuate_d(c, b):
-            d_sbuf[c, b] = d_ring[:, PASSES * (c % 2) + b, :]
-            for k in range(PACK // per_bank):
-                nc.scalar.copy(out=d_sbuf[c, b][:, k * BANK : (k + 1) * BANK], in_=d_banks[c, b, k][:])
+        def evacuate_d(c, b, place):
+            d_sbuf[c, b] = place
+            for k in range(len(D_BANKS[c, b])):
+                nc.scalar.copy(out=place[:, k * BANK : (k + 1) * BANK], in_=d_banks[c, b, k][:])
+
+        def gpsimd_copy(out, in_):
+            nc.gpsimd.tensor_scalar(out, in_, 1.0, 0.0, MULT, ADD)
 
         h_planes = {}
         h_mixed = {}
 
-        def clamp(c, b):
-            h_planes[c, b] = work.tile([P, PACK, CHUNK], BF16, name="h_planes%d%d" % (c, b), tag="h_planes%d%d" % (c % 2, b))
+        def clamp(c, b, engines, tag):
+            w = WIDTHS[c]
+            h_planes[c, b] = work.tile([P, PACK, w], BF16, name="h_planes%d%d" % (c, b), tag=tag, align_bytes=64)
             for t in range(PACK):
-                src = d_sbuf[c, b][:, t * CHUNK : (t + 1) * CHUNK] if (c, b) in d_sbuf else d_view(c, b, t)
-                nc.vector.tensor_scalar(
-                    h_planes[c, b][:, t, :], src, lo_cols[:, b, t : t + 1], hi_cols[:, b, t : t + 1], MAX, MIN
+                src = d_sbuf[c, b][:, t * w : (t + 1) * w] if (c, b) in d_sbuf else d_view(c, b, t)
+                engines[t].tensor_scalar(
+                    h_planes[c, b][:, t, :], src, hi_cols[:, b, t : t + 1], lo_cols[:, b, t : t + 1], MIN, MAX
                 )
 
-        def mix_h(c, b, copy):
+        def mix_h(c, b, copies, tag):
             h_mixed[c, b] = work.tile(
-                [P, PACK * CHUNK], BF16, name="h_mixed%d%d" % (c, b), tag="h_mixed%d%d" % (c % 2, b), align_bytes=64
+                [P, PACK * WIDTHS[c]], BF16, name="h_mixed%d%d" % (c, b), tag=tag, align_bytes=64
             )
-            interleave(copy, h_mixed[c, b][:], h_planes[c, b][:])
+            interleave_shared(copies, h_mixed[c, b][:], h_planes[c, b][:])
 
         y_banks = {}
 
-        def quantize_h_and_multiply(c, b, place=None):
-            if place is None:
-                place = work.tile(
-                    [P, CHUNK], U32, name="h_codes%d%d" % (c, b), tag="h_codes%d%d" % (c % 2, b), align_bytes=64
-                )
-            codes = place[:, 0:CHUNK]
-            scales = work.tile([P, CHUNK], U8, name="h_scales%d%d" % (c, b), tag="h_scales%d%d" % (c % 2, b), align_bytes=64)
+        def quantize_h(c, b, codes):
+            scales = keep.tile([P, WIDTHS[c]], U8, name="h_scales%d%d" % (c, b), align_bytes=64)
             nc.vector.quantize_mx(out=codes.bitcast(FP8X4), scales=scales[:], in_=h_mixed[c, b][:])
+            return scales
+
+        def quantize_h_and_multiply(c, b, codes):
+            multiply_h(c, b, codes, quantize_h(c, b, codes))
+
+        def multiply_h(c, b, codes, scales):
+            w = WIDTHS[c]
+            per_bank = BANK // w
             for n in range(N_TILES):
                 k, u = divmod(n, per_bank)
                 if b == 0 and u == 0:
-                    y_banks[c, k] = psum.tile([P, BANK], F32, name="y%d%d" % (c, k), tag="bank%d%d" % (Y_SLOTS[c], k))
+                    y_banks[c, k] = psum.tile([P, BANK], F32, name="y%d%d" % (c, k), tag="bank%d" % Y_BANKS[c][k])
                 cols = slice(n * P, (n + 1) * P)
                 nc.tensor.matmul_mx(
-                    out=y_banks[c, k][:, u * CHUNK : (u + 1) * CHUNK],
+                    out=y_banks[c, k][:, u * w : (u + 1) * w],
                     lhsT=wr_codes[:, b, cols].bitcast(FP8X4),
                     lhsT_scale=wr_planes[4 * b : P, cols],
                     rhs=codes.bitcast(FP8X4),
@@ -332,119 +336,116 @@ def tile_list_wildfire_spread_rates_kernel(
                 )
 
         def finish(c, places):
-            cols = slice(c * CHUNK, (c + 1) * CHUNK)
-            for k in range(2):
+            w = WIDTHS[c]
+            per_bank = BANK // w
+            cols = slice(STARTS[c], STARTS[c] + w)
+            for k in range(len(Y_BANKS[c])):
                 tiles = slice(k * per_bank, min((k + 1) * per_bank, N_TILES))
                 count = tiles.stop - tiles.start
-                result = places[k][:, 0 : count * CHUNK].rearrange("p (n j) -> p n j", n=count)
-                sums = y_banks[c, k][:, 0 : count * CHUNK].rearrange("p (n j) -> p n j", n=count)
+                result = places[k][:, 0 : count * w].rearrange("p (n j) -> p n j", n=count)
+                sums = y_banks[c, k][:, 0 : count * w].rearrange("p (n j) -> p n j", n=count)
                 nc.vector.tensor_tensor(result, sums, slope_cols[:, tiles, cols], MULT)
                 rows = out[tiles.start * P : tiles.stop * P, cols]
                 nc.sync.dma_start(out=rows.rearrange("(n p) j -> p n j", p=P), in_=result)
 
-        def flat(sums):
-            return sums[:].rearrange("p t j -> p (t j)")
+        def floats(width, tag):
+            return work.tile([P, width], F32, name="floats_" + tag, tag=tag, align_bytes=64)[:]
 
-        def spare_tile(width, tag):
-            return work.tile([P, width], F32, name="spare_" + tag, tag=tag, align_bytes=64)[:]
+        def words(width, tag):
+            return work.tile([P, width], U32, name="words_" + tag, tag=tag, align_bytes=64)[:]
 
-        def codes_tile(name, tag):
-            return work.tile([P, K_PASS], U32, name=name, tag=tag, align_bytes=64)[:]
+        def parts(place, width):
+            return [place[:, j : j + width] for j in range(0, place.shape[1], width)]
 
-        picked = spare_tile(BANK, "plane0a")
+        def as_floats(planes):
+            return planes[:].rearrange("p t j -> p (t j)").bitcast(F32)
+
+        both = range(PASSES)
+        vector, gpsimd, scalar = nc.vector, nc.gpsimd, nc.scalar
+        picked = floats(BANK, "plane0a")
         for t in range(3):
-            gather_first(t, [picked, spare_tile(BANK, "plane%db" % t)])
+            gather_first(t, [picked, floats(BANK, "plane%db" % t)])
             reorder_wf(t // 2, t % 2, "plane%db" % t)
         cast_wx(0, 0)
         cast_wx(0, 1)
         slope_cols = work.tile([P, N_TILES, S], F32, name="slope_cols", tag="wide0")
         nc.sync.dma_start(out=slope_cols[:], in_=slope.rearrange("(n p) j -> p n j", p=P))
-        gather_first(3, [spare_tile(BANK, "plane3a"), spare_tile(BANK, "plane3b")])
-        mix_first(0)
-        mix_first(1)
-        early_codes = work.tile([P, PASSES, K_PASS], U32, name="early_codes", tag="plane3a", align_bytes=64)
-        for b in range(PASSES):
-            quantize_wx(0, b, early_codes[:, b, :])
+        gather_first(3, [floats(BANK, "plane3a"), floats(BANK, "plane3b")])
+        for u in range(2):
+            interleave(scalar.copy, first_mixed[u][:], first_sums[u][:])
+        for b, codes in enumerate(parts(words(2 * K_PASS, "plane3a"), K_PASS)):
+            quantize_wx(0, b, codes)
         reorder_wf(1, 1, "wx_bf1")
-        gather_v(0, 0, S, "plane3b")
-        new_sums(0)
-        new_sums(1)
-        spares = [spare_tile(CHUNK, "plane4a"), spare_tile(CHUNK, "plane4b")]
-        gather_plane(0, spares)
-        quantize_first(0, "plane4a")
-        gather_plane(1, [spare_tile(CHUNK, "plane5a"), spares[1]])
-        quantize_first(1, "plane5a")
+        gather_v(0, 0, words(S, "plane3b"))
+
+        wide_sums = work.tile([P, PACK, BANK], F32, name="wide_sums", tag="wide_sums", align_bytes=64)
+        chain = floats(NARROW, "chain")
+        gather_halves(4, [floats(NARROW, "plane4a"), chain], parts(wide_sums[:, 0, :], NARROW))
+        quantize_first(0, words(BANK, "plane4a"))
+        gather_halves(5, [floats(NARROW, "plane5a"), chain], parts(wide_sums[:, 1, :], NARROW))
+        quantize_first(1, words(NARROW, "plane5a"))
         cast_wx(1, 0)
         cast_wx(1, 1)
-        d_ring = work.tile([P, 2 * PASSES, PACK * CHUNK], F32, name="d_ring", tag="wide1")
-        gather_plane(2, [spare_tile(CHUNK, "plane6a"), spare_tile(CHUNK, "plane4b")])
-        quantize_wx(1, 0, codes_tile("wx_codes10", "plane6a"))
-        gather_v(1, 0, BANK, "plane4b")
-        gather_plane(3, [spare_tile(CHUNK, "plane7a"), spare_tile(CHUNK, "plane7b")])
-        quantize_wx(1, 1, codes_tile("wx_codes11", "plane7a"))
-        gather_v(1, BANK, BANK, "plane7b")
-        both = range(PASSES)
-
-        def as_floats(planes):
-            return flat(planes).bitcast(F32)
-
-        def fresh_places(c, tag):
-            place = work.tile([P, 2 * BANK], F32, name="result%d" % c, tag=tag, align_bytes=64)
-            return [place[:, k * BANK : (k + 1) * BANK] for k in range(2)]
-
-        for c in range(2):
-            open_d(c, both)
-            mix_x(c)
+        d_wide = work.tile([P, PASSES, PACK * BANK], F32, name="d_wide", tag="wide1")
+        gather_halves(6, [floats(NARROW, "plane6a"), chain], parts(wide_sums[:, 2, :], NARROW))
+        quantize_wx(1, 0, words(K_PASS, "plane6a"))
+        gather_v(1, 0, words(BANK, "chain"))
+        gather_halves(7, [floats(NARROW, "plane7a"), floats(NARROW, "plane7b")], parts(wide_sums[:, 3, :], NARROW))
+        quantize_wx(1, 1, words(K_PASS, "plane7a"))
+        for b in both:
+            open_d(0, b)
+        mix_x(0, wide_sums[:], [scalar.copy], "x_mixed0")
+        waiting = parts(floats(PACK * NARROW, "plane7b"), NARROW)
+        for t in range(PACK):
+            pick_upwind(PACK + t, STARTS[1], waiting[t])
         quantize_x(0)
         close_d(0)
-        new_sums(2)
-        gather_pair(2, 0, halves(flat(x_sums[0])))
+        narrow_sums = wide_sums[:, :, 0:NARROW]
+        for t in range(PACK):
+            add_downwind(PACK + t, STARTS[1], waiting[t], narrow_sums[:, t, :])
+        gather_v(1, BANK, words(BANK, "x_mixed0"))
+        waiting = [wide_sums[:, t, NARROW:BANK] for t in range(PACK)]
+        for t in range(PACK):
+            pick_upwind(PACK + t, STARTS[2], waiting[t])
+        for b in both:
+            evacuate_d(0, b, d_wide[:, b, :])
+        for b in both:
+            open_d(1, b)
+        mix_x(1, narrow_sums, [scalar.copy], "x_codes0")
+        clamp(0, 0, [gpsimd] * PACK, "plane7b")
+        mix_h(0, 0, [scalar.copy], "sums0")
+        clamp(0, 1, [vector] * PACK, "wx_bf0")
         quantize_x(1)
         close_d(1)
+        quantize_first(2, words(NARROW, "x_codes0"))
         for b in both:
-            evacuate_d(0, b)
-        open_d(2, both)
-        for b in both:
-            clamp(0, b)
-            mix_h(0, b, nc.scalar.copy)
-        for b in both:
-            evacuate_d(1, b)
-        gather_pair(2, 2, halves(d_sbuf[0, 1]))
-        mix_x(2)
-        for b in both:
-            quantize_h_and_multiply(0, b)
-        open_d(3, [0])
-        new_sums(3)
-        gather_pair(3, 0, halves(as_floats(h_planes[0, 1])))
-        for b in both:
-            clamp(1, b)
+            open_d(2, b)
+        for t in range(PACK):
+            add_downwind(PACK + t, STARTS[2], waiting[t], narrow_sums[:, t, :])
+        evacuate_d(1, 0, floats(PACK * NARROW, "plane7b"))
+        evacuate_d(1, 1, d_wide[:, 0, 0 : PACK * NARROW])
+        mix_x(2, narrow_sums, [scalar.copy], "x_codes1")
+        wide_codes = words(BANK, "tab0")
+        wide_scales = quantize_h(0, 0, wide_codes)
+        mix_h(0, 1, [scalar.copy], "wide_sums")
+        clamp(1, 0, [vector] * PACK, "h_planes10")
+        mix_h(1, 0, [scalar.copy], "h_mixed10")
+        clamp(1, 1, [vector] * PACK, "h_planes11")
+        mix_h(1, 1, [gpsimd_copy], "h_mixed11")
         quantize_x(2)
         close_d(2)
-        finish(0, fresh_places(0, "tab0"))
-        for b in both:
-            mix_h(1, b, nc.scalar.copy)
-        for b in both:
-            evacuate_d(2, b)
-        open_d(3, [1])
-        gather_pair(3, 2, halves(flat(x_sums[2])))
-        mix_x(3)
-        for b in both:
-            quantize_h_and_multiply(1, b)
-        for b in both:
-            clamp(2, b)
-        quantize_x(3)
-        close_d(3)
-        for b in both:
-            mix_h(2, b, nc.scalar.copy)
-        finish(1, [flat(x_sums[3])[:, 0:BANK], flat(x_sums[3])[:, BANK : 2 * BANK]])
-        clamp(3, 0)
-        mix_h(3, 0, nc.scalar.copy)
-        held = work.tile([P, PASSES * CHUNK], U32, name="held_codes", tag="xq%d" % CHUNKS, align_bytes=64)
-        quantize_h_and_multiply(2, 0, held[:, 0:CHUNK])
-        clamp(3, 1)
-        quantize_h_and_multiply(2, 1, held[:, CHUNK : 2 * CHUNK])
-        mix_h(3, 1, nc.vector.tensor_copy)
-        for b in both:
-            quantize_h_and_multiply(3, b)
-        finish(2, [as_floats(h_planes[3, 1]), as_floats(h_planes[3, 0])])
-        finish(3, fresh_places(3, "sums0"))
+        multiply_h(0, 0, wide_codes, wide_scales)
+        clamp(2, 0, [vector] * PACK, "h_planes20")
+        mix_h(2, 0, [scalar.copy], "h_mixed20")
+        clamp(2, 1, [vector] * PACK, "h_planes21")
+        mix_h(2, 1, [scalar.copy], "h_mixed21")
+        late_codes = words(BANK + 4 * NARROW, "x_codes2")
+        quantize_h_and_multiply(0, 1, late_codes[:, 0:BANK])
+        h_codes = parts(late_codes[:, BANK : BANK + 4 * NARROW], NARROW)
+        quantize_h_and_multiply(1, 0, h_codes[0])
+        quantize_h_and_multiply(1, 1, h_codes[1])
+        quantize_h_and_multiply(2, 0, h_codes[2])
+        quantize_h_and_multiply(2, 1, h_codes[3])
+        finish(0, parts(floats(N_TILES * BANK, "sums1"), BANK))
+        finish(1, parts(floats(2 * BANK, "wide_sums"), BANK))
+        finish(2, parts(floats(2 * BANK, "mixed0"), BANK))

@@ -59,7 +59,7 @@ def tile_list_wildfire_spread_rates_kernel(
         wr_planes = keep.tile([P, N], U8, name="wr_planes", align_bytes=64)
         lo_cols = keep.tile([P, PASSES, PACK], F32, name="lo_cols")
         hi_cols = keep.tile([P, PASSES, PACK], F32, name="hi_cols")
-        wx_raw = [work.tile([P, PACK * H], F32, name="wx_raw%d" % a, tag="wide%d" % a) for a in range(PASSES)]
+        wx_raw = [work.tile([P, PACK * H], F32, name="wx_raw%d" % a, tag="wide%d" % a, align_bytes=64) for a in range(PASSES)]
 
         for rows in (tab_bytes, wf_raw_scales):
             nc.vector.memset(rows[32:64, :].bitcast(I32), 0)
@@ -225,7 +225,7 @@ def tile_list_wildfire_spread_rates_kernel(
 
         def quantize_x(c):
             x_codes[c, 1] = work.tile([P, WIDTHS[c]], U32, name="x_codes%d" % c, tag="x_codes%d" % c, align_bytes=64)[:]
-            x_scales[c, 1] = keep.tile([P, WIDTHS[c]], U8, name="x_scales%d" % c, align_bytes=64)[:]
+            x_scales[c, 1] = work.tile([P, WIDTHS[c]], U8, name="x_scales%d" % c, tag="x_scales%d" % c, align_bytes=64)[:]
             nc.vector.quantize_mx(out=x_codes[c, 1].bitcast(FP8X4), scales=x_scales[c, 1], in_=x_mixed[c][:])
 
         d_banks = {}
@@ -274,8 +274,8 @@ def tile_list_wildfire_spread_rates_kernel(
                     for t in tiles:
                         fuel_pass(c, b, t, a)
 
-        def close_d(c):
-            for b in range(PASSES):
+        def close_d(c, order):
+            for b in order:
                 for t in range(PACK):
                     x_pass(c, b, t, 1)
 
@@ -292,12 +292,15 @@ def tile_list_wildfire_spread_rates_kernel(
         h_planes = {}
         h_mixed = {}
 
-        def clamp(c, b, engines, tag):
+        def halfwords(width, tag):
+            return work.tile([P, width], BF16, name="halfwords_" + tag, tag=tag, align_bytes=64)[:]
+
+        def clamp(c, b, place):
             w = WIDTHS[c]
-            h_planes[c, b] = work.tile([P, PACK, w], BF16, name="h_planes%d%d" % (c, b), tag=tag, align_bytes=64)
+            h_planes[c, b] = place.rearrange("p (t j) -> p t j", t=PACK)
             for t in range(PACK):
                 src = d_sbuf[c, b][:, t * w : (t + 1) * w] if (c, b) in d_sbuf else d_view(c, b, t)
-                engines[t].tensor_scalar(
+                nc.vector.tensor_scalar(
                     h_planes[c, b][:, t, :], src, hi_cols[:, b, t : t + 1], lo_cols[:, b, t : t + 1], MIN, MAX
                 )
 
@@ -305,7 +308,7 @@ def tile_list_wildfire_spread_rates_kernel(
             h_mixed[c, b] = work.tile(
                 [P, PACK * WIDTHS[c]], BF16, name="h_mixed%d%d" % (c, b), tag=tag, align_bytes=64
             )
-            interleave_shared(copies, h_mixed[c, b][:], h_planes[c, b][:])
+            interleave_shared(copies, h_mixed[c, b][:], h_planes[c, b])
 
         y_banks = {}
 
@@ -368,7 +371,7 @@ def tile_list_wildfire_spread_rates_kernel(
             reorder_wf(t // 2, t % 2, "plane%db" % t)
         cast_wx(0, 0)
         cast_wx(0, 1)
-        slope_cols = work.tile([P, N_TILES, S], F32, name="slope_cols", tag="wide0")
+        slope_cols = work.tile([P, N_TILES, S], F32, name="slope_cols", tag="wide0", align_bytes=64)
         nc.sync.dma_start(out=slope_cols[:], in_=slope.rearrange("(n p) j -> p n j", p=P))
         gather_first(3, [floats(BANK, "plane3a"), floats(BANK, "plane3b")])
         for u in range(2):
@@ -386,7 +389,7 @@ def tile_list_wildfire_spread_rates_kernel(
         quantize_first(1, words(NARROW, "plane5a"))
         cast_wx(1, 0)
         cast_wx(1, 1)
-        d_wide = work.tile([P, PASSES, PACK * BANK], F32, name="d_wide", tag="wide1")
+        d_wide = parts(floats(PASSES * PACK * BANK, "wide1"), PACK * BANK)
         gather_halves(6, [floats(NARROW, "plane6a"), chain], parts(wide_sums[:, 2, :], NARROW))
         quantize_wx(1, 0, words(K_PASS, "plane6a"))
         gather_v(1, 0, words(BANK, "chain"))
@@ -399,53 +402,53 @@ def tile_list_wildfire_spread_rates_kernel(
         for t in range(PACK):
             pick_upwind(PACK + t, STARTS[1], waiting[t])
         quantize_x(0)
-        close_d(0)
+        close_d(0, both)
         narrow_sums = wide_sums[:, :, 0:NARROW]
         for t in range(PACK):
             add_downwind(PACK + t, STARTS[1], waiting[t], narrow_sums[:, t, :])
         gather_v(1, BANK, words(BANK, "x_mixed0"))
-        waiting = [wide_sums[:, t, NARROW:BANK] for t in range(PACK)]
-        for t in range(PACK):
-            pick_upwind(PACK + t, STARTS[2], waiting[t])
         for b in both:
-            evacuate_d(0, b, d_wide[:, b, :])
+            evacuate_d(0, b, d_wide[b])
         for b in both:
             open_d(1, b)
         mix_x(1, narrow_sums, [scalar.copy], "x_codes0")
-        clamp(0, 0, [gpsimd] * PACK, "plane7b")
-        mix_h(0, 0, [scalar.copy], "sums0")
-        clamp(0, 1, [vector] * PACK, "wx_bf0")
+        clamp(0, 0, halfwords(PACK * BANK, "plane7b"))
+        mix_h(0, 0, [scalar.copy], "x_scales0")
+        late_picks = d_wide[0][:, 2 * BANK : 4 * BANK]
+        waiting = parts(late_picks, NARROW)
+        for t in range(PACK):
+            pick_upwind(PACK + t, STARTS[2], waiting[t])
         quantize_x(1)
-        close_d(1)
+        close_d(1, both)
         quantize_first(2, words(NARROW, "x_codes0"))
         for b in both:
             open_d(2, b)
         for t in range(PACK):
             add_downwind(PACK + t, STARTS[2], waiting[t], narrow_sums[:, t, :])
-        evacuate_d(1, 0, floats(PACK * NARROW, "plane7b"))
-        evacuate_d(1, 1, d_wide[:, 0, 0 : PACK * NARROW])
+        evacuate_d(1, 0, d_wide[0][:, 0 : PACK * NARROW])
+        evacuate_d(1, 1, floats(PACK * NARROW, "sums0"))
         mix_x(2, narrow_sums, [scalar.copy], "x_codes1")
+        clamp(0, 1, late_picks.bitcast(BF16))
+        mix_h(0, 1, [scalar.copy], "wide_sums")
         wide_codes = words(BANK, "tab0")
         wide_scales = quantize_h(0, 0, wide_codes)
-        mix_h(0, 1, [scalar.copy], "wide_sums")
-        clamp(1, 0, [vector] * PACK, "h_planes10")
-        mix_h(1, 0, [scalar.copy], "h_mixed10")
-        clamp(1, 1, [vector] * PACK, "h_planes11")
-        mix_h(1, 1, [gpsimd_copy], "h_mixed11")
         quantize_x(2)
-        close_d(2)
+        close_d(2, both)
         multiply_h(0, 0, wide_codes, wide_scales)
-        clamp(2, 0, [vector] * PACK, "h_planes20")
-        mix_h(2, 0, [scalar.copy], "h_mixed20")
-        clamp(2, 1, [vector] * PACK, "h_planes21")
-        mix_h(2, 1, [scalar.copy], "h_mixed21")
+        narrow_planes = parts(halfwords(2 * PACK * NARROW, "x_codes1"), PACK * NARROW)
+        for b in both:
+            clamp(1, b, narrow_planes[b])
+            mix_h(1, b, [scalar.copy], ("mixed0", "wx_bf0")[b])
+        for b in both:
+            clamp(2, b, halfwords(PACK * NARROW, ("plane0a", "sums1")[b]))
+            mix_h(2, b, [scalar.copy], ("mixed1", "plane7b")[b])
         late_codes = words(BANK + 4 * NARROW, "x_codes2")
         quantize_h_and_multiply(0, 1, late_codes[:, 0:BANK])
         h_codes = parts(late_codes[:, BANK : BANK + 4 * NARROW], NARROW)
-        quantize_h_and_multiply(1, 0, h_codes[0])
-        quantize_h_and_multiply(1, 1, h_codes[1])
-        quantize_h_and_multiply(2, 0, h_codes[2])
-        quantize_h_and_multiply(2, 1, h_codes[3])
-        finish(0, parts(floats(N_TILES * BANK, "sums1"), BANK))
-        finish(1, parts(floats(2 * BANK, "wide_sums"), BANK))
-        finish(2, parts(floats(2 * BANK, "mixed0"), BANK))
+        for c in (1, 2):
+            for b in both:
+                quantize_h_and_multiply(c, b, h_codes[2 * (c - 1) + b])
+        results = parts(floats(4 * BANK, "sums1"), BANK)
+        finish(0, [floats(BANK, "plane0a")] + results[0:2])
+        finish(1, results[2:4])
+        finish(2, parts(floats(2 * BANK, "tab1"), BANK))

@@ -61,11 +61,11 @@ def tile_list_wildfire_spread_rates_kernel(
         hi_cols = keep.tile([P, PASSES, PACK], F32, name="hi_cols")
         wx_raw = [work.tile([P, PACK * H], F32, name="wx_raw%d" % a, tag="wide%d" % a, align_bytes=64) for a in range(PASSES)]
 
-        for rows in (tab_bytes, wf_raw_scales):
-            nc.vector.memset(rows[32:64, :].bitcast(I32), 0)
-            nc.vector.memset(rows[64:P, :].bitcast(I32), 0)
+        for rows, engine in ((tab_bytes, nc.vector), (wf_raw_scales, nc.gpsimd)):
+            engine.memset(rows[32:64, :].bitcast(I32), 0)
+            engine.memset(rows[64:P, :].bitcast(I32), 0)
         for plane in (v_planes, wf_planes, wr_planes):
-            nc.vector.memset(plane[:].bitcast(I32), 0)
+            nc.gpsimd.memset(plane[:].bitcast(I32), 0)
 
         def load_rows(rows, scales):
             nc.sync.dma_start(out=rows[0:32, :].bitcast(I32), in_=scales.bitcast(I32).rearrange("a q c -> q a c"))
@@ -263,15 +263,15 @@ def tile_list_wildfire_spread_rates_kernel(
                     stop=False,
                 )
 
-        def open_d(c, b):
-            per_bank = BANK // WIDTHS[c]
-            for k, number in enumerate(D_BANKS[c, b]):
-                d_banks[c, b, k] = psum.tile([P, BANK], F32, name="d%d%d%d" % (c, b, k), tag="bank%d" % number)
-                tiles = range(k * per_bank, (k + 1) * per_bank)
-                for t in tiles:
+        def open_d(c, order):
+            for b in order:
+                for k, number in enumerate(D_BANKS[c, b]):
+                    d_banks[c, b, k] = psum.tile([P, BANK], F32, name="d%d%d%d" % (c, b, k), tag="bank%d" % number)
+                for t in range(PACK):
                     x_pass(c, b, t, 0)
-                for a in range(PASSES):
-                    for t in tiles:
+            for a in range(PASSES):
+                for b in order:
+                    for t in range(PACK):
                         fuel_pass(c, b, t, a)
 
         def close_d(c, order):
@@ -279,36 +279,36 @@ def tile_list_wildfire_spread_rates_kernel(
                 for t in range(PACK):
                     x_pass(c, b, t, 1)
 
-        d_sbuf = {}
-
         def evacuate_d(c, b, place):
-            d_sbuf[c, b] = place
+            per_bank = BANK // WIDTHS[c]
             for k in range(len(D_BANKS[c, b])):
-                nc.scalar.copy(out=place[:, k * BANK : (k + 1) * BANK], in_=d_banks[c, b, k][:])
+                sums = d_banks[c, b, k][:].rearrange("p (t j) -> p t j", t=per_bank)
+                nc.scalar.copy(out=place[:, k * per_bank : (k + 1) * per_bank, :], in_=sums)
 
-        def gpsimd_copy(out, in_):
-            nc.gpsimd.tensor_scalar(out, in_, 1.0, 0.0, MULT, ADD)
-
-        h_planes = {}
         h_mixed = {}
 
         def halfwords(width, tag):
             return work.tile([P, width], BF16, name="halfwords_" + tag, tag=tag, align_bytes=64)[:]
 
-        def clamp(c, b, place):
-            w = WIDTHS[c]
-            h_planes[c, b] = place.rearrange("p (t j) -> p t j", t=PACK)
+        def by_plane(place):
+            return place.rearrange("p (t j) -> p t j", t=PACK)
+
+        def clamp(b, drivers, planes):
             for t in range(PACK):
-                src = d_sbuf[c, b][:, t * w : (t + 1) * w] if (c, b) in d_sbuf else d_view(c, b, t)
                 nc.vector.tensor_scalar(
-                    h_planes[c, b][:, t, :], src, hi_cols[:, b, t : t + 1], lo_cols[:, b, t : t + 1], MIN, MAX
+                    planes[:, t, :], drivers[t], hi_cols[:, b, t : t + 1], lo_cols[:, b, t : t + 1], MIN, MAX
                 )
 
-        def mix_h(c, b, copies, tag):
+        def clamp_from_psum(c, b, planes):
+            for t in range(PACK):
+                low = lo_cols[:, b, t : t + 1].to_broadcast([P, WIDTHS[c]])
+                nc.vector.scalar_tensor_tensor(planes[:, t, :], d_view(c, b, t), hi_cols[:, b, t : t + 1], low, MIN, MAX)
+
+        def mix_h(c, b, planes, tag):
             h_mixed[c, b] = work.tile(
                 [P, PACK * WIDTHS[c]], BF16, name="h_mixed%d%d" % (c, b), tag=tag, align_bytes=64
             )
-            interleave_shared(copies, h_mixed[c, b][:], h_planes[c, b])
+            interleave(nc.scalar.copy, h_mixed[c, b][:], planes)
 
         y_banks = {}
 
@@ -389,14 +389,15 @@ def tile_list_wildfire_spread_rates_kernel(
         quantize_first(1, words(NARROW, "plane5a"))
         cast_wx(1, 0)
         cast_wx(1, 1)
-        d_wide = parts(floats(PASSES * PACK * BANK, "wide1"), PACK * BANK)
+        d_store = floats(PACK * (2 * BANK + NARROW), "wide1")
+        d_first = by_plane(d_store[:, 0 : PACK * BANK])
+        d_second = by_plane(d_store[:, PACK * BANK : PACK * (2 * BANK + NARROW)])
         gather_halves(6, [floats(NARROW, "plane6a"), chain], parts(wide_sums[:, 2, :], NARROW))
         quantize_wx(1, 0, words(K_PASS, "plane6a"))
         gather_v(1, 0, words(BANK, "chain"))
         gather_halves(7, [floats(NARROW, "plane7a"), floats(NARROW, "plane7b")], parts(wide_sums[:, 3, :], NARROW))
         quantize_wx(1, 1, words(K_PASS, "plane7a"))
-        for b in both:
-            open_d(0, b)
+        open_d(0, both)
         mix_x(0, wide_sums[:], [scalar.copy], "x_mixed0")
         waiting = parts(floats(PACK * NARROW, "plane7b"), NARROW)
         for t in range(PACK):
@@ -407,41 +408,45 @@ def tile_list_wildfire_spread_rates_kernel(
         for t in range(PACK):
             add_downwind(PACK + t, STARTS[1], waiting[t], narrow_sums[:, t, :])
         gather_v(1, BANK, words(BANK, "x_mixed0"))
-        for b in both:
-            evacuate_d(0, b, d_wide[b])
-        for b in both:
-            open_d(1, b)
+        evacuate_d(0, 0, d_first)
+        evacuate_d(0, 1, d_second[:, :, 0:BANK])
+        open_d(1, both)
         mix_x(1, narrow_sums, [scalar.copy], "x_codes0")
-        clamp(0, 0, halfwords(PACK * BANK, "plane7b"))
-        mix_h(0, 0, [scalar.copy], "x_scales0")
-        late_picks = d_wide[0][:, 2 * BANK : 4 * BANK]
-        waiting = parts(late_picks, NARROW)
-        for t in range(PACK):
+        planes = by_plane(halfwords(PACK * BANK, "plane7b"))
+        clamp(0, [d_first[:, t, :] for t in range(PACK)], planes)
+        mix_h(0, 0, planes, "x_scales0")
+        late_picks = d_store[:, BANK : PACK * BANK]
+        waiting = [by_plane(late_picks)[:, t, 0:NARROW] for t in range(PACK)]
+        for t in reversed(range(PACK)):
             pick_upwind(PACK + t, STARTS[2], waiting[t])
         quantize_x(1)
-        close_d(1, both)
+        close_d(1, (1, 0))
         quantize_first(2, words(NARROW, "x_codes0"))
-        for b in both:
-            open_d(2, b)
+        open_d(2, both)
         for t in range(PACK):
             add_downwind(PACK + t, STARTS[2], waiting[t], narrow_sums[:, t, :])
-        evacuate_d(1, 0, d_wide[0][:, 0 : PACK * NARROW])
-        evacuate_d(1, 1, floats(PACK * NARROW, "sums0"))
+        evacuate_d(1, 1, d_second[:, :, BANK : BANK + NARROW])
+        d_narrow = by_plane(floats(PACK * NARROW, "mixed0"))
+        evacuate_d(1, 0, d_narrow)
         mix_x(2, narrow_sums, [scalar.copy], "x_codes1")
-        clamp(0, 1, late_picks.bitcast(BF16))
-        mix_h(0, 1, [scalar.copy], "wide_sums")
-        wide_codes = words(BANK, "tab0")
-        wide_scales = quantize_h(0, 0, wide_codes)
+        planes = by_plane(late_picks.bitcast(BF16))
+        clamp(1, [d_second[:, t, :] for t in range(PACK)], planes)
+        mix_h(0, 1, planes[:, :, 0:BANK], "sums0")
+        held_planes = planes[:, :, BANK : BANK + NARROW]
         quantize_x(2)
         close_d(2, both)
-        multiply_h(0, 0, wide_codes, wide_scales)
-        narrow_planes = parts(halfwords(2 * PACK * NARROW, "x_codes1"), PACK * NARROW)
+        quantize_h_and_multiply(0, 0, words(BANK, "wide_sums"))
+        planes = by_plane(halfwords(PACK * NARROW, "x_codes1"))
+        clamp(0, [d_narrow[:, t, :] for t in range(PACK)], planes)
+        mix_h(1, 0, planes, "x_scales0")
+        h_mixed[1, 1] = work.tile([P, PACK * NARROW], BF16, name="h_mixed11", tag="mixed0", align_bytes=64)
+        nc.gpsimd.tensor_scalar(
+            h_mixed[1, 1][:].rearrange("p (j t) -> p j t", t=PACK), held_planes.rearrange("p t j -> p j t"), 1.0, 0.0, MULT, ADD
+        )
         for b in both:
-            clamp(1, b, narrow_planes[b])
-            mix_h(1, b, [scalar.copy], ("mixed0", "wx_bf0")[b])
-        for b in both:
-            clamp(2, b, halfwords(PACK * NARROW, ("plane0a", "sums1")[b]))
-            mix_h(2, b, [scalar.copy], ("mixed1", "plane7b")[b])
+            planes = by_plane(halfwords(PACK * NARROW, ("plane0a", "sums1")[b]))
+            clamp_from_psum(2, b, planes)
+            mix_h(2, b, planes, ("mixed1", "plane7b")[b])
         late_codes = words(BANK + 4 * NARROW, "x_codes2")
         quantize_h_and_multiply(0, 1, late_codes[:, 0:BANK])
         h_codes = parts(late_codes[:, BANK : BANK + 4 * NARROW], NARROW)

@@ -121,14 +121,14 @@ def tile_list_wildfire_spread_rates_kernel(
         load_x_plane(3)
         load_tab(0)
         load_x_plane(4)
-        spread_rows(wf_planes, wf_rows)
-        spread_rows(v_planes, v_rows)
         load_x_plane(5)
         load_wx(1, 0)
         load_wx(1, 1)
         load_x_plane(6)
         load_tab(1)
         load_x_plane(7)
+        spread_rows(wf_planes, wf_rows)
+        spread_rows(v_planes, v_rows)
         nc.sync.dma_start(out=lo_cols[:], in_=lo.rearrange("(b p t) -> p b t", b=PASSES, t=PACK))
         nc.sync.dma_start(out=hi_cols[:], in_=hi.rearrange("(b p t) -> p b t", b=PASSES, t=PACK))
         nc.sync.dma_start(
@@ -158,13 +158,15 @@ def tile_list_wildfire_spread_rates_kernel(
 
         wf_codes = {}
 
-        def reorder_wf(a, b, tag):
-            wf_codes[a, b] = work.tile([P, 2 * K_PASS], U8, name="wf_codes%d%d" % (a, b), tag=tag, align_bytes=64)
-            col = a * H + b * K_PASS
-            nc.gpsimd.tensor_copy(
-                out=wf_codes[a, b][:].rearrange("p (t m e) -> p t m e", t=PACK, e=2),
-                in_=wf_raw[:, 2 * col : 2 * (col + K_PASS)].rearrange("p (m t e) -> p t m e", t=PACK, e=2),
-            )
+        def reorder_wf(a, tag):
+            ordered = work.tile([P, 2 * H], U8, name="wf_codes%d" % a, tag=tag, align_bytes=64)
+            for b in range(PASSES):
+                wf_codes[a, b] = ordered[:, 2 * b * K_PASS : 2 * (b + 1) * K_PASS]
+                col = a * H + b * K_PASS
+                nc.gpsimd.tensor_copy(
+                    out=wf_codes[a, b].rearrange("p (t m e) -> p t m e", t=PACK, e=2),
+                    in_=wf_raw[:, 2 * col : 2 * (col + K_PASS)].rearrange("p (m t e) -> p t m e", t=PACK, e=2),
+                )
 
         def list_cols(first, width):
             return slice(first // LIST_ROWS, (first + width) // LIST_ROWS)
@@ -196,8 +198,14 @@ def tile_list_wildfire_spread_rates_kernel(
         x_codes = {}
         x_scales = {}
 
-        def gather_first(t, spares):
-            gather_halves(t, spares, [first_sums[u][:, t, :] for u in range(2)])
+        def gather_first(t):
+            upwind = floats(S, ("upwind0", "upwind1", "upwind0", "upwind3")[t])
+            downwind = floats(S, "downwind%d" % (t % 2))
+            nc.vector.tensor_copy(upwind, x_planes[t][:].indirect(upwind_list[:]))
+            nc.vector.tensor_copy(downwind, x_planes[t][:].indirect(downwind_list[:]))
+            for u in range(2):
+                cols = slice(u * BANK, (u + 1) * BANK)
+                nc.gpsimd.tensor_tensor(first_sums[u][:, t, :], upwind[:, cols], downwind[:, cols], ADD)
 
         def quantize_first(c, codes):
             u, first = divmod(STARTS[c], BANK)
@@ -365,40 +373,39 @@ def tile_list_wildfire_spread_rates_kernel(
 
         both = range(PASSES)
         vector, gpsimd, scalar = nc.vector, nc.gpsimd, nc.scalar
-        picked = floats(BANK, "plane0a")
-        for t in range(3):
-            gather_first(t, [picked, floats(BANK, "plane%db" % t)])
-            reorder_wf(t // 2, t % 2, "plane%db" % t)
+        for t in range(PACK):
+            gather_first(t)
+            if t < PASSES:
+                reorder_wf(t, ("wf_first", "upwind1")[t])
         cast_wx(0, 0)
         cast_wx(0, 1)
         slope_cols = work.tile([P, N_TILES, S], F32, name="slope_cols", tag="wide0", align_bytes=64)
         nc.sync.dma_start(out=slope_cols[:], in_=slope.rearrange("(n p) j -> p n j", p=P))
-        gather_first(3, [floats(BANK, "plane3a"), floats(BANK, "plane3b")])
         for u in range(2):
             interleave(scalar.copy, first_mixed[u][:], first_sums[u][:])
-        for b, codes in enumerate(parts(words(2 * K_PASS, "plane3a"), K_PASS)):
-            quantize_wx(0, b, codes)
-        reorder_wf(1, 1, "wx_bf1")
-        gather_v(0, 0, words(S, "plane3b"))
+        gather_v(0, 0, words(S, "v_first"))
 
         wide_sums = work.tile([P, PACK, BANK], F32, name="wide_sums", tag="wide_sums", align_bytes=64)
         chain = floats(NARROW, "chain")
         gather_halves(4, [floats(NARROW, "plane4a"), chain], parts(wide_sums[:, 0, :], NARROW))
-        quantize_first(0, words(BANK, "plane4a"))
+        for b, codes in enumerate(parts(words(2 * K_PASS, "plane4a"), K_PASS)):
+            quantize_wx(0, b, codes)
         gather_halves(5, [floats(NARROW, "plane5a"), chain], parts(wide_sums[:, 1, :], NARROW))
-        quantize_first(1, words(NARROW, "plane5a"))
+        quantize_first(0, words(BANK, "plane5a"))
         cast_wx(1, 0)
         cast_wx(1, 1)
         d_store = floats(PACK * (2 * BANK + NARROW), "wide1")
         d_first = by_plane(d_store[:, 0 : PACK * BANK])
         d_second = by_plane(d_store[:, PACK * BANK : PACK * (2 * BANK + NARROW)])
         gather_halves(6, [floats(NARROW, "plane6a"), chain], parts(wide_sums[:, 2, :], NARROW))
-        quantize_wx(1, 0, words(K_PASS, "plane6a"))
+        after_six = words(K_PASS + NARROW, "plane6a")
+        quantize_first(1, after_six[:, K_PASS : K_PASS + NARROW])
+        quantize_wx(1, 0, after_six[:, 0:K_PASS])
         gather_v(1, 0, words(BANK, "chain"))
         gather_halves(7, [floats(NARROW, "plane7a"), floats(NARROW, "plane7b")], parts(wide_sums[:, 3, :], NARROW))
         quantize_wx(1, 1, words(K_PASS, "plane7a"))
         open_d(0, both)
-        mix_x(0, wide_sums[:], [scalar.copy], "x_mixed0")
+        mix_x(0, wide_sums[:], [scalar.copy], "upwind3")
         waiting = parts(floats(PACK * NARROW, "plane7b"), NARROW)
         for t in range(PACK):
             pick_upwind(PACK + t, STARTS[1], waiting[t])
@@ -407,7 +414,7 @@ def tile_list_wildfire_spread_rates_kernel(
         narrow_sums = wide_sums[:, :, 0:NARROW]
         for t in range(PACK):
             add_downwind(PACK + t, STARTS[1], waiting[t], narrow_sums[:, t, :])
-        gather_v(1, BANK, words(BANK, "x_mixed0"))
+        gather_v(1, BANK, words(BANK, "upwind3"))
         evacuate_d(0, 0, d_first)
         evacuate_d(0, 1, d_second[:, :, 0:BANK])
         open_d(1, both)
@@ -444,7 +451,7 @@ def tile_list_wildfire_spread_rates_kernel(
             h_mixed[1, 1][:].rearrange("p (j t) -> p j t", t=PACK), held_planes.rearrange("p t j -> p j t"), 1.0, 0.0, MULT, ADD
         )
         for b in both:
-            planes = by_plane(halfwords(PACK * NARROW, ("plane0a", "sums1")[b]))
+            planes = by_plane(halfwords(PACK * NARROW, ("upwind0", "sums1")[b]))
             clamp_from_psum(2, b, planes)
             mix_h(2, b, planes, ("mixed1", "plane7b")[b])
         late_codes = words(BANK + 4 * NARROW, "x_codes2")
@@ -454,6 +461,6 @@ def tile_list_wildfire_spread_rates_kernel(
             for b in both:
                 quantize_h_and_multiply(c, b, h_codes[2 * (c - 1) + b])
         results = parts(floats(4 * BANK, "sums1"), BANK)
-        finish(0, [floats(BANK, "plane0a")] + results[0:2])
+        finish(0, [floats(BANK, "upwind0")] + results[0:2])
         finish(1, results[2:4])
-        finish(2, parts(floats(2 * BANK, "tab1"), BANK))
+        finish(2, parts(floats(2 * BANK, "downwind1"), BANK))

@@ -51,7 +51,7 @@ def tile_list_wildfire_spread_rates_kernel(
         v_codes = {}
         v_rows = work.tile([P, S], U8, name="v_rows", tag="v_rows")
         v_planes = keep.tile([P, PASSES * S], U8, name="v_planes", align_bytes=64)
-        wf_raw = keep.tile([P, PASSES * H * 2], U8, name="wf_raw")
+        wf_raw = [work.tile([P, 2 * H], U8, name="wf_raw%d" % a, tag="sums%d" % a, align_bytes=64) for a in range(PASSES)]
         wf_raw_scales = keep.tile([P, H], U8, name="wf_raw_scales")
         wf_rows = work.tile([P, H], U8, name="wf_rows", tag="wf_rows")
         wf_planes = keep.tile([P, PASSES * H], U8, name="wf_planes", align_bytes=64)
@@ -110,10 +110,8 @@ def tile_list_wildfire_spread_rates_kernel(
             out=wf_rows[:].rearrange("p (b t m) -> p b t m", t=PACK, m=P),
             in_=wf_raw_scales[:].rearrange("p (b m t) -> p b t m", t=PACK, m=P),
         )
-        nc.sync.dma_start(
-            out=wf_raw[:].bitcast(I32).rearrange("p (a c) -> p a c", a=PASSES),
-            in_=wf_words.bitcast(I32).rearrange("a p c -> p a c"),
-        )
+        for a in range(PASSES):
+            nc.sync.dma_start(out=wf_raw[a][:].bitcast(I32), in_=wf_words[a].bitcast(I32))
         load_x_plane(1)
         load_wx(0, 0)
         load_x_plane(2)
@@ -162,11 +160,14 @@ def tile_list_wildfire_spread_rates_kernel(
             ordered = work.tile([P, 2 * H], U8, name="wf_codes%d" % a, tag=tag, align_bytes=64)
             for b in range(PASSES):
                 wf_codes[a, b] = ordered[:, 2 * b * K_PASS : 2 * (b + 1) * K_PASS]
-                col = a * H + b * K_PASS
+                col = b * K_PASS
                 nc.gpsimd.tensor_copy(
                     out=wf_codes[a, b].rearrange("p (t m e) -> p t m e", t=PACK, e=2),
-                    in_=wf_raw[:, 2 * col : 2 * (col + K_PASS)].rearrange("p (m t e) -> p t m e", t=PACK, e=2),
+                    in_=wf_raw[a][:, 2 * col : 2 * (col + K_PASS)].rearrange("p (m t e) -> p t m e", t=PACK, e=2),
                 )
+
+        for a in range(PASSES):
+            reorder_wf(a, "wf_codes%d" % a)
 
         def list_cols(first, width):
             return slice(first // LIST_ROWS, (first + width) // LIST_ROWS)
@@ -199,8 +200,8 @@ def tile_list_wildfire_spread_rates_kernel(
         x_scales = {}
 
         def gather_first(t):
-            upwind = floats(S, ("upwind0", "upwind1", "upwind0", "upwind3")[t])
-            downwind = floats(S, "downwind%d" % (t % 2))
+            upwind = floats(S, "upwind%d" % (t % 3))
+            downwind = floats(S, "downwind%d" % (t % 3))
             nc.vector.tensor_copy(upwind, x_planes[t][:].indirect(upwind_list[:]))
             nc.vector.tensor_copy(downwind, x_planes[t][:].indirect(downwind_list[:]))
             for u in range(2):
@@ -375,8 +376,6 @@ def tile_list_wildfire_spread_rates_kernel(
         vector, gpsimd, scalar = nc.vector, nc.gpsimd, nc.scalar
         for t in range(PACK):
             gather_first(t)
-            if t < PASSES:
-                reorder_wf(t, ("wf_first", "upwind1")[t])
         cast_wx(0, 0)
         cast_wx(0, 1)
         slope_cols = work.tile([P, N_TILES, S], F32, name="slope_cols", tag="wide0", align_bytes=64)
@@ -405,7 +404,7 @@ def tile_list_wildfire_spread_rates_kernel(
         gather_halves(7, [floats(NARROW, "plane7a"), floats(NARROW, "plane7b")], parts(wide_sums[:, 3, :], NARROW))
         quantize_wx(1, 1, words(K_PASS, "plane7a"))
         open_d(0, both)
-        mix_x(0, wide_sums[:], [scalar.copy], "upwind3")
+        mix_x(0, wide_sums[:], [scalar.copy], "upwind2")
         waiting = parts(floats(PACK * NARROW, "plane7b"), NARROW)
         for t in range(PACK):
             pick_upwind(PACK + t, STARTS[1], waiting[t])
@@ -414,7 +413,7 @@ def tile_list_wildfire_spread_rates_kernel(
         narrow_sums = wide_sums[:, :, 0:NARROW]
         for t in range(PACK):
             add_downwind(PACK + t, STARTS[1], waiting[t], narrow_sums[:, t, :])
-        gather_v(1, BANK, words(BANK, "upwind3"))
+        gather_v(1, BANK, words(BANK, "upwind2"))
         evacuate_d(0, 0, d_first)
         evacuate_d(0, 1, d_second[:, :, 0:BANK])
         open_d(1, both)

@@ -101,10 +101,10 @@ def tile_list_wildfire_spread_rates_kernel(
 
         nc.sync.dma_start(fuel_list[:], offs)
         load_rows(tab_bytes, tab_scales)
-        load_rows(wf_raw_scales, wf_scales)
         load_x_plane(0)
         nc.sync.dma_start(upwind_list[:], offs2)
         nc.sync.dma_start(downwind_list[:], offs3)
+        load_rows(wf_raw_scales, wf_scales)
         nc.vector.tensor_copy(v_rows[:], tab_bytes[:].indirect(fuel_list[:]))
         nc.gpsimd.tensor_copy(
             out=wf_rows[:].rearrange("p (b t m) -> p b t m", t=PACK, m=P),
@@ -305,13 +305,13 @@ def tile_list_wildfire_spread_rates_kernel(
         def clamp(b, drivers, planes):
             for t in range(PACK):
                 nc.vector.tensor_scalar(
-                    planes[:, t, :], drivers[t], hi_cols[:, b, t : t + 1], lo_cols[:, b, t : t + 1], MIN, MAX
+                    planes[:, t, :], drivers[t], lo_cols[:, b, t : t + 1], hi_cols[:, b, t : t + 1], MAX, MIN
                 )
 
         def clamp_from_psum(c, b, planes):
             for t in range(PACK):
-                low = lo_cols[:, b, t : t + 1].to_broadcast([P, WIDTHS[c]])
-                nc.vector.scalar_tensor_tensor(planes[:, t, :], d_view(c, b, t), hi_cols[:, b, t : t + 1], low, MIN, MAX)
+                high = hi_cols[:, b, t : t + 1].to_broadcast([P, WIDTHS[c]])
+                nc.vector.scalar_tensor_tensor(planes[:, t, :], d_view(c, b, t), lo_cols[:, b, t : t + 1], high, MAX, MIN)
 
         def mix_h(c, b, planes, tag):
             h_mixed[c, b] = work.tile(

@@ -23,49 +23,70 @@ PACK = 4
 K_PASS = P * PACK
 PASSES = K // K_PASS
 BANK = 512
-NARROW = 256
-WIDTHS = (BANK, NARROW, NARROW)
-STARTS = (0, BANK, BANK + NARROW)
+HALF = 256
+WIDTHS = (512, 256, 256)
+STARTS = (0, 512, 768)
+WIDE, MIDDLE, LAST = 0, 1, 2
 LIST_ROWS = 16
-FP4_WIDTH = 128
 N_TILES = N // P
 D_BANKS = {(0, 0): (0, 1, 2, 3), (0, 1): (4, 5, 6, 7), (1, 0): (0, 1), (1, 1): (2, 3), (2, 0): (4, 5), (2, 1): (6, 7)}
 Y_BANKS = ((0, 1, 2), (3, 4), (5, 6))
+
+
+def pieces(index, width):
+    found = []
+    first = 0
+    while first < width:
+        bank, column = divmod(index * width + first, BANK)
+        count = max(n for n in (512, 256, 128) if n <= min(width - first, BANK - column))
+        found.append((bank, column, count, first))
+        first = first + count
+    return found
 
 
 def tile_list_wildfire_spread_rates_kernel(
     tc, tab_words, tab_scales, offs, xT, offs2, offs3, wf_words, wf_scales, wx, lo, hi, wr_words, wr_scales, slope, out
 ):
     nc = tc.nc
+    vector, gpsimd, scalar = nc.vector, nc.gpsimd, nc.scalar
+    both = range(PASSES)
     with ExitStack() as ctx:
         keep = ctx.enter_context(tc.tile_pool(name="keep", bufs=1))
         work = ctx.enter_context(tc.tile_pool(name="work", bufs=1))
         psum = ctx.enter_context(tc.psum_pool(name="psum", bufs=1))
 
+        def place(dtype, width, tag):
+            return work.tile([P, width], dtype, name="tile_" + tag, tag=tag, align_bytes=64)[:]
+
+        def parts(whole, width):
+            return [whole[:, j : min(j + width, whole.shape[1])] for j in range(0, whole.shape[1], width)]
+
+        def by_plane(whole):
+            return whole.rearrange("p (t j) -> p t j", t=PACK)
+
         fuel_list = keep.tile([P, S // LIST_ROWS], U16, name="fuel_list")
         upwind_list = keep.tile([P, S // LIST_ROWS], U16, name="upwind_list")
         downwind_list = keep.tile([P, S // LIST_ROWS], U16, name="downwind_list")
-        x_planes = [keep.tile([P, T], F32, name="x_plane%d" % i) for i in range(PASSES * PACK)]
-        tab_codes = [work.tile([P, T], U32, name="tab_codes%d" % a, tag="tab%d" % a, align_bytes=64) for a in range(PASSES)]
+        x_planes = [place(F32, T, "plane%d" % i) for i in range(PASSES * PACK)]
+        tab_codes = [place(U32, T, "tab%d" % a) for a in both]
         tab_bytes = keep.tile([P, T], U8, name="tab_bytes")
-        v_codes = {}
-        v_rows = work.tile([P, S], U8, name="v_rows", tag="v_rows")
+        v_rows = keep.tile([P, S], U8, name="v_rows")
         v_planes = keep.tile([P, PASSES * S], U8, name="v_planes", align_bytes=64)
-        wf_raw = [work.tile([P, 2 * H], U8, name="wf_raw%d" % a, tag="sums%d" % a, align_bytes=64) for a in range(PASSES)]
+        wf_raw = [place(U8, 2 * H, "sums%d" % a) for a in both]
         wf_raw_scales = keep.tile([P, H], U8, name="wf_raw_scales")
-        wf_rows = work.tile([P, H], U8, name="wf_rows", tag="wf_rows")
+        wf_rows = keep.tile([P, H], U8, name="wf_rows")
         wf_planes = keep.tile([P, PASSES * H], U8, name="wf_planes", align_bytes=64)
         wr_codes = keep.tile([P, PASSES, N], U32, name="wr_codes", align_bytes=64)
         wr_planes = keep.tile([P, N], U8, name="wr_planes", align_bytes=64)
         lo_cols = keep.tile([P, PASSES, PACK], F32, name="lo_cols")
         hi_cols = keep.tile([P, PASSES, PACK], F32, name="hi_cols")
-        wx_raw = [work.tile([P, PACK * H], F32, name="wx_raw%d" % a, tag="wide%d" % a, align_bytes=64) for a in range(PASSES)]
+        wx_raw = {(a, b): place(F32, PACK * K_PASS, "wx_raw%d%d" % (a, b)) for a in both for b in both}
 
-        for rows, engine in ((tab_bytes, nc.vector), (wf_raw_scales, nc.gpsimd)):
+        for rows, engine in ((tab_bytes, vector), (wf_raw_scales, gpsimd)):
             engine.memset(rows[32:64, :].bitcast(I32), 0)
             engine.memset(rows[64:P, :].bitcast(I32), 0)
         for plane in (v_planes, wf_planes, wr_planes):
-            nc.gpsimd.memset(plane[:].bitcast(I32), 0)
+            gpsimd.memset(plane[:].bitcast(I32), 0)
 
         def load_rows(rows, scales):
             nc.sync.dma_start(out=rows[0:32, :].bitcast(I32), in_=scales.bitcast(I32).rearrange("a q c -> q a c"))
@@ -87,17 +108,187 @@ def tile_list_wildfire_spread_rates_kernel(
         def load_x_plane(i):
             a, t = divmod(i, PACK)
             rows = xT[a * K_PASS : (a + 1) * K_PASS, :].rearrange("(p t) c -> p t c", t=PACK)
-            nc.sync.dma_start(out=x_planes[i][:], in_=rows[:, t, :])
+            nc.sync.dma_start(out=x_planes[i], in_=rows[:, t, :])
 
-        def load_wx(a, u):
-            rows = wx[a * K_PASS : (a + 1) * K_PASS, :].rearrange("(p i) c -> p (i c)", i=PACK)
-            cols = slice(2 * u * H, 2 * (u + 1) * H)
-            nc.sync.dma_start(out=wx_raw[a][:, cols], in_=rows[:, cols])
+        def load_wx(a, b):
+            rows = wx[a * K_PASS : (a + 1) * K_PASS, b * K_PASS : (b + 1) * K_PASS]
+            nc.sync.dma_start(out=by_plane(wx_raw[a, b]), in_=rows.rearrange("(p i) c -> p i c", i=PACK))
 
         def load_tab(a):
+            nc.sync.dma_start(out=tab_codes[a].bitcast(I32), in_=tab_words[a].rearrange("p t i -> p (t i)").bitcast(I32))
+
+        slopes = {}
+
+        def load_slope(c, tag):
+            slopes[c] = place(F32, N_TILES * WIDTHS[c], tag)
+            cols = slope[:, STARTS[c] : STARTS[c] + WIDTHS[c]]
             nc.sync.dma_start(
-                out=tab_codes[a][:].bitcast(I32), in_=tab_words[a].rearrange("p t i -> p (t i)").bitcast(I32)
+                out=slopes[c].rearrange("p (n j) -> p n j", n=N_TILES), in_=cols.rearrange("(n p) j -> p n j", p=P)
             )
+
+        wx_codes = {}
+        wx_scales = {}
+        wx_grouped = {}
+
+        def cast_wx(a, b, tag):
+            wx_grouped[a, b] = place(BF16, PACK * K_PASS, tag)
+            scalar.copy(
+                out=wx_grouped[a, b].rearrange("p (t m i) -> p m t i", t=PACK, i=PACK),
+                in_=wx_raw[a, b].rearrange("p (i m t) -> p m t i", i=PACK, t=PACK),
+            )
+
+        def quantize(values, codes, name):
+            scales = keep.tile([P, codes.shape[1]], U8, name=name, align_bytes=64)[:]
+            vector.quantize_mx(out=codes.bitcast(FP8X4), scales=scales, in_=values)
+            return scales
+
+        def quantize_wx(a, b, codes):
+            wx_codes[a, b] = codes
+            wx_scales[a, b] = quantize(wx_grouped[a, b], codes, "wx_scales%d%d" % (a, b))
+
+        wf_codes = {}
+
+        def reorder_wf(a):
+            ordered = place(U8, 2 * H, "wf_codes%d" % a)
+            for b in both:
+                cols = slice(2 * b * K_PASS, 2 * (b + 1) * K_PASS)
+                wf_codes[a, b] = ordered[:, cols]
+                gpsimd.tensor_copy(
+                    out=wf_codes[a, b].rearrange("p (t m e) -> p t m e", t=PACK, e=2),
+                    in_=wf_raw[a][:, cols].rearrange("p (m t e) -> p t m e", t=PACK, e=2),
+                )
+
+        def list_cols(first, width):
+            return slice(first // LIST_ROWS, (first + width) // LIST_ROWS)
+
+        def pick(i, cells, first, picks):
+            vector.tensor_copy(picks, x_planes[i].indirect(cells[:, list_cols(first, picks.shape[1])]))
+
+        def add_downwind(i, first, upwind, total):
+            cols = list_cols(first, upwind.shape[1])
+            vector.tensor_tensor(total, x_planes[i].indirect(downwind_list[:, cols]), upwind, ADD)
+
+        def gather_halves(i, spares, sums, ahead=None):
+            for u in range(2):
+                pick(i, upwind_list, u * HALF, spares[u])
+            if ahead is not None:
+                pick(i, upwind_list, STARTS[MIDDLE], ahead)
+            for u in range(2):
+                add_downwind(i, u * HALF, spares[u], sums[u])
+
+        def interleave(dst, src):
+            scalar.copy(
+                out=dst.rearrange("p (c i t) -> p c t i", i=PACK, t=PACK), in_=src.rearrange("p t (c i) -> p c t i", i=PACK)
+            )
+
+        x_codes = {}
+        x_scales = {}
+        v_codes = {}
+
+        def chunks_in(first, width):
+            return [c for c in range(len(WIDTHS)) if first <= STARTS[c] < first + width]
+
+        def quantize_x(a, first, values, codes):
+            scales = quantize(values, codes, "x_scales%d_%d" % (a, first))
+            for c in chunks_in(first, codes.shape[1]):
+                cols = slice(STARTS[c] - first, STARTS[c] - first + WIDTHS[c])
+                x_codes[c, a] = codes[:, cols]
+                x_scales[c, a] = scales[:, cols]
+
+        def gather_v(a, first, picks):
+            width = picks.shape[1]
+            vector.tensor_copy(picks, tab_codes[a].indirect(fuel_list[:, list_cols(first, width)]))
+            for c in chunks_in(first, width):
+                v_codes[c, a] = picks[:, STARTS[c] - first : STARTS[c] - first + WIDTHS[c]]
+
+        d_banks = {}
+
+        def bank_tile(name, number):
+            return psum.tile([P, BANK], F32, name=name, tag="bank%d" % number)
+
+        def x_passes(c, b, a, closing=False):
+            if a == 0:
+                d_banks[c, b] = [bank_tile("d%d%d%d" % (c, b, n), n) for n in D_BANKS[c, b]]
+            for t in range(PACK):
+                cols = slice(t * P, (t + 1) * P)
+                for bank, column, count, first in pieces(t, WIDTHS[c]):
+                    nc.tensor.matmul_mx(
+                        out=d_banks[c, b][bank][:, column : column + count],
+                        lhsT=wx_codes[a, b][:, cols].bitcast(FP8X4),
+                        lhsT_scale=wx_scales[a, b][:, cols],
+                        rhs=x_codes[c, a][:, first : first + count].bitcast(FP8X4),
+                        rhs_scale=x_scales[c, a][:, first : first + count],
+                        start=(a == 0 and column == 0),
+                        stop=(closing and column + count == BANK),
+                    )
+
+        def fuel_passes(c, b, a, closing=False):
+            for t in range(PACK):
+                col = a * H + b * K_PASS + t * P
+                for bank, column, count, first in pieces(t, WIDTHS[c]):
+                    entry = a * S + STARTS[c] + first
+                    nc.tensor.matmul_mx(
+                        out=d_banks[c, b][bank][:, column : column + count],
+                        lhsT=wf_codes[a, b][:, 2 * t * P : 2 * (t + 1) * P].bitcast(FP4X4),
+                        lhsT_scale=wf_planes[:, col : col + P],
+                        rhs=v_codes[c, a][:, first : first + count].bitcast(FP8X4),
+                        rhs_scale=v_planes[:, entry : entry + count],
+                        start=False,
+                        stop=(closing and column + count == BANK),
+                    )
+
+        def evacuate(banks, whole):
+            for bank, part in zip(banks, parts(whole, BANK)):
+                scalar.copy(out=part, in_=bank[:, 0 : part.shape[1]])
+
+        def in_banks(c, b):
+            return [part for bank in d_banks[c, b] for part in parts(bank[:], WIDTHS[c])]
+
+        def clamp(b, drivers, planes):
+            for t in range(PACK):
+                vector.tensor_scalar(
+                    planes[:, t, :], drivers[t], lo_cols[:, b, t : t + 1], hi_cols[:, b, t : t + 1], MAX, MIN
+                )
+
+        def clamp_on_gpsimd(b, drivers, planes):
+            for t in range(PACK):
+                gpsimd.tensor_scalar(
+                    planes[:, t, :], drivers[t], hi_cols[:, b, t : t + 1], lo_cols[:, b, t : t + 1], MIN, MAX
+                )
+
+        y_banks = {}
+
+        h_codes = {}
+
+        def quantize_h(c, b, values, codes):
+            h_codes[c, b] = (codes, quantize(values, codes, "h_scales%d%d" % (c, b)))
+
+        def y_passes(c, b, tiles=range(N_TILES)):
+            codes, scales = h_codes[c, b]
+            for n in tiles:
+                cols = slice(n * P, (n + 1) * P)
+                for bank, column, count, first in pieces(n, WIDTHS[c]):
+                    if b == 0 and column == 0:
+                        y_banks[c, bank] = bank_tile("y%d%d" % (c, bank), Y_BANKS[c][bank])
+                    ends = column + count == BANK or (n == N_TILES - 1 and first + count == WIDTHS[c])
+                    nc.tensor.matmul_mx(
+                        out=y_banks[c, bank][:, column : column + count],
+                        lhsT=wr_codes[:, b, cols].bitcast(FP8X4),
+                        lhsT_scale=wr_planes[4 * b : P, cols],
+                        rhs=codes[:, first : first + count].bitcast(FP8X4),
+                        rhs_scale=scales[:, first : first + count],
+                        start=(b == 0 and column == 0),
+                        stop=(b == PASSES - 1 and ends),
+                    )
+
+        def finish_bank(c, k, tag):
+            factors = parts(slopes[c], BANK)[k]
+            w = WIDTHS[c]
+            result = place(F32, factors.shape[1], tag)
+            vector.tensor_tensor(result, y_banks[c, k][:, 0 : factors.shape[1]], factors, MULT)
+            first = k * BANK // w
+            rows = out[first * P : (first + factors.shape[1] // w) * P, STARTS[c] : STARTS[c] + w]
+            nc.sync.dma_start(out=rows.rearrange("(n p) j -> p n j", p=P), in_=result.rearrange("p (n j) -> p n j", j=w))
 
         nc.sync.dma_start(fuel_list[:], offs)
         load_rows(tab_bytes, tab_scales)
@@ -105,13 +296,13 @@ def tile_list_wildfire_spread_rates_kernel(
         nc.sync.dma_start(upwind_list[:], offs2)
         nc.sync.dma_start(downwind_list[:], offs3)
         load_rows(wf_raw_scales, wf_scales)
-        nc.vector.tensor_copy(v_rows[:], tab_bytes[:].indirect(fuel_list[:]))
-        nc.gpsimd.tensor_copy(
+        vector.tensor_copy(v_rows[:], tab_bytes[:].indirect(fuel_list[:]))
+        gpsimd.tensor_copy(
             out=wf_rows[:].rearrange("p (b t m) -> p b t m", t=PACK, m=P),
             in_=wf_raw_scales[:].rearrange("p (b m t) -> p b t m", t=PACK, m=P),
         )
-        for a in range(PASSES):
-            nc.sync.dma_start(out=wf_raw[a][:].bitcast(I32), in_=wf_words[a].bitcast(I32))
+        for a in both:
+            nc.sync.dma_start(out=wf_raw[a].bitcast(I32), in_=wf_words[a].bitcast(I32))
         load_x_plane(1)
         load_wx(0, 0)
         load_x_plane(2)
@@ -129,337 +320,130 @@ def tile_list_wildfire_spread_rates_kernel(
         spread_rows(v_planes, v_rows)
         nc.sync.dma_start(out=lo_cols[:], in_=lo.rearrange("(b p t) -> p b t", b=PASSES, t=PACK))
         nc.sync.dma_start(out=hi_cols[:], in_=hi.rearrange("(b p t) -> p b t", b=PASSES, t=PACK))
-        nc.sync.dma_start(
-            out=wr_codes[:].bitcast(I32), in_=wr_words.rearrange("a p c i -> p a (c i)").bitcast(I32)
-        )
+        nc.sync.dma_start(out=wr_codes[:].bitcast(I32), in_=wr_words.rearrange("a p c i -> p a (c i)").bitcast(I32))
         load_scale_rows(wr_planes, wr_scales)
 
-        wx_codes = {}
-        wx_scales = {}
-        wx_grouped = {}
-
-        def cast_wx(a, b):
-            grouped = work.tile([P, PACK * K_PASS], BF16, name="wx_bf%d%d" % (a, b), tag=("wx_bf%d", "sums%d")[a] % b, align_bytes=64)
-            src = wx_raw[a][:].rearrange("p (i c) -> p i c", i=PACK)[:, :, b * K_PASS : (b + 1) * K_PASS]
-            nc.scalar.copy(
-                out=grouped[:].rearrange("p (t m i) -> p m t i", t=PACK, i=PACK),
-                in_=src.rearrange("p i (m t) -> p m t i", t=PACK),
-            )
-            wx_grouped[a, b] = grouped
-
-        def quantize_wx(a, b, codes):
-            wx_codes[a, b] = codes
-            wx_scales[a, b] = keep.tile([P, K_PASS], U8, name="wx_scales%d%d" % (a, b), align_bytes=64)
-            nc.vector.quantize_mx(
-                out=codes.bitcast(FP8X4), scales=wx_scales[a, b][:], in_=wx_grouped[a, b][:]
-            )
-
-        wf_codes = {}
-
-        def reorder_wf(a, tag):
-            ordered = work.tile([P, 2 * H], U8, name="wf_codes%d" % a, tag=tag, align_bytes=64)
-            for b in range(PASSES):
-                wf_codes[a, b] = ordered[:, 2 * b * K_PASS : 2 * (b + 1) * K_PASS]
-                col = b * K_PASS
-                nc.gpsimd.tensor_copy(
-                    out=wf_codes[a, b].rearrange("p (t m e) -> p t m e", t=PACK, e=2),
-                    in_=wf_raw[a][:, 2 * col : 2 * (col + K_PASS)].rearrange("p (m t e) -> p t m e", t=PACK, e=2),
-                )
-
-        for a in range(PASSES):
-            reorder_wf(a, "wf_codes%d" % a)
-
-        def list_cols(first, width):
-            return slice(first // LIST_ROWS, (first + width) // LIST_ROWS)
-
-        def pick_upwind(i, first, upwind):
-            cols = list_cols(first, upwind.shape[1])
-            nc.vector.tensor_copy(upwind, x_planes[i][:].indirect(upwind_list[:, cols]))
-
-        def add_downwind(i, first, upwind, total):
-            cols = list_cols(first, upwind.shape[1])
-            nc.vector.tensor_tensor(total, x_planes[i][:].indirect(downwind_list[:, cols]), upwind, ADD)
-
-        def gather_halves(i, spares, sums):
-            width = spares[0].shape[1]
-            for u in range(2):
-                pick_upwind(i, u * width, spares[u])
-            for u in range(2):
-                add_downwind(i, u * width, spares[u], sums[u])
-
-        def interleave(copy, dst, src):
-            copy(
-                out=dst.rearrange("p (c i t) -> p c t i", i=PACK, t=PACK), in_=src.rearrange("p t (c i) -> p c t i", i=PACK)
-            )
-
-        first_sums = [work.tile([P, PACK, BANK], F32, name="first_sums%d" % u, tag="sums%d" % u, align_bytes=64) for u in range(2)]
-        first_mixed = [
-            work.tile([P, PACK * BANK], BF16, name="first_mixed%d" % u, tag="mixed%d" % u, align_bytes=64) for u in range(2)
-        ]
-        x_codes = {}
-        x_scales = {}
-
-        def gather_first(t):
-            upwind = floats(S, "upwind%d" % (t % 3))
-            downwind = floats(S, "downwind%d" % (t % 3))
-            nc.vector.tensor_copy(upwind, x_planes[t][:].indirect(upwind_list[:]))
-            nc.vector.tensor_copy(downwind, x_planes[t][:].indirect(downwind_list[:]))
+        for a in both:
+            reorder_wf(a)
+        first_sums = [by_plane(place(F32, PACK * BANK, "sums%d" % u)) for u in range(2)]
+        for t in range(PACK):
+            upwind = place(F32, S, "upwind%d" % (t % 3))
+            downwind = place(F32, S, "downwind%d" % (t % 3))
+            pick(t, upwind_list, 0, upwind)
+            pick(t, downwind_list, 0, downwind)
             for u in range(2):
                 cols = slice(u * BANK, (u + 1) * BANK)
-                nc.gpsimd.tensor_tensor(first_sums[u][:, t, :], upwind[:, cols], downwind[:, cols], ADD)
-
-        def quantize_first(c, codes):
-            u, first = divmod(STARTS[c], BANK)
-            x_codes[c, 0] = codes
-            x_scales[c, 0] = keep.tile([P, WIDTHS[c]], U8, name="first_scales%d" % c, align_bytes=64)[:]
-            values = first_mixed[u][:, PACK * first : PACK * (first + WIDTHS[c])]
-            nc.vector.quantize_mx(out=codes.bitcast(FP8X4), scales=x_scales[c, 0], in_=values)
-
-        def gather_v(a, first, picks):
-            width = picks.shape[1]
-            nc.vector.tensor_copy(picks, tab_codes[a][:].indirect(fuel_list[:, list_cols(first, width)]))
-            for j in range(0, width, BANK):
-                v_codes[a, (first + j) // BANK] = picks[:, j : j + BANK]
-
-        x_mixed = {}
-
-        def interleave_shared(copies, dst, src):
-            w = src.shape[2] // len(copies)
-            for u, copy in enumerate(copies):
-                interleave(copy, dst[:, PACK * u * w : PACK * (u + 1) * w], src[:, :, u * w : (u + 1) * w])
-
-        def mix_x(c, sums, copies, tag):
-            x_mixed[c] = work.tile([P, PACK * WIDTHS[c]], BF16, name="x_mixed%d" % c, tag=tag, align_bytes=64)
-            interleave_shared(copies, x_mixed[c][:], sums)
-
-        def quantize_x(c):
-            x_codes[c, 1] = work.tile([P, WIDTHS[c]], U32, name="x_codes%d" % c, tag="x_codes%d" % c, align_bytes=64)[:]
-            x_scales[c, 1] = work.tile([P, WIDTHS[c]], U8, name="x_scales%d" % c, tag="x_scales%d" % c, align_bytes=64)[:]
-            nc.vector.quantize_mx(out=x_codes[c, 1].bitcast(FP8X4), scales=x_scales[c, 1], in_=x_mixed[c][:])
-
-        d_banks = {}
-
-        def d_view(c, b, t):
-            w = WIDTHS[c]
-            k, u = divmod(t, BANK // w)
-            return d_banks[c, b, k][:, u * w : (u + 1) * w]
-
-        def x_pass(c, b, t, a):
-            per_bank = BANK // WIDTHS[c]
-            cols = slice(t * P, (t + 1) * P)
-            nc.tensor.matmul_mx(
-                out=d_view(c, b, t),
-                lhsT=wx_codes[a, b][:, cols].bitcast(FP8X4),
-                lhsT_scale=wx_scales[a, b][:, cols],
-                rhs=x_codes[c, a].bitcast(FP8X4),
-                rhs_scale=x_scales[c, a],
-                start=(a == 0 and t % per_bank == 0),
-                stop=(a == PASSES - 1 and t % per_bank == per_bank - 1),
-            )
-
-        def fuel_pass(c, b, t, a):
-            step = BANK if WIDTHS[c] == BANK else FP4_WIDTH
-            col = a * H + b * K_PASS + t * P
-            for j in range(0, WIDTHS[c], step):
-                first = STARTS[c] + j
-                nc.tensor.matmul_mx(
-                    out=d_view(c, b, t)[:, j : j + step],
-                    lhsT=wf_codes[a, b][:, 2 * t * P : 2 * (t + 1) * P].bitcast(FP4X4),
-                    lhsT_scale=wf_planes[:, col : col + P],
-                    rhs=v_codes[a, first // BANK][:, first % BANK : first % BANK + step].bitcast(FP8X4),
-                    rhs_scale=v_planes[:, a * S + first : a * S + first + step],
-                    start=False,
-                    stop=False,
-                )
-
-        def open_d(c, order):
-            for b in order:
-                for k, number in enumerate(D_BANKS[c, b]):
-                    d_banks[c, b, k] = psum.tile([P, BANK], F32, name="d%d%d%d" % (c, b, k), tag="bank%d" % number)
-                for t in range(PACK):
-                    x_pass(c, b, t, 0)
-            for a in range(PASSES):
-                for b in order:
-                    for t in range(PACK):
-                        fuel_pass(c, b, t, a)
-
-        def close_d(c, order):
-            for b in order:
-                for t in range(PACK):
-                    x_pass(c, b, t, 1)
-
-        def evacuate_d(c, b, place):
-            per_bank = BANK // WIDTHS[c]
-            for k in range(len(D_BANKS[c, b])):
-                sums = d_banks[c, b, k][:].rearrange("p (t j) -> p t j", t=per_bank)
-                nc.scalar.copy(out=place[:, k * per_bank : (k + 1) * per_bank, :], in_=sums)
-
-        h_mixed = {}
-
-        def halfwords(width, tag):
-            return work.tile([P, width], BF16, name="halfwords_" + tag, tag=tag, align_bytes=64)[:]
-
-        def by_plane(place):
-            return place.rearrange("p (t j) -> p t j", t=PACK)
-
-        def clamp(b, drivers, planes):
-            for t in range(PACK):
-                nc.vector.tensor_scalar(
-                    planes[:, t, :], drivers[t], lo_cols[:, b, t : t + 1], hi_cols[:, b, t : t + 1], MAX, MIN
-                )
-
-        def clamp_from_psum(c, b, planes):
-            for t in range(PACK):
-                high = hi_cols[:, b, t : t + 1].to_broadcast([P, WIDTHS[c]])
-                nc.vector.scalar_tensor_tensor(planes[:, t, :], d_view(c, b, t), lo_cols[:, b, t : t + 1], high, MAX, MIN)
-
-        def mix_h(c, b, planes, tag):
-            h_mixed[c, b] = work.tile(
-                [P, PACK * WIDTHS[c]], BF16, name="h_mixed%d%d" % (c, b), tag=tag, align_bytes=64
-            )
-            interleave(nc.scalar.copy, h_mixed[c, b][:], planes)
-
-        y_banks = {}
-
-        def quantize_h(c, b, codes):
-            scales = keep.tile([P, WIDTHS[c]], U8, name="h_scales%d%d" % (c, b), align_bytes=64)
-            nc.vector.quantize_mx(out=codes.bitcast(FP8X4), scales=scales[:], in_=h_mixed[c, b][:])
-            return scales
-
-        def quantize_h_and_multiply(c, b, codes):
-            multiply_h(c, b, codes, quantize_h(c, b, codes))
-
-        def multiply_h(c, b, codes, scales):
-            w = WIDTHS[c]
-            per_bank = BANK // w
-            for n in range(N_TILES):
-                k, u = divmod(n, per_bank)
-                if b == 0 and u == 0:
-                    y_banks[c, k] = psum.tile([P, BANK], F32, name="y%d%d" % (c, k), tag="bank%d" % Y_BANKS[c][k])
-                cols = slice(n * P, (n + 1) * P)
-                nc.tensor.matmul_mx(
-                    out=y_banks[c, k][:, u * w : (u + 1) * w],
-                    lhsT=wr_codes[:, b, cols].bitcast(FP8X4),
-                    lhsT_scale=wr_planes[4 * b : P, cols],
-                    rhs=codes.bitcast(FP8X4),
-                    rhs_scale=scales[:],
-                    start=(b == 0 and u == 0),
-                    stop=(b == PASSES - 1 and (u == per_bank - 1 or n == N_TILES - 1)),
-                )
-
-        def finish(c, places):
-            w = WIDTHS[c]
-            per_bank = BANK // w
-            cols = slice(STARTS[c], STARTS[c] + w)
-            for k in range(len(Y_BANKS[c])):
-                tiles = slice(k * per_bank, min((k + 1) * per_bank, N_TILES))
-                count = tiles.stop - tiles.start
-                result = places[k][:, 0 : count * w].rearrange("p (n j) -> p n j", n=count)
-                sums = y_banks[c, k][:, 0 : count * w].rearrange("p (n j) -> p n j", n=count)
-                nc.vector.tensor_tensor(result, sums, slope_cols[:, tiles, cols], MULT)
-                rows = out[tiles.start * P : tiles.stop * P, cols]
-                nc.sync.dma_start(out=rows.rearrange("(n p) j -> p n j", p=P), in_=result)
-
-        def floats(width, tag):
-            return work.tile([P, width], F32, name="floats_" + tag, tag=tag, align_bytes=64)[:]
-
-        def words(width, tag):
-            return work.tile([P, width], U32, name="words_" + tag, tag=tag, align_bytes=64)[:]
-
-        def parts(place, width):
-            return [place[:, j : j + width] for j in range(0, place.shape[1], width)]
-
-        def as_floats(planes):
-            return planes[:].rearrange("p t j -> p (t j)").bitcast(F32)
-
-        both = range(PASSES)
-        vector, gpsimd, scalar = nc.vector, nc.gpsimd, nc.scalar
-        for t in range(PACK):
-            gather_first(t)
-        cast_wx(0, 0)
-        cast_wx(0, 1)
-        slope_cols = work.tile([P, N_TILES, S], F32, name="slope_cols", tag="wide0", align_bytes=64)
-        nc.sync.dma_start(out=slope_cols[:], in_=slope.rearrange("(n p) j -> p n j", p=P))
+                gpsimd.tensor_tensor(first_sums[u][:, t, :], upwind[:, cols], downwind[:, cols], ADD)
+        for c in range(len(WIDTHS)):
+            load_slope(c, ("plane0", "plane1", "slope2")[c])
+        cast_wx(0, 0, "wx_bf0")
+        cast_wx(0, 1, "wx_bf1")
+        first_mixed = [place(BF16, PACK * BANK, "mixed%d" % u) for u in range(2)]
         for u in range(2):
-            interleave(scalar.copy, first_mixed[u][:], first_sums[u][:])
-        gather_v(0, 0, words(S, "v_first"))
+            interleave(first_mixed[u], first_sums[u])
+        gather_v(0, 0, place(U32, BANK, "v_first"))
 
-        wide_sums = work.tile([P, PACK, BANK], F32, name="wide_sums", tag="wide_sums", align_bytes=64)
-        chain = floats(NARROW, "chain")
-        gather_halves(4, [floats(NARROW, "plane4a"), chain], parts(wide_sums[:, 0, :], NARROW))
-        for b, codes in enumerate(parts(words(2 * K_PASS, "plane4a"), K_PASS)):
-            quantize_wx(0, b, codes)
-        gather_halves(5, [floats(NARROW, "plane5a"), chain], parts(wide_sums[:, 1, :], NARROW))
-        quantize_first(0, words(BANK, "plane5a"))
-        cast_wx(1, 0)
-        cast_wx(1, 1)
-        d_store = floats(PACK * (2 * BANK + NARROW), "wide1")
-        d_first = by_plane(d_store[:, 0 : PACK * BANK])
-        d_second = by_plane(d_store[:, PACK * BANK : PACK * (2 * BANK + NARROW)])
-        gather_halves(6, [floats(NARROW, "plane6a"), chain], parts(wide_sums[:, 2, :], NARROW))
-        after_six = words(K_PASS + NARROW, "plane6a")
-        quantize_first(1, after_six[:, K_PASS : K_PASS + NARROW])
-        quantize_wx(1, 0, after_six[:, 0:K_PASS])
-        gather_v(1, 0, words(BANK, "chain"))
-        gather_halves(7, [floats(NARROW, "plane7a"), floats(NARROW, "plane7b")], parts(wide_sums[:, 3, :], NARROW))
-        quantize_wx(1, 1, words(K_PASS, "plane7a"))
-        open_d(0, both)
-        mix_x(0, wide_sums[:], [scalar.copy], "upwind2")
-        waiting = parts(floats(PACK * NARROW, "plane7b"), NARROW)
-        for t in range(PACK):
-            pick_upwind(PACK + t, STARTS[1], waiting[t])
-        quantize_x(0)
-        close_d(0, both)
-        narrow_sums = wide_sums[:, :, 0:NARROW]
-        for t in range(PACK):
-            add_downwind(PACK + t, STARTS[1], waiting[t], narrow_sums[:, t, :])
-        gather_v(1, BANK, words(BANK, "upwind2"))
-        evacuate_d(0, 0, d_first)
-        evacuate_d(0, 1, d_second[:, :, 0:BANK])
-        open_d(1, both)
-        mix_x(1, narrow_sums, [scalar.copy], "x_codes0")
-        planes = by_plane(halfwords(PACK * BANK, "plane7b"))
-        clamp(0, [d_first[:, t, :] for t in range(PACK)], planes)
-        mix_h(0, 0, planes, "x_scales0")
-        late_picks = d_store[:, BANK : PACK * BANK]
-        waiting = [by_plane(late_picks)[:, t, 0:NARROW] for t in range(PACK)]
-        for t in reversed(range(PACK)):
-            pick_upwind(PACK + t, STARTS[2], waiting[t])
-        quantize_x(1)
-        close_d(1, (1, 0))
-        quantize_first(2, words(NARROW, "x_codes0"))
-        open_d(2, both)
-        for t in range(PACK):
-            add_downwind(PACK + t, STARTS[2], waiting[t], narrow_sums[:, t, :])
-        evacuate_d(1, 1, d_second[:, :, BANK : BANK + NARROW])
-        d_narrow = by_plane(floats(PACK * NARROW, "mixed0"))
-        evacuate_d(1, 0, d_narrow)
-        mix_x(2, narrow_sums, [scalar.copy], "x_codes1")
-        planes = by_plane(late_picks.bitcast(BF16))
-        clamp(1, [d_second[:, t, :] for t in range(PACK)], planes)
-        mix_h(0, 1, planes[:, :, 0:BANK], "sums0")
-        held_planes = planes[:, :, BANK : BANK + NARROW]
-        quantize_x(2)
-        close_d(2, both)
-        quantize_h_and_multiply(0, 0, words(BANK, "wide_sums"))
-        planes = by_plane(halfwords(PACK * NARROW, "x_codes1"))
-        clamp(0, [d_narrow[:, t, :] for t in range(PACK)], planes)
-        mix_h(1, 0, planes, "x_scales0")
-        h_mixed[1, 1] = work.tile([P, PACK * NARROW], BF16, name="h_mixed11", tag="mixed0", align_bytes=64)
-        nc.gpsimd.tensor_scalar(
-            h_mixed[1, 1][:].rearrange("p (j t) -> p j t", t=PACK), held_planes.rearrange("p t j -> p j t"), 1.0, 0.0, MULT, ADD
-        )
+        wide_sums = [by_plane(place(F32, PACK * HALF, "plane%d" % (2 + u))) for u in range(2)]
+        chain = place(F32, HALF, "chain")
+        middle_picks = parts(place(F32, 3 * HALF, "middle_picks"), HALF)
+        gather_halves(4, [place(F32, HALF, "pick4"), chain], [half[:, 0, :] for half in wide_sums], middle_picks[0])
+        quantize_wx(0, 0, place(U32, K_PASS, "pick4"))
+        gather_halves(5, [place(F32, HALF, "pick5"), chain], [half[:, 1, :] for half in wide_sums], middle_picks[1])
+        quantize_x(0, 0, first_mixed[0], place(U32, BANK, "pick5"))
+        x_passes(WIDE, 0, 0)
         for b in both:
-            planes = by_plane(halfwords(PACK * NARROW, ("upwind0", "sums1")[b]))
-            clamp_from_psum(2, b, planes)
-            mix_h(2, b, planes, ("mixed1", "plane7b")[b])
-        late_codes = words(BANK + 4 * NARROW, "x_codes2")
-        quantize_h_and_multiply(0, 1, late_codes[:, 0:BANK])
-        h_codes = parts(late_codes[:, BANK : BANK + 4 * NARROW], NARROW)
-        for c in (1, 2):
-            for b in both:
-                quantize_h_and_multiply(c, b, h_codes[2 * (c - 1) + b])
-        results = parts(floats(4 * BANK, "sums1"), BANK)
-        finish(0, [floats(BANK, "upwind0")] + results[0:2])
-        finish(1, results[2:4])
-        finish(2, parts(floats(2 * BANK, "downwind1"), BANK))
+            cast_wx(1, b, "sums%d" % b)
+        gather_halves(6, [place(F32, HALF, "pick6"), chain], [half[:, 2, :] for half in wide_sums], middle_picks[2])
+        quantize_wx(0, 1, place(U32, K_PASS, "pick6"))
+        x_passes(WIDE, 1, 0)
+        gather_v(1, 0, place(U32, BANK, "chain"))
+        spares = [place(F32, HALF, "pick7"), place(F32, HALF, "pick8")]
+        gather_halves(7, spares, [half[:, 3, :] for half in wide_sums])
+        wide_mixed = place(BF16, PACK * BANK, "upwind2")
+        for u in range(2):
+            interleave(parts(wide_mixed, PACK * HALF)[u], wide_sums[u])
+        middle_picks.append(place(F32, HALF, "pick7"))
+        pick(2 * PACK - 1, upwind_list, STARTS[MIDDLE], middle_picks[3])
+        quantize_x(0, BANK, first_mixed[1], place(U32, BANK, "pick8"))
+        for b, codes in enumerate(parts(place(U32, 2 * K_PASS, "plane2"), K_PASS)):
+            quantize_wx(1, b, codes)
+        for a in both:
+            fuel_passes(WIDE, 0, a)
+        fuel_passes(WIDE, 1, 0)
+        quantize_x(1, 0, wide_mixed, place(U32, BANK, "mixed1"))
+        x_passes(WIDE, 0, 1, closing=True)
+        x_passes(WIDE, 1, 1)
+        fuel_passes(WIDE, 1, 1, closing=True)
+        wide_d = [place(F32, PACK * BANK, "wx_raw0%d" % b) for b in both]
+        for b in both:
+            evacuate(d_banks[WIDE, b], wide_d[b])
+        first_planes = by_plane(place(F32, PACK * BANK, "wx_raw10"))
+        clamp_on_gpsimd(0, parts(wide_d[0], BANK), first_planes)
+        for a, picks in enumerate(parts(place(U32, 2 * BANK, "upwind2"), BANK)):
+            gather_v(a, BANK, picks)
+        for b in both:
+            x_passes(MIDDLE, b, 0)
+            for a in both:
+                fuel_passes(MIDDLE, b, a)
+        last_picks = [wide_sums[1][:, t, :] for t in range(PACK - 1)] + [place(F32, HALF, "tab0")]
+        for t in range(PACK):
+            pick(PACK + t, upwind_list, STARTS[LAST], last_picks[t])
+        shared = place(F32, (2 + PACK) * HALF, "wx_raw00")
+        middle_sums = by_plane(shared[:, 2 * HALF : (2 + PACK) * HALF])
+        last_sums = by_plane(shared[:, 0 : PACK * HALF])
+        for t in range(PACK):
+            add_downwind(PACK + t, STARTS[MIDDLE], middle_picks[t], middle_sums[:, t, :])
+        wide_h = [place(BF16, PACK * BANK, "downwind%d" % b) for b in both]
+        interleave(wide_h[0], first_planes)
+        middle_mixed = place(BF16, PACK * HALF, "wx_bf0")
+        interleave(middle_mixed, middle_sums)
+        h_planes = by_plane(place(BF16, PACK * BANK, "middle_picks"))
+        clamp(1, parts(wide_d[1], BANK), h_planes)
+        interleave(wide_h[1], h_planes)
+        for t in range(2):
+            add_downwind(PACK + t, STARTS[LAST], last_picks[t], last_sums[:, t, :])
+        quantize_x(1, STARTS[MIDDLE], middle_mixed, place(U32, HALF, "x_middle"))
+        for b in both:
+            x_passes(MIDDLE, b, 1, closing=True)
+        for b in both:
+            x_passes(LAST, b, 0)
+            for a in both:
+                fuel_passes(LAST, b, a)
+        for t in range(2, PACK):
+            add_downwind(PACK + t, STARTS[LAST], last_picks[t], last_sums[:, t, :])
+        middle_planes = [by_plane(place(BF16, PACK * HALF, "sums%d" % b)) for b in both]
+        clamp(0, in_banks(MIDDLE, 0), middle_planes[0])
+        wide_codes = parts(place(U32, 2 * BANK, "plane3"), BANK)
+        for b in both:
+            quantize_h(WIDE, b, wide_h[b], wide_codes[b])
+        last_mixed = place(BF16, PACK * HALF, "wx_bf0")
+        interleave(last_mixed, last_sums)
+        middle_d = place(F32, PACK * HALF, "upwind1")
+        evacuate(d_banks[MIDDLE, 1], middle_d)
+        for b in both:
+            y_passes(WIDE, b, range(2))
+        quantize_x(1, STARTS[LAST], last_mixed, place(U32, HALF, "x_last"))
+        for b in both:
+            x_passes(LAST, b, 1, closing=True)
+        for b in both:
+            y_passes(WIDE, b, range(2, N_TILES))
+        finish_bank(WIDE, 0, "wx_raw00")
+        clamp(1, parts(middle_d, HALF), middle_planes[1])
+        middle_h = [place(BF16, PACK * HALF, tag) for tag in ("wx_bf1", "downwind2")]
+        for b in both:
+            interleave(middle_h[b], middle_planes[b])
+        last_h = [place(BF16, PACK * HALF, tag) for tag in ("wx_raw11", "wx_raw01")]
+        late_codes = parts(place(U32, 4 * HALF, "tab1"), HALF)
+        for b in both:
+            h_planes = by_plane(place(BF16, PACK * HALF, "upwind%d" % b))
+            clamp(b, in_banks(LAST, b), h_planes)
+            interleave(last_h[b], h_planes)
+            quantize_h(MIDDLE, b, middle_h[b], late_codes[b])
+            y_passes(MIDDLE, b)
+        for b in both:
+            finish_bank(WIDE, 1 + b, ("wx_bf1", "downwind2")[b])
+            quantize_h(LAST, b, last_h[b], late_codes[2 + b])
+            y_passes(LAST, b)
+        for c in (MIDDLE, LAST):
+            for k in range(2):
+                finish_bank(c, k, "plane%d" % (2 * c + 2 + k))

@@ -206,10 +206,10 @@ def tile_list_wildfire_spread_rates_kernel(
         def bank_tile(name, number):
             return psum.tile([P, BANK], F32, name=name, tag="bank%d" % number)
 
-        def x_passes(c, b, a, closing=False):
+        def x_passes(c, b, a, closing=False, slots=range(PACK)):
             if a == 0:
                 d_banks[c, b] = [bank_tile("d%d%d%d" % (c, b, n), n) for n in D_BANKS[c, b]]
-            for t in range(PACK):
+            for t in slots:
                 cols = slice(t * P, (t + 1) * P)
                 for bank, column, count, first in pieces(t, WIDTHS[c]):
                     nc.tensor.matmul_mx(
@@ -222,8 +222,8 @@ def tile_list_wildfire_spread_rates_kernel(
                         stop=(closing and column + count == BANK),
                     )
 
-        def fuel_passes(c, b, a, closing=False):
-            for t in range(PACK):
+        def fuel_passes(c, b, a, closing=False, slots=range(PACK)):
+            for t in slots:
                 col = a * H + b * K_PASS + t * P
                 for bank, column, count, first in pieces(t, WIDTHS[c]):
                     entry = a * S + STARTS[c] + first
@@ -244,17 +244,13 @@ def tile_list_wildfire_spread_rates_kernel(
         def in_banks(c, b):
             return [part for bank in d_banks[c, b] for part in parts(bank[:], WIDTHS[c])]
 
-        def clamp(b, drivers, planes):
-            for t in range(PACK):
-                vector.tensor_scalar(
-                    planes[:, t, :], drivers[t], lo_cols[:, b, t : t + 1], hi_cols[:, b, t : t + 1], MAX, MIN
-                )
-
-        def clamp_on_gpsimd(b, drivers, planes):
-            for t in range(PACK):
-                gpsimd.tensor_scalar(
-                    planes[:, t, :], drivers[t], hi_cols[:, b, t : t + 1], lo_cols[:, b, t : t + 1], MIN, MAX
-                )
+        def clamp(engine, b, drivers, planes, slots=range(PACK)):
+            for t in slots:
+                low, high = lo_cols[:, b, t : t + 1], hi_cols[:, b, t : t + 1]
+                if engine is vector:
+                    vector.tensor_scalar(planes[:, t, :], drivers[t], low, high, MAX, MIN)
+                else:
+                    engine.tensor_scalar(planes[:, t, :], drivers[t], high, low, MIN, MAX)
 
         y_banks = {}
 
@@ -345,61 +341,75 @@ def tile_list_wildfire_spread_rates_kernel(
 
         wide_sums = [by_plane(place(F32, PACK * HALF, "plane%d" % (2 + u))) for u in range(2)]
         chain = place(F32, HALF, "chain")
-        middle_picks = parts(place(F32, 3 * HALF, "middle_picks"), HALF)
+        middle_picks = {0: place(F32, HALF, "middle_picks")}
         gather_halves(4, [place(F32, HALF, "pick4"), chain], [half[:, 0, :] for half in wide_sums], middle_picks[0])
         quantize_wx(0, 0, place(U32, K_PASS, "pick4"))
-        gather_halves(5, [place(F32, HALF, "pick5"), chain], [half[:, 1, :] for half in wide_sums], middle_picks[1])
-        quantize_x(0, 0, first_mixed[0], place(U32, BANK, "pick5"))
-        x_passes(WIDE, 0, 0)
+        gather_halves(5, [place(F32, HALF, "pick5"), chain], [half[:, 1, :] for half in wide_sums])
+        quantize_wx(0, 1, place(U32, K_PASS, "pick5"))
+        last_picks = [place(F32, HALF, "early_pick")]
+        pick(PACK, upwind_list, STARTS[LAST], last_picks[0])
         for b in both:
             cast_wx(1, b, "sums%d" % b)
-        gather_halves(6, [place(F32, HALF, "pick6"), chain], [half[:, 2, :] for half in wide_sums], middle_picks[2])
-        quantize_wx(0, 1, place(U32, K_PASS, "pick6"))
-        x_passes(WIDE, 1, 0)
+        gather_halves(6, [place(F32, HALF, "pick6"), chain], [half[:, 2, :] for half in wide_sums])
+        quantize_x(0, 0, first_mixed[0], place(U32, BANK, "pick6"))
+        for b in both:
+            x_passes(WIDE, b, 0)
         gather_v(1, 0, place(U32, BANK, "chain"))
         spares = [place(F32, HALF, "pick7"), place(F32, HALF, "pick8")]
         gather_halves(7, spares, [half[:, 3, :] for half in wide_sums])
         wide_mixed = place(BF16, PACK * BANK, "upwind2")
         for u in range(2):
             interleave(parts(wide_mixed, PACK * HALF)[u], wide_sums[u])
-        middle_picks.append(place(F32, HALF, "pick7"))
-        pick(2 * PACK - 1, upwind_list, STARTS[MIDDLE], middle_picks[3])
+        middle_picks.update({1: place(F32, HALF, "pick7")})
+        pick(PACK + 1, upwind_list, STARTS[MIDDLE], middle_picks[1])
         quantize_x(0, BANK, first_mixed[1], place(U32, BANK, "pick8"))
         for b, codes in enumerate(parts(place(U32, 2 * K_PASS, "plane2"), K_PASS)):
             quantize_wx(1, b, codes)
         for a in both:
             fuel_passes(WIDE, 0, a)
-        fuel_passes(WIDE, 1, 0)
+        fuel_passes(WIDE, 1, 0, slots=range(2))
         quantize_x(1, 0, wide_mixed, place(U32, BANK, "mixed1"))
         x_passes(WIDE, 0, 1, closing=True)
-        x_passes(WIDE, 1, 1)
-        fuel_passes(WIDE, 1, 1, closing=True)
-        wide_d = [place(F32, PACK * BANK, "wx_raw0%d" % b) for b in both]
-        for b in both:
-            evacuate(d_banks[WIDE, b], wide_d[b])
+        for t in range(PACK):
+            if t >= 2:
+                fuel_passes(WIDE, 1, 0, slots=[t])
+            x_passes(WIDE, 1, 1, slots=[t])
+            fuel_passes(WIDE, 1, 1, closing=True, slots=[t])
+        shared = place(F32, (2 + PACK) * HALF, "plane3")
+        middle_sums = by_plane(shared[:, 2 * HALF : (2 + PACK) * HALF])
+        last_sums = by_plane(shared[:, 0 : PACK * HALF])
+        for t in range(2):
+            add_downwind(PACK + t, STARTS[MIDDLE], middle_picks[t], middle_sums[:, t, :])
+        first_d = parts(place(F32, PACK * BANK, "wx_raw00"), BANK)
+        second_d = [shared[:, 2 * BANK : 3 * BANK], shared[:, 0:BANK]] + parts(place(F32, 2 * BANK, "wx_raw01"), BANK)
+        for b, drivers in enumerate((first_d, second_d)):
+            for t in range(PACK):
+                scalar.copy(out=drivers[t], in_=d_banks[WIDE, b][t][:])
         first_planes = by_plane(place(F32, PACK * BANK, "wx_raw10"))
-        clamp_on_gpsimd(0, parts(wide_d[0], BANK), first_planes)
+        second_store = place(F32, PACK * BANK, "middle_picks")
+        second_planes = by_plane(second_store)
+        clamp(gpsimd, 0, first_d, first_planes)
+        clamp(gpsimd, 1, second_d, second_planes, range(1))
         for a, picks in enumerate(parts(place(U32, 2 * BANK, "upwind2"), BANK)):
             gather_v(a, BANK, picks)
         for b in both:
             x_passes(MIDDLE, b, 0)
             for a in both:
                 fuel_passes(MIDDLE, b, a)
-        last_picks = [wide_sums[1][:, t, :] for t in range(PACK - 1)] + [place(F32, HALF, "tab0")]
-        for t in range(PACK):
+        middle_picks.update({2: second_store[:, 2 * BANK - HALF // 2 : 2 * BANK + HALF // 2], 3: second_planes[:, 3, 0:HALF]})
+        for t in range(2, PACK):
+            pick(PACK + t, upwind_list, STARTS[MIDDLE], middle_picks[t])
+        last_picks = last_picks + parts(place(F32, 2 * HALF, "pick7"), HALF) + [place(F32, HALF, "tab0")]
+        for t in range(1, PACK):
             pick(PACK + t, upwind_list, STARTS[LAST], last_picks[t])
-        shared = place(F32, (2 + PACK) * HALF, "wx_raw00")
-        middle_sums = by_plane(shared[:, 2 * HALF : (2 + PACK) * HALF])
-        last_sums = by_plane(shared[:, 0 : PACK * HALF])
-        for t in range(PACK):
+        for t in range(2, PACK):
             add_downwind(PACK + t, STARTS[MIDDLE], middle_picks[t], middle_sums[:, t, :])
         wide_h = [place(BF16, PACK * BANK, "downwind%d" % b) for b in both]
         interleave(wide_h[0], first_planes)
         middle_mixed = place(BF16, PACK * HALF, "wx_bf0")
         interleave(middle_mixed, middle_sums)
-        h_planes = by_plane(place(BF16, PACK * BANK, "middle_picks"))
-        clamp(1, parts(wide_d[1], BANK), h_planes)
-        interleave(wide_h[1], h_planes)
+        clamp(vector, 1, second_d, second_planes, range(1, PACK))
+        interleave(wide_h[1], second_planes)
         for t in range(2):
             add_downwind(PACK + t, STARTS[LAST], last_picks[t], last_sums[:, t, :])
         quantize_x(1, STARTS[MIDDLE], middle_mixed, place(U32, HALF, "x_middle"))
@@ -412,8 +422,8 @@ def tile_list_wildfire_spread_rates_kernel(
         for t in range(2, PACK):
             add_downwind(PACK + t, STARTS[LAST], last_picks[t], last_sums[:, t, :])
         middle_planes = [by_plane(place(BF16, PACK * HALF, "sums%d" % b)) for b in both]
-        clamp(0, in_banks(MIDDLE, 0), middle_planes[0])
-        wide_codes = parts(place(U32, 2 * BANK, "plane3"), BANK)
+        clamp(vector, 0, in_banks(MIDDLE, 0), middle_planes[0])
+        wide_codes = parts(place(U32, 2 * BANK, "pick7"), BANK)
         for b in both:
             quantize_h(WIDE, b, wide_h[b], wide_codes[b])
         last_mixed = place(BF16, PACK * HALF, "wx_bf0")
@@ -427,8 +437,8 @@ def tile_list_wildfire_spread_rates_kernel(
             x_passes(LAST, b, 1, closing=True)
         for b in both:
             y_passes(WIDE, b, range(2, N_TILES))
-        finish_bank(WIDE, 0, "wx_raw00")
-        clamp(1, parts(middle_d, HALF), middle_planes[1])
+        finish_bank(WIDE, 0, "plane3")
+        clamp(vector, 1, parts(middle_d, HALF), middle_planes[1])
         middle_h = [place(BF16, PACK * HALF, tag) for tag in ("wx_bf1", "downwind2")]
         for b in both:
             interleave(middle_h[b], middle_planes[b])
@@ -436,7 +446,7 @@ def tile_list_wildfire_spread_rates_kernel(
         late_codes = parts(place(U32, 4 * HALF, "tab1"), HALF)
         for b in both:
             h_planes = by_plane(place(BF16, PACK * HALF, "upwind%d" % b))
-            clamp(b, in_banks(LAST, b), h_planes)
+            clamp(vector, b, in_banks(LAST, b), h_planes)
             interleave(last_h[b], h_planes)
             quantize_h(MIDDLE, b, middle_h[b], late_codes[b])
             y_passes(MIDDLE, b)

@@ -89,13 +89,16 @@ def tile_list_wildfire_spread_rates_kernel(
             gpsimd.memset(plane[:].bitcast(I32), 0)
 
         def load_rows(rows, scales):
-            nc.sync.dma_start(out=rows[0:32, :].bitcast(I32), in_=scales.bitcast(I32).rearrange("a q c -> q a c"))
+            for a in both:
+                nc.sync.dma_start(
+                    out=rows[a:32:2, :].bitcast(I32), in_=scales[a].bitcast(I32).rearrange("(q r) c -> r q c", r=4)
+                )
 
         def spread_rows(planes, rows):
-            for q in range(4):
+            for r in range(4):
                 nc.sync.dma_start(
-                    out=planes[32 * q : 32 * q + 4, :].bitcast(I32).rearrange("r (a c) -> r a c", a=PASSES),
-                    in_=rows[8 * q : 8 * q + 8, :].bitcast(I32),
+                    out=planes[r:P:32, :].bitcast(I32).rearrange("q (a c) -> q a c", a=PASSES),
+                    in_=rows[8 * r : 8 * r + 8, :].bitcast(I32),
                 )
 
         def load_scale_rows(plane, scales):

@@ -94,8 +94,8 @@ def tile_list_wildfire_spread_rates_kernel(
                     out=rows[a:32:2, :].bitcast(I32), in_=scales[a].bitcast(I32).rearrange("(q r) c -> r q c", r=4)
                 )
 
-        def spread_rows(planes, rows):
-            for r in range(4):
+        def spread_rows(planes, rows, which=range(4)):
+            for r in which:
                 nc.sync.dma_start(
                     out=planes[r:P:32, :].bitcast(I32).rearrange("q (a c) -> q a c", a=PASSES),
                     in_=rows[8 * r : 8 * r + 8, :].bitcast(I32),
@@ -314,8 +314,9 @@ def tile_list_wildfire_spread_rates_kernel(
         load_wx(1, 1)
         load_x_plane(6)
         load_tab(1)
+        spread_rows(wf_planes, wf_rows, range(1))
         load_x_plane(7)
-        spread_rows(wf_planes, wf_rows)
+        spread_rows(wf_planes, wf_rows, range(1, 4))
         spread_rows(v_planes, v_rows)
         nc.sync.dma_start(out=lo_cols[:], in_=lo.rearrange("(b p t) -> p b t", b=PASSES, t=PACK))
         nc.sync.dma_start(out=hi_cols[:], in_=hi.rearrange("(b p t) -> p b t", b=PASSES, t=PACK))
@@ -348,15 +349,15 @@ def tile_list_wildfire_spread_rates_kernel(
         gather_halves(4, [place(F32, HALF, "pick4"), chain], [half[:, 0, :] for half in wide_sums], middle_picks[0])
         quantize_wx(0, 0, place(U32, K_PASS, "pick4"))
         gather_halves(5, [place(F32, HALF, "pick5"), chain], [half[:, 1, :] for half in wide_sums])
-        quantize_wx(0, 1, place(U32, K_PASS, "pick5"))
+        quantize_x(0, 0, first_mixed[0], place(U32, BANK, "pick5"))
+        x_passes(WIDE, 0, 0)
         last_picks = [place(F32, HALF, "early_pick")]
         pick(PACK, upwind_list, STARTS[LAST], last_picks[0])
         for b in both:
             cast_wx(1, b, "sums%d" % b)
         gather_halves(6, [place(F32, HALF, "pick6"), chain], [half[:, 2, :] for half in wide_sums])
-        quantize_x(0, 0, first_mixed[0], place(U32, BANK, "pick6"))
-        for b in both:
-            x_passes(WIDE, b, 0)
+        quantize_wx(0, 1, place(U32, K_PASS, "pick6"))
+        x_passes(WIDE, 1, 0)
         gather_v(1, 0, place(U32, BANK, "chain"))
         spares = [place(F32, HALF, "pick7"), place(F32, HALF, "pick8")]
         gather_halves(7, spares, [half[:, 3, :] for half in wide_sums])
@@ -370,12 +371,10 @@ def tile_list_wildfire_spread_rates_kernel(
             quantize_wx(1, b, codes)
         for a in both:
             fuel_passes(WIDE, 0, a)
-        fuel_passes(WIDE, 1, 0, slots=range(2))
+        fuel_passes(WIDE, 1, 0)
         quantize_x(1, 0, wide_mixed, place(U32, BANK, "mixed1"))
         x_passes(WIDE, 0, 1, closing=True)
         for t in range(PACK):
-            if t >= 2:
-                fuel_passes(WIDE, 1, 0, slots=[t])
             x_passes(WIDE, 1, 1, slots=[t])
             fuel_passes(WIDE, 1, 1, closing=True, slots=[t])
         shared = place(F32, (2 + PACK) * HALF, "plane3")

@@ -30,7 +30,7 @@ WIDE, MIDDLE, LAST = 0, 1, 2
 LIST_ROWS = 16
 N_TILES = N // P
 D_BANKS = {(0, 0): (0, 1, 2, 3), (0, 1): (4, 5, 6, 7), (1, 0): (0, 1), (1, 1): (2, 3), (2, 0): (4, 5), (2, 1): (6, 7)}
-Y_BANKS = ((0, 1, 2), (3, 4), (5, 6))
+Y_BANKS = ((0, 1, 7), (2, 3), (4, 5))
 
 
 def pieces(index, width):
@@ -240,6 +240,15 @@ def tile_list_wildfire_spread_rates_kernel(
                         stop=(closing and column + count == BANK),
                     )
 
+        def interleave_shared(dst, src):
+            cut = src.shape[2] // 2
+            interleave(dst[:, 0 : PACK * cut], src[:, :, 0:cut])
+            gpsimd.tensor_scalar(
+                dst[:, PACK * cut : 2 * PACK * cut].rearrange("p (j t) -> p j t", t=PACK),
+                src[:, :, cut : 2 * cut].rearrange("p t j -> p j t"),
+                1.0, 0.0, MULT, ADD,
+            )
+
         def evacuate(banks, whole):
             for bank, part in zip(banks, parts(whole, BANK)):
                 scalar.copy(out=part, in_=bank[:, 0 : part.shape[1]])
@@ -280,11 +289,13 @@ def tile_list_wildfire_spread_rates_kernel(
                         stop=(b == PASSES - 1 and ends),
                     )
 
-        def finish_bank(c, k, tag):
+        def finish_bank(c, k, tag, engine=vector, rates=None):
             factors = parts(slopes[c], BANK)[k]
             w = WIDTHS[c]
             result = place(F32, factors.shape[1], tag)
-            vector.tensor_tensor(result, y_banks[c, k][:, 0 : factors.shape[1]], factors, MULT)
+            if rates is None:
+                rates = y_banks[c, k][:, 0 : factors.shape[1]]
+            engine.tensor_tensor(result, rates, factors, MULT)
             first = k * BANK // w
             rows = out[first * P : (first + factors.shape[1] // w) * P, STARTS[c] : STARTS[c] + w]
             nc.sync.dma_start(out=rows.rearrange("(n p) j -> p n j", p=P), in_=result.rearrange("p (n j) -> p n j", j=w))
@@ -425,37 +436,44 @@ def tile_list_wildfire_spread_rates_kernel(
             add_downwind(PACK + t, STARTS[LAST], last_picks[t], last_sums[:, t, :])
         middle_planes = [by_plane(place(BF16, PACK * HALF, "sums%d" % b)) for b in both]
         clamp(vector, 0, in_banks(MIDDLE, 0), middle_planes[0])
-        wide_codes = parts(place(U32, 2 * BANK, "pick7"), BANK)
-        for b in both:
-            quantize_h(WIDE, b, wide_h[b], wide_codes[b])
+        quantize_h(WIDE, 0, wide_h[0], place(U32, BANK, "pick7"))
         last_mixed = place(BF16, PACK * HALF, "wx_bf0")
-        interleave(last_mixed, last_sums)
+        interleave_shared(last_mixed, last_sums)
         middle_d = place(F32, PACK * HALF, "upwind1")
         evacuate(d_banks[MIDDLE, 1], middle_d)
-        for b in both:
-            y_passes(WIDE, b, range(2))
         quantize_x(1, STARTS[LAST], last_mixed, place(U32, HALF, "x_last"))
         for b in both:
             x_passes(LAST, b, 1, closing=True)
-        for b in both:
-            y_passes(WIDE, b, range(2, N_TILES))
-        finish_bank(WIDE, 0, "plane3")
+        quantize_h(WIDE, 1, wide_h[1], place(U32, BANK, "plane3"))
+        for n in range(2):
+            for b in both:
+                y_passes(WIDE, b, [n])
         clamp(vector, 1, parts(middle_d, HALF), middle_planes[1])
         middle_h = [place(BF16, PACK * HALF, tag) for tag in ("wx_bf1", "downwind2")]
-        for b in both:
-            interleave(middle_h[b], middle_planes[b])
+        interleave(middle_h[0], middle_planes[0])
+        interleave_shared(middle_h[1], middle_planes[1])
+        first_rates = place(F32, BANK, "wx_raw10")
+        evacuate([y_banks[WIDE, 0]], first_rates)
+        last_planes = [by_plane(place(BF16, PACK * HALF, "upwind%d" % b)) for b in both]
         last_h = [place(BF16, PACK * HALF, tag) for tag in ("wx_raw11", "wx_raw01")]
-        late_codes = parts(place(U32, 4 * HALF, "tab1"), HALF)
+        clamp(vector, 0, in_banks(LAST, 0), last_planes[0])
+        interleave(last_h[0], last_planes[0])
+        quantize_h(MIDDLE, 0, middle_h[0], place(U32, HALF, "tab1"))
+        y_passes(MIDDLE, 0)
+        finish_bank(WIDE, 0, "wx_bf1", gpsimd, first_rates)
+        clamp(vector, 1, in_banks(LAST, 1), last_planes[1])
+        interleave(last_h[1], last_planes[1])
         for b in both:
-            h_planes = by_plane(place(BF16, PACK * HALF, "upwind%d" % b))
-            clamp(vector, b, in_banks(LAST, b), h_planes)
-            interleave(last_h[b], h_planes)
-            quantize_h(MIDDLE, b, middle_h[b], late_codes[b])
-            y_passes(MIDDLE, b)
-        for b in both:
-            finish_bank(WIDE, 1 + b, ("wx_bf1", "downwind2")[b])
-            quantize_h(LAST, b, last_h[b], late_codes[2 + b])
-            y_passes(LAST, b)
+            y_passes(WIDE, b, [2])
+        late_codes = parts(place(U32, 3 * HALF, "wx_raw10"), HALF)
+        finish_bank(WIDE, 1, "wx_raw00")
+        quantize_h(MIDDLE, 1, middle_h[1], late_codes[0])
+        y_passes(MIDDLE, 1)
+        quantize_h(LAST, 0, last_h[0], late_codes[1])
+        y_passes(LAST, 0)
+        finish_bank(WIDE, 2, "sums0")
+        quantize_h(LAST, 1, last_h[1], late_codes[2])
+        y_passes(LAST, 1)
         for c in (MIDDLE, LAST):
             for k in range(2):
                 finish_bank(c, k, "plane%d" % (2 * c + 2 + k))

from contextlib import ExitStack

import concourse.mybir as mybir

K, H, N, T, S = 1024, 1024, 384, 2048, 1024
FLOPS = 2 * S * (2 * K * H + H * N)

F32 = mybir.dt.float32
BF16 = mybir.dt.bfloat16
I32 = mybir.dt.int32
U32 = mybir.dt.uint32
U16 = mybir.dt.uint16
U8 = mybir.dt.uint8
FP8X4 = mybir.dt.float8_e4m3fn_x4
FP4X4 = mybir.dt.float4_e2m1fn_x4
ADD = mybir.AluOpType.add
MULT = mybir.AluOpType.mult
MAX = mybir.AluOpType.max
MIN = mybir.AluOpType.min

P = 128
PACK = 4
K_PASS = P * PACK
PASSES = K // K_PASS
BANK = 512
HALF = 256
WIDTHS = (512, 256, 256)
STARTS = (0, 512, 768)
WIDE, MIDDLE, LAST = 0, 1, 2
LIST_ROWS = 16
N_TILES = N // P
D_BANKS = {(0, 0): (0, 1, 2, 3), (0, 1): (4, 5, 6, 7), (1, 0): (0, 1), (1, 1): (2, 3), (2, 0): (4, 5), (2, 1): (6, 7)}
Y_BANKS = ((0, 1, 7), (2, 3), (4, 5))


def pieces(index, width):
    found = []
    first = 0
    while first < width:
        bank, column = divmod(index * width + first, BANK)
        count = max(n for n in (512, 256, 128) if n <= min(width - first, BANK - column))
        found.append((bank, column, count, first))
        first = first + count
    return found


def tile_list_wildfire_spread_rates_kernel(
    tc, tab_words, tab_scales, offs, xT, offs2, offs3, wf_words, wf_scales, wx, lo, hi, wr_words, wr_scales, slope, out
):
    nc = tc.nc
    vector, gpsimd, scalar = nc.vector, nc.gpsimd, nc.scalar
    both = range(PASSES)
    with ExitStack() as ctx:
        keep = ctx.enter_context(tc.tile_pool(name="keep", bufs=1))
        work = ctx.enter_context(tc.tile_pool(name="work", bufs=1))
        psum = ctx.enter_context(tc.psum_pool(name="psum", bufs=1))

        def place(dtype, width, tag):
            return work.tile([P, width], dtype, name="tile_" + tag, tag=tag, align_bytes=64)[:]

        def parts(whole, width):
            return [whole[:, j : min(j + width, whole.shape[1])] for j in range(0, whole.shape[1], width)]

        def by_plane(whole):
            return whole.rearrange("p (t j) -> p t j", t=PACK)

        fuel_list = keep.tile([P, S // LIST_ROWS], U16, name="fuel_list")
        upwind_list = keep.tile([P, S // LIST_ROWS], U16, name="upwind_list")
        downwind_list = keep.tile([P, S // LIST_ROWS], U16, name="downwind_list")
        x_planes = [place(F32, T, "plane%d" % i) for i in range(PASSES * PACK)]
        tab_codes = [place(U32, T, "tab%d" % a) for a in both]
        tab_bytes = keep.tile([P, T], U8, name="tab_bytes")
        v_rows = keep.tile([P, S], U8, name="v_rows")
        v_planes = keep.tile([P, PASSES * S], U8, name="v_planes", align_bytes=64)
        wf_raw = [place(U8, 2 * H, "sums%d" % a) for a in both]
        wf_raw_scales = keep.tile([P, H], U8, name="wf_raw_scales")
        wf_rows = keep.tile([P, H], U8, name="wf_rows")
        wf_planes = keep.tile([P, PASSES * H], U8, name="wf_planes", align_bytes=64)
        wr_codes = keep.tile([P, PASSES, N], U32, name="wr_codes", align_bytes=64)
        wr_planes = keep.tile([P, N], U8, name="wr_planes", align_bytes=64)
        lo_cols = keep.tile([P, PASSES, PACK], F32, name="lo_cols")
        hi_cols = keep.tile([P, PASSES, PACK], F32, name="hi_cols")
        wx_raw = {(a, b): place(F32, PACK * K_PASS, "wx_raw%d%d" % (a, b)) for a in both for b in both}

        for rows, engine in ((tab_bytes, vector), (wf_raw_scales, gpsimd)):
            engine.memset(rows[32:64, :].bitcast(I32), 0)
            engine.memset(rows[64:P, :].bitcast(I32), 0)
        for plane in (v_planes, wf_planes, wr_planes):
            gpsimd.memset(plane[:].bitcast(I32), 0)

        def load_rows(rows, scales):
            for a in both:
                nc.sync.dma_start(
                    out=rows[a:32:2, :].bitcast(I32), in_=scales[a].bitcast(I32).rearrange("(q r) c -> r q c", r=4)
                )

        def spread_rows(planes, rows, which=range(4)):
            for r in which:
                nc.sync.dma_start(
                    out=planes[r:P:32, :].bitcast(I32).rearrange("q (a c) -> q a c", a=PASSES),
                    in_=rows[8 * r : 8 * r + 8, :].bitcast(I32),
                )

        def load_scale_rows(plane, scales):
            for q in range(4):
                nc.sync.dma_start(
                    out=plane[32 * q : 32 * q + 4 * PASSES, :].bitcast(I32),
                    in_=scales[:, 4 * q : 4 * q + 4, :].bitcast(I32),
                )

        def load_x_plane(i):
            a, t = divmod(i, PACK)
            rows = xT[a * K_PASS : (a + 1) * K_PASS, :].rearrange("(p t) c -> p t c", t=PACK)
            nc.sync.dma_start(out=x_planes[i], in_=rows[:, t, :])

        def load_wx(a, b):
            rows = wx[a * K_PASS : (a + 1) * K_PASS, b * K_PASS : (b + 1) * K_PASS]
            nc.sync.dma_start(out=by_plane(wx_raw[a, b]), in_=rows.rearrange("(p i) c -> p i c", i=PACK))

        def load_tab(a):
            nc.sync.dma_start(out=tab_codes[a].bitcast(I32), in_=tab_words[a].rearrange("p t i -> p (t i)").bitcast(I32))

        slopes = {}

        def load_slope(c, tag):
            slopes[c] = place(F32, N_TILES * WIDTHS[c], tag)
            cols = slope[:, STARTS[c] : STARTS[c] + WIDTHS[c]]
            nc.sync.dma_start(
                out=slopes[c].rearrange("p (n j) -> p n j", n=N_TILES), in_=cols.rearrange("(n p) j -> p n j", p=P)
            )

        wx_codes = {}
        wx_scales = {}
        wx_grouped = {}

        def cast_wx(a, b, tag):
            wx_grouped[a, b] = place(BF16, PACK * K_PASS, tag)
            scalar.copy(
                out=wx_grouped[a, b].rearrange("p (t m i) -> p m t i", t=PACK, i=PACK),
                in_=wx_raw[a, b].rearrange("p (i m t) -> p m t i", i=PACK, t=PACK),
            )

        def quantize(values, codes, name):
            scales = keep.tile([P, codes.shape[1]], U8, name=name, align_bytes=64)[:]
            vector.quantize_mx(out=codes.bitcast(FP8X4), scales=scales, in_=values)
            return scales

        def quantize_wx(a, b, codes):
            wx_codes[a, b] = codes
            wx_scales[a, b] = quantize(wx_grouped[a, b], codes, "wx_scales%d%d" % (a, b))

        wf_codes = {}

        def reorder_wf(a):
            ordered = place(U8, 2 * H, "wf_codes%d" % a)
            for b in both:
                cols = slice(2 * b * K_PASS, 2 * (b + 1) * K_PASS)
                wf_codes[a, b] = ordered[:, cols]
                gpsimd.tensor_copy(
                    out=wf_codes[a, b].rearrange("p (t m e) -> p t m e", t=PACK, e=2),
                    in_=wf_raw[a][:, cols].rearrange("p (m t e) -> p t m e", t=PACK, e=2),
                )

        def list_cols(first, width):
            return slice(first // LIST_ROWS, (first + width) // LIST_ROWS)

        def pick(i, cells, first, picks):
            vector.tensor_copy(picks, x_planes[i].indirect(cells[:, list_cols(first, picks.shape[1])]))

        def add_downwind(i, first, upwind, total):
            cols = list_cols(first, upwind.shape[1])
            vector.tensor_tensor(total, x_planes[i].indirect(downwind_list[:, cols]), upwind, ADD)

        def gather_halves(i, spares, sums, ahead=None):
            for u in range(2):
                pick(i, upwind_list, u * HALF, spares[u])
            if ahead is not None:
                pick(i, upwind_list, STARTS[MIDDLE], ahead)
            for u in range(2):
                add_downwind(i, u * HALF, spares[u], sums[u])

        def interleave(dst, src):
            scalar.copy(
                out=dst.rearrange("p (c i t) -> p c t i", i=PACK, t=PACK), in_=src.rearrange("p t (c i) -> p c t i", i=PACK)
            )

        x_codes = {}
        x_scales = {}
        v_codes = {}

        def chunks_in(first, width):
            return [c for c in range(len(WIDTHS)) if first <= STARTS[c] < first + width]

        def quantize_x(a, first, values, codes):
            scales = quantize(values, codes, "x_scales%d_%d" % (a, first))
            for c in chunks_in(first, codes.shape[1]):
                cols = slice(STARTS[c] - first, STARTS[c] - first + WIDTHS[c])
                x_codes[c, a] = codes[:, cols]
                x_scales[c, a] = scales[:, cols]

        def gather_v(a, first, picks):
            width = picks.shape[1]
            vector.tensor_copy(picks, tab_codes[a].indirect(fuel_list[:, list_cols(first, width)]))
            for c in chunks_in(first, width):
                v_codes[c, a] = picks[:, STARTS[c] - first : STARTS[c] - first + WIDTHS[c]]

        d_banks = {}

        def bank_tile(name, number):
            return psum.tile([P, BANK], F32, name=name, tag="bank%d" % number)

        def x_passes(c, b, a, closing=False, slots=range(PACK)):
            if a == 0:
                d_banks[c, b] = [bank_tile("d%d%d%d" % (c, b, n), n) for n in D_BANKS[c, b]]
            for t in slots:
                cols = slice(t * P, (t + 1) * P)
                for bank, column, count, first in pieces(t, WIDTHS[c]):
                    nc.tensor.matmul_mx(
                        out=d_banks[c, b][bank][:, column : column + count],
                        lhsT=wx_codes[a, b][:, cols].bitcast(FP8X4),
                        lhsT_scale=wx_scales[a, b][:, cols],
                        rhs=x_codes[c, a][:, first : first + count].bitcast(FP8X4),
                        rhs_scale=x_scales[c, a][:, first : first + count],
                        start=(a == 0 and column == 0),
                        stop=(closing and column + count == BANK),
                    )

        def fuel_passes(c, b, a, closing=False, slots=range(PACK)):
            for t in slots:
                col = a * H + b * K_PASS + t * P
                for bank, column, count, first in pieces(t, WIDTHS[c]):
                    entry = a * S + STARTS[c] + first
                    nc.tensor.matmul_mx(
                        out=d_banks[c, b][bank][:, column : column + count],
                        lhsT=wf_codes[a, b][:, 2 * t * P : 2 * (t + 1) * P].bitcast(FP4X4),
                        lhsT_scale=wf_planes[:, col : col + P],
                        rhs=v_codes[c, a][:, first : first + count].bitcast(FP8X4),
                        rhs_scale=v_planes[:, entry : entry + count],
                        start=False,
                        stop=(closing and column + count == BANK),
                    )

        def interleave_shared(dst, src):
            cut = src.shape[2] // 2
            interleave(dst[:, 0 : PACK * cut], src[:, :, 0:cut])
            gpsimd.tensor_scalar(
                dst[:, PACK * cut : 2 * PACK * cut].rearrange("p (j t) -> p j t", t=PACK),
                src[:, :, cut : 2 * cut].rearrange("p t j -> p j t"),
                1.0, 0.0, MULT, ADD,
            )

        def evacuate(banks, whole):
            for bank, part in zip(banks, parts(whole, BANK)):
                scalar.copy(out=part, in_=bank[:, 0 : part.shape[1]])

        def in_banks(c, b):
            return [part for bank in d_banks[c, b] for part in parts(bank[:], WIDTHS[c])]

        def clamp(engine, b, drivers, planes, slots=range(PACK)):
            for t in slots:
                low, high = lo_cols[:, b, t : t + 1], hi_cols[:, b, t : t + 1]
                if engine is vector:
                    vector.tensor_scalar(planes[:, t, :], drivers[t], low, high, MAX, MIN)
                else:
                    engine.tensor_scalar(planes[:, t, :], drivers[t], high, low, MIN, MAX)

        y_banks = {}

        h_codes = {}

        def quantize_h(c, b, values, codes):
            h_codes[c, b] = (codes, quantize(values, codes, "h_scales%d%d" % (c, b)))

        def y_passes(c, b, tiles=range(N_TILES)):
            codes, scales = h_codes[c, b]
            for n in tiles:
                cols = slice(n * P, (n + 1) * P)
                for bank, column, count, first in pieces(n, WIDTHS[c]):
                    if b == 0 and column == 0:
                        y_banks[c, bank] = bank_tile("y%d%d" % (c, bank), Y_BANKS[c][bank])
                    ends = column + count == BANK or (n == N_TILES - 1 and first + count == WIDTHS[c])
                    nc.tensor.matmul_mx(
                        out=y_banks[c, bank][:, column : column + count],
                        lhsT=wr_codes[:, b, cols].bitcast(FP8X4),
                        lhsT_scale=wr_planes[4 * b : P, cols],
                        rhs=codes[:, first : first + count].bitcast(FP8X4),
                        rhs_scale=scales[:, first : first + count],
                        start=(b == 0 and column == 0),
                        stop=(b == PASSES - 1 and ends),
                    )

        def finish_bank(c, k, tag, engine=vector, rates=None):
            factors = parts(slopes[c], BANK)[k]
            w = WIDTHS[c]
            result = place(F32, factors.shape[1], tag)
            if rates is None:
                rates = y_banks[c, k][:, 0 : factors.shape[1]]
            engine.tensor_tensor(result, rates, factors, MULT)
            first = k * BANK // w
            rows = out[first * P : (first + factors.shape[1] // w) * P, STARTS[c] : STARTS[c] + w]
            nc.sync.dma_start(out=rows.rearrange("(n p) j -> p n j", p=P), in_=result.rearrange("p (n j) -> p n j", j=w))

        nc.sync.dma_start(fuel_list[:], offs)
        load_rows(tab_bytes, tab_scales)
        load_x_plane(0)
        nc.sync.dma_start(upwind_list[:], offs2)
        nc.sync.dma_start(downwind_list[:], offs3)
        load_rows(wf_raw_scales, wf_scales)
        vector.tensor_copy(v_rows[:], tab_bytes[:].indirect(fuel_list[:]))
        gpsimd.tensor_copy(
            out=wf_rows[:].rearrange("p (b t m) -> p b t m", t=PACK, m=P),
            in_=wf_raw_scales[:].rearrange("p (b m t) -> p b t m", t=PACK, m=P),
        )
        for a in both:
            nc.sync.dma_start(out=wf_raw[a].bitcast(I32), in_=wf_words[a].bitcast(I32))
        load_x_plane(1)
        load_wx(0, 0)
        load_x_plane(2)
        load_wx(0, 1)
        load_x_plane(3)
        load_tab(0)
        load_x_plane(4)
        load_x_plane(5)
        load_wx(1, 0)
        load_wx(1, 1)
        load_x_plane(6)
        load_tab(1)
        spread_rows(wf_planes, wf_rows, range(1))
        load_x_plane(7)
        spread_rows(wf_planes, wf_rows, range(1, 4))
        spread_rows(v_planes, v_rows)
        nc.sync.dma_start(out=lo_cols[:], in_=lo.rearrange("(b p t) -> p b t", b=PASSES, t=PACK))
        nc.sync.dma_start(out=hi_cols[:], in_=hi.rearrange("(b p t) -> p b t", b=PASSES, t=PACK))
        nc.sync.dma_start(out=wr_codes[:].bitcast(I32), in_=wr_words.rearrange("a p c i -> p a (c i)").bitcast(I32))
        load_scale_rows(wr_planes, wr_scales)

        for a in both:
            reorder_wf(a)
        first_sums = [by_plane(place(F32, PACK * BANK, "sums%d" % u)) for u in range(2)]
        for t in range(PACK):
            upwind = place(F32, S, "upwind%d" % (t % 3))
            downwind = place(F32, S, "downwind%d" % (t % 3))
            pick(t, upwind_list, 0, upwind)
            pick(t, downwind_list, 0, downwind)
            for u in range(2):
                cols = slice(u * BANK, (u + 1) * BANK)
                gpsimd.tensor_tensor(first_sums[u][:, t, :], upwind[:, cols], downwind[:, cols], ADD)
        for c in range(len(WIDTHS)):
            load_slope(c, ("plane0", "plane1", "slope2")[c])
        cast_wx(0, 0, "wx_bf0")
        cast_wx(0, 1, "wx_bf1")
        first_mixed = [place(BF16, PACK * BANK, "mixed%d" % u) for u in range(2)]
        for u in range(2):
            interleave(first_mixed[u], first_sums[u])
        gather_v(0, 0, place(U32, BANK, "v_first"))

        wide_sums = [by_plane(place(F32, PACK * HALF, "plane%d" % (2 + u))) for u in range(2)]
        chain = place(F32, HALF, "chain")
        middle_picks = {0: place(F32, HALF, "middle_picks")}
        gather_halves(4, [place(F32, HALF, "pick4"), chain], [half[:, 0, :] for half in wide_sums], middle_picks[0])
        quantize_wx(0, 0, place(U32, K_PASS, "pick4"))
        gather_halves(5, [place(F32, HALF, "pick5"), chain], [half[:, 1, :] for half in wide_sums])
        quantize_x(0, 0, first_mixed[0], place(U32, BANK, "pick5"))
        x_passes(WIDE, 0, 0)
        last_picks = [place(F32, HALF, "early_pick")]
        pick(PACK, upwind_list, STARTS[LAST], last_picks[0])
        for b in both:
            cast_wx(1, b, "sums%d" % b)
        gather_halves(6, [place(F32, HALF, "pick6"), chain], [half[:, 2, :] for half in wide_sums])
        quantize_wx(0, 1, place(U32, K_PASS, "pick6"))
        x_passes(WIDE, 1, 0)
        gather_v(1, 0, place(U32, BANK, "chain"))
        spares = [place(F32, HALF, "pick7"), place(F32, HALF, "pick8")]
        gather_halves(7, spares, [half[:, 3, :] for half in wide_sums])
        wide_mixed = place(BF16, PACK * BANK, "upwind2")
        for u in range(2):
            interleave(parts(wide_mixed, PACK * HALF)[u], wide_sums[u])
        middle_picks.update({1: place(F32, HALF, "pick7")})
        pick(PACK + 1, upwind_list, STARTS[MIDDLE], middle_picks[1])
        quantize_x(0, BANK, first_mixed[1], place(U32, BANK, "pick8"))
        for b, codes in enumerate(parts(place(U32, 2 * K_PASS, "plane2"), K_PASS)):
            quantize_wx(1, b, codes)
        for a in both:
            fuel_passes(WIDE, 0, a)
        fuel_passes(WIDE, 1, 0)
        quantize_x(1, 0, wide_mixed, place(U32, BANK, "mixed1"))
        x_passes(WIDE, 0, 1, closing=True)
        for t in range(PACK):
            x_passes(WIDE, 1, 1, slots=[t])
            fuel_passes(WIDE, 1, 1, closing=True, slots=[t])
        shared = place(F32, (2 + PACK) * HALF, "plane3")
        middle_sums = by_plane(shared[:, 2 * HALF : (2 + PACK) * HALF])
        last_sums = by_plane(shared[:, 0 : PACK * HALF])
        for t in range(2):
            add_downwind(PACK + t, STARTS[MIDDLE], middle_picks[t], middle_sums[:, t, :])
        first_d = parts(place(F32, PACK * BANK, "wx_raw00"), BANK)
        second_d = [shared[:, 2 * BANK : 3 * BANK], shared[:, 0:BANK]] + parts(place(F32, 2 * BANK, "wx_raw01"), BANK)
        for b, drivers in enumerate((first_d, second_d)):
            for t in range(PACK):
                scalar.copy(out=drivers[t], in_=d_banks[WIDE, b][t][:])
        first_planes = by_plane(place(F32, PACK * BANK, "wx_raw10"))
        second_store = place(F32, PACK * BANK, "middle_picks")
        second_planes = by_plane(second_store)
        clamp(gpsimd, 0, first_d, first_planes)
        clamp(gpsimd, 1, second_d, second_planes, range(1))
        for a, picks in enumerate(parts(place(U32, 2 * BANK, "upwind2"), BANK)):
            gather_v(a, BANK, picks)
        for b in both:
            x_passes(MIDDLE, b, 0)
            for a in both:
                fuel_passes(MIDDLE, b, a)
        middle_picks.update({2: second_store[:, 2 * BANK - HALF // 2 : 2 * BANK + HALF // 2], 3: second_planes[:, 3, 0:HALF]})
        for t in range(2, PACK):
            pick(PACK + t, upwind_list, STARTS[MIDDLE], middle_picks[t])
        last_picks = last_picks + parts(place(F32, 2 * HALF, "pick7"), HALF) + [place(F32, HALF, "tab0")]
        for t in range(1, PACK):
            pick(PACK + t, upwind_list, STARTS[LAST], last_picks[t])
        for t in range(2, PACK):
            add_downwind(PACK + t, STARTS[MIDDLE], middle_picks[t], middle_sums[:, t, :])
        wide_h = [place(BF16, PACK * BANK, "downwind%d" % b) for b in both]
        interleave(wide_h[0], first_planes)
        middle_mixed = place(BF16, PACK * HALF, "wx_bf0")
        interleave(middle_mixed, middle_sums)
        clamp(vector, 1, second_d, second_planes, range(1, PACK))
        interleave(wide_h[1], second_planes)
        for t in range(2):
            add_downwind(PACK + t, STARTS[LAST], last_picks[t], last_sums[:, t, :])
        quantize_x(1, STARTS[MIDDLE], middle_mixed, place(U32, HALF, "x_middle"))
        for b in both:
            x_passes(MIDDLE, b, 1, closing=True)
        for b in both:
            x_passes(LAST, b, 0)
            for a in both:
                fuel_passes(LAST, b, a)
        for t in range(2, PACK):
            add_downwind(PACK + t, STARTS[LAST], last_picks[t], last_sums[:, t, :])
        middle_planes = [by_plane(place(BF16, PACK * HALF, "sums%d" % b)) for b in both]
        clamp(vector, 0, in_banks(MIDDLE, 0), middle_planes[0])
        quantize_h(WIDE, 0, wide_h[0], place(U32, BANK, "pick7"))
        last_mixed = place(BF16, PACK * HALF, "wx_bf0")
        interleave_shared(last_mixed, last_sums)
        middle_d = place(F32, PACK * HALF, "upwind1")
        evacuate(d_banks[MIDDLE, 1], middle_d)
        quantize_x(1, STARTS[LAST], last_mixed, place(U32, HALF, "x_last"))
        for b in both:
            x_passes(LAST, b, 1, closing=True)
        quantize_h(WIDE, 1, wide_h[1], place(U32, BANK, "plane3"))
        for n in range(2):
            for b in both:
                y_passes(WIDE, b, [n])
        clamp(vector, 1, parts(middle_d, HALF), middle_planes[1])
        middle_h = [place(BF16, PACK * HALF, tag) for tag in ("wx_bf1", "downwind2")]
        interleave(middle_h[0], middle_planes[0])
        interleave_shared(middle_h[1], middle_planes[1])
        first_rates = place(F32, BANK, "wx_raw10")
        evacuate([y_banks[WIDE, 0]], first_rates)
        last_planes = [by_plane(place(BF16, PACK * HALF, "upwind%d" % b)) for b in both]
        last_h = [place(BF16, PACK * HALF, tag) for tag in ("wx_raw11", "wx_raw01")]
        clamp(vector, 0, in_banks(LAST, 0), last_planes[0])
        interleave(last_h[0], last_planes[0])
        quantize_h(MIDDLE, 0, middle_h[0], place(U32, HALF, "tab1"))
        y_passes(MIDDLE, 0)
        finish_bank(WIDE, 0, "wx_bf1", gpsimd, first_rates)
        clamp(vector, 1, in_banks(LAST, 1), last_planes[1])
        interleave(last_h[1], last_planes[1])
        for b in both:
            y_passes(WIDE, b, [2])
        late_codes = parts(place(U32, 3 * HALF, "wx_raw10"), HALF)
        finish_bank(WIDE, 1, "wx_raw00")
        quantize_h(MIDDLE, 1, middle_h[1], late_codes[0])
        y_passes(MIDDLE, 1)
        quantize_h(LAST, 0, last_h[0], late_codes[1])
        y_passes(LAST, 0)
        finish_bank(WIDE, 2, "sums0")
        quantize_h(LAST, 1, last_h[1], late_codes[2])
        y_passes(LAST, 1)
        for c in (MIDDLE, LAST):
            for k in range(2):
                finish_bank(c, k, "plane%d" % (2 * c + 2 + k))
